import numpy as np
import ml_dtypes


def mxq(x, axis, fmt="e4m3"):
    dtype, down = {"e4m3": (ml_dtypes.float8_e4m3fn, 7), "e5m2": (ml_dtypes.float8_e5m2, 14)}[fmt]
    v = np.moveaxis(np.asarray(x, np.float32).astype(ml_dtypes.bfloat16).astype(np.float64), axis, -1)
    blocks = v.reshape(v.shape[:-1] + (-1, 32))
    amax = np.abs(blocks).max(-1, keepdims=True)
    byte = np.maximum(np.where(amax > 0, np.frexp(amax)[1] - 1 + 127, 0) - down, 1)
    scale = np.exp2(byte - 127.0)
    codes = (blocks / scale).astype(np.float32).astype(dtype).astype(np.float64)
    return np.moveaxis((codes * scale).reshape(v.shape), -1, axis)


WIDE = False


def mx_kscale(k):
    if not WIDE:
        return np.ones(k)
    levels = np.array([30, -30])
    if k % 512:
        return np.exp2(np.random.permutation(np.resize(levels, k // 32))).repeat(32)
    a = np.empty((k // 512, 16))
    for p in range(k // 512):
        a[p, :8] = np.random.permutation(np.resize(levels, 8))
        for g in range(8):
            far = levels[np.abs(levels - a[p, g]) >= 10]
            a[p, g + 8] = far[np.random.randint(len(far))]
    return np.exp2(a.ravel()).repeat(32)


BF16 = ml_dtypes.bfloat16


def bf(x):
    return np.asarray(x, np.float32).astype(BF16)


def f64(x):
    return np.asarray(x).astype(np.float64)


E2M1 = np.array([0.0, 0.5, 1.0, 1.5, 2.0, 3.0, 4.0, 6.0, -0.0, -0.5, -1.0, -1.5, -2.0, -3.0, -4.0, -6.0])


def pack_weight(w, fmt):
    k, n = w.shape
    w = f64(bf(w)).reshape(k // 32, 32, n)
    amax = np.abs(w).max(1)
    if fmt in ("e4m3", "e5m2"):
        byte = np.frexp(amax)[1] - 1 + 127 - (7 if fmt == "e4m3" else 14)
    else:
        mant, ex = np.frexp(amax / 6.0)
        byte = np.where(mant > 0.5, ex, ex - 1) + 127
    byte = np.clip(np.where(amax > 0, byte, 1), 1, 254)
    scaled = (w * np.exp2(127.0 - byte)[:, None, :]).reshape(k, n).astype(np.float32)
    by_word = np.ascontiguousarray(scaled.reshape(k // 512, 128, 4, n).transpose(0, 1, 3, 2))
    if fmt in ("e4m3", "e5m2"):
        words = by_word.astype(ml_dtypes.float8_e4m3fn if fmt == "e4m3" else ml_dtypes.float8_e5m2).view(np.uint8)
    else:
        c = by_word.astype(ml_dtypes.float4_e2m1fn).view(np.uint8) & 0xF
        words = c[..., 0::2] | (c[..., 1::2] << 4)
    return np.ascontiguousarray(words), np.ascontiguousarray(byte.astype(np.uint8).reshape(k // 512, 16, n))


def unpack_weight(words, scales, fmt):
    g, p, n, _ = words.shape
    if fmt in ("e4m3", "e5m2"):
        vals = np.ascontiguousarray(words).view(ml_dtypes.float8_e4m3fn if fmt == "e4m3" else ml_dtypes.float8_e5m2).astype(np.float64)
    else:
        nib = np.empty((g, p, n, 4), np.uint8)
        nib[..., 0::2] = words & 0xF
        nib[..., 1::2] = words >> 4
        vals = E2M1[nib]
    vals = vals * np.repeat(np.exp2(scales.astype(np.float64) - 127.0), 8, axis=1)[..., None]
    return vals.transpose(0, 1, 3, 2).reshape(g * 512, n)

def planes(Y):
    n, m = Y.shape
    b = f64(bf(Y)).reshape(n // 32, 32, m)
    amax = np.abs(b).max(1)
    byte = np.clip(np.where(amax > 0, np.frexp(amax)[1] - 1 + 127 - 7, 1), 1, 254)
    codes = (b * np.exp2(127.0 - byte)[:, None, :]).reshape(n, m).astype(np.float32).astype(ml_dtypes.float8_e4m3fn).view(np.uint8)
    words = codes.reshape(n // 512, 128, 4, m).transpose(0, 1, 3, 2)
    return np.ascontiguousarray(words), np.ascontiguousarray(byte.astype(np.uint8).reshape(n // 512, 16, m))


IMG, PTS, CLU, DIM = 4, 1024, 256, 1024


def setup_inputs():
    s = mx_kscale(PTS)[:, None]
    popularity = 0.5 * np.random.randn(CLU)
    logits = 2.0 * np.random.randn(IMG, PTS, CLU) + popularity
    e = np.exp(logits - logits.max(axis=-1, keepdims=True))
    a = e / e.sum(axis=-1, keepdims=True)
    a_words, a_scales = pack_weight((a / s).reshape(IMG * PTS, CLU), "e5m2")
    mass = a.sum(axis=1)
    x = np.random.randn(IMG, PTS, DIM) * s
    centres = 0.2 * np.random.randn(CLU, DIM)
    gain = 0.5 * np.exp(0.8 * np.random.randn(DIM))
    return {"a_words": a_words, "a_scales": a_scales, "x": bf(x),
            "mass": bf(mass), "centres": bf(centres), "gain": bf(gain)}


def reference(a_words, a_scales, x, mass, centres, gain):
    A = unpack_weight(a_words, a_scales, "e5m2").reshape(IMG, PTS, CLU)
    xq = mxq(f64(x), 1, "e4m3")
    sums = A.transpose(0, 2, 1) @ xq
    y = (sums - f64(mass)[:, :, None] * f64(centres)) * f64(gain)
    Y = y.reshape(IMG * CLU, DIM).T
    words, scales = planes(Y)
    return y, words, scales

@@ -1,0 +1,236 @@
+from contextlib import ExitStack
+
+import concourse.mybir as mybir
+from concourse.masks import make_identity
+
+IMG, PTS, CLU, DIM = 4, 1024, 256, 1024
+FLOPS = 2 * IMG * PTS * CLU * DIM
+
+F32 = mybir.dt.float32
+BF16 = mybir.dt.bfloat16
+U32 = mybir.dt.uint32
+I32 = mybir.dt.int32
+U8 = mybir.dt.uint8
+E4M3X4 = mybir.dt.float8_e4m3fn_x4
+E5M2X4 = mybir.dt.float8_e5m2_x4
+ALU = mybir.AluOpType
+ACT = mybir.ActivationFunctionType
+
+P = 128
+PACK = 4
+K_PASS = P * PACK
+HALF = 512
+PASSES = PTS // K_PASS
+CTILES = CLU // P
+UNITS = IMG * (DIM // HALF)
+
+V_COLS = [(352, 352), (400, 0)] + [(304, 0)] * 6
+
+
+def tile_vlad_residual_sums_k2_kernel(tc, a_words, a_scales, x, mass, centres, gain, out_0, out_1, out_2):
+    nc = tc.nc
+    with ExitStack() as ctx:
+        keep = ctx.enter_context(tc.tile_pool(name="keep", bufs=1))
+        work = ctx.enter_context(tc.tile_pool(name="work", bufs=4))
+        psum = ctx.enter_context(tc.psum_pool(name="psum", bufs=4))
+        ctx.enter_context(tc.manual_schedule())
+
+        ident32 = keep.tile([P, P], F32, name="ident32", align_bytes=64)
+        ident16 = keep.tile([P, P], BF16, name="ident16", align_bytes=64)
+        rows = keep.tile([P, P], BF16, name="rows", align_bytes=64)
+        cols = keep.tile([P, 8], BF16, name="cols", align_bytes=64)
+        neg_mass = keep.tile([P, 8], F32, name="neg_mass", align_bytes=64)
+        gain_all = keep.tile([P, DIM], BF16, name="gain_all", align_bytes=64)
+        cen = keep.tile([P, 2, CTILES, HALF], BF16, name="cen", align_bytes=64)
+        a_codes = keep.tile([P, IMG * PASSES, CLU], U32, name="a_codes", align_bytes=64)
+        a_plane = keep.tile([P, IMG * PASSES, CLU], U8, name="a_plane", align_bytes=64)
+        y_codes = keep.tile([P, 2, IMG * CLU], U32, name="y_codes", align_bytes=64)
+        early_plane = keep.tile([P, 2, (IMG - 1) * CLU], U8, name="early_plane", align_bytes=64)
+        late_plane = keep.tile([P, 2, CLU], U8, name="late_plane", align_bytes=64)
+        raw = {}
+
+        def load_x(b, g, c0, c1):
+            src = x[b, g * K_PASS:(g + 1) * K_PASS, c0:c1].rearrange("(p j) d -> p j d", j=PACK)
+            piece = keep.tile([P, PACK, c1 - c0], BF16, name="raw%d%d%d" % (b, g, c0), align_bytes=64)
+            nc.sync.dma_start(out=piece[:], in_=src)
+            for c in range(c0, c1, HALF):
+                raw[b, g, c // HALF] = piece[:, :, c - c0:c - c0 + HALF]
+
+        def load_a(g0, g1):
+            src = a_words[g0:g1].rearrange("g p n t -> p g (n t)").bitcast(I32)
+            nc.sync.dma_start(out=a_codes[:, g0:g1, :].bitcast(I32), in_=src)
+
+        nc.vector.memset(rows[:], 0.0)
+        nc.vector.memset(a_plane[:].rearrange("p g n -> p (g n)").bitcast(I32), 0)
+        make_identity(nc, ident32[:])
+
+        def load_centres(h):
+            cl = slice(h * HALF, (h + 1) * HALF)
+            nc.sync.dma_start(out=cen[:, h, :, :], in_=centres.rearrange("(ct p) d -> p ct d", p=P)[:, :, cl])
+
+        nc.scalar.dma_start(out=rows[0:8, :], in_=gain.rearrange("(r c) -> r c", c=P))
+        nc.scalar.dma_start(out=rows[8:16, :], in_=mass.rearrange("b (h c) -> (b h) c", c=P))
+        nc.scalar.copy(out=ident16[:], in_=ident32[:])
+        load_x(0, 0, 0, HALF)
+        load_x(0, 1, 0, HALF)
+        for q in range(4):
+            nc.sync.dma_start(
+                out=a_plane[32 * q:32 * q + 4, :, :].bitcast(I32),
+                in_=a_scales[:, 4 * q:4 * q + 4, :].rearrange("g r n -> r g n").bitcast(I32))
+        load_x(0, 0, HALF, DIM)
+        load_a(0, PASSES)
+        load_x(0, 1, HALF, DIM)
+        load_centres(0)
+        load_centres(1)
+        load_x(1, 0, 0, HALF)
+        load_x(1, 1, 0, HALF)
+        load_a(PASSES, 2 * PASSES)
+        load_x(1, 0, HALF, DIM)
+        load_x(1, 1, HALF, DIM)
+        load_a(2 * PASSES, IMG * PASSES)
+        for b in range(2, IMG):
+            for g in range(PASSES):
+                load_x(b, g, 0, DIM)
+
+        grouped = {}
+        xq = {}
+        acc = {}
+        ys = {}
+        yb = {}
+
+        def interleave(engine_copy, u, g, c0, c1):
+            b, h = divmod(u, 2)
+            if (u, g) not in grouped:
+                grouped[u, g] = work.tile([P, HALF, PACK], BF16, name="grouped", align_bytes=64)
+            if c1 > c0:
+                engine_copy(
+                    out=grouped[u, g][:, c0:c1, :].rearrange("p (c i) t -> p c t i", i=4),
+                    in_=raw[b, g, h][:, :, c0:c1].rearrange("p t (c i) -> p c t i", i=4))
+
+        def quantize_x(u, g):
+            codes = work.tile([P, HALF], U32, name="x_codes", align_bytes=64)
+            plane = work.tile([P, HALF], U8, name="x_plane", align_bytes=64)
+            nc.vector.quantize_mx(out=codes[:].bitcast(E4M3X4), scales=plane[:],
+                                  in_=grouped[u, g][:].rearrange("p c t -> p (c t)"))
+            xq[u, g] = (codes, plane)
+
+        def multiply(u, g):
+            b = u // 2
+            codes, plane = xq[u, g]
+            for ct in range(CTILES):
+                if g == 0:
+                    acc[u, ct] = psum.tile([P, HALF], F32, name="acc")
+                cl = slice(ct * P, (ct + 1) * P)
+                nc.tensor.matmul_mx(
+                    out=acc[u, ct][:],
+                    lhsT=a_codes[:, PASSES * b + g, cl].bitcast(E5M2X4), lhsT_scale=a_plane[:, PASSES * b + g, cl],
+                    rhs=codes[:].bitcast(E4M3X4), rhs_scale=plane[:],
+                    start=(g == 0), stop=(g == PASSES - 1))
+
+        def residual(u, ct):
+            b, h = divmod(u, 2)
+            if ct == 0:
+                ys[u] = work.tile([P, CTILES, HALF], F32, name="y", bufs=UNITS, align_bytes=64)
+            nc.vector.scalar_tensor_tensor(
+                out=ys[u][:, ct, :], in0=cen[:, h, ct, :],
+                scalar=neg_mass[:, CTILES * b + ct:CTILES * b + ct + 1], in1=acc[u, ct][:],
+                op0=ALU.mult, op1=ALU.add)
+
+        def scale(u, ct):
+            h = u % 2
+            nc.vector.tensor_tensor(out=ys[u][:, ct, :], in0=ys[u][:, ct, :],
+                                    in1=gain_all[:, h * HALF:(h + 1) * HALF], op=ALU.mult)
+
+        turned = {}
+
+        def turn(u, ct):
+            turned[u, ct] = psum.tile([P, PACK, P], F32, name="turned")
+            for t in range(PACK):
+                nc.tensor.transpose(turned[u, ct][:, t, :], ys[u][:, ct, t:HALF:PACK], ident32[:])
+
+        def round_y(u, ct):
+            if ct == 0:
+                yb[u] = work.tile([P, CLU, PACK], BF16, name="yb", bufs=3, align_bytes=64)
+            nc.scalar.copy(out=yb[u][:, ct * P:(ct + 1) * P, :], in_=turned[u, ct][:].rearrange("p t c -> p c t"))
+
+        def quantize_y(u, c0, c1):
+            b, h = divmod(u, 2)
+            m = slice(b * CLU + c0, b * CLU + c1)
+            plane = late_plane[:, h, c0:c1] if b == IMG - 1 else early_plane[:, h, m]
+            nc.vector.quantize_mx(out=y_codes[:, h, m].bitcast(E4M3X4), scales=plane,
+                                  in_=yb[u][:, c0:c1, :].rearrange("p c t -> p (c t)"))
+
+        def store_y(u, ct0, ct1):
+            b, h = divmod(u, 2)
+            nc.sync.dma_start(out=out_0[b].rearrange("(ct p) d -> p ct d", p=P)[:, ct0:ct1, h * HALF:(h + 1) * HALF],
+                              in_=ys[u][:, ct0:ct1, :])
+
+        def store_scales(queue, q, plane, m0, m1):
+            queue.dma_start(
+                out=out_2[:, 4 * q:4 * q + 4, m0:m1].rearrange("g r m -> r g m").bitcast(I32),
+                in_=plane[32 * q:32 * q + 4, :, :].bitcast(I32))
+
+        def store_codes(u, c0, c1):
+            b, h = divmod(u, 2)
+            m = slice(b * CLU + c0, b * CLU + c1)
+            nc.sync.dma_start(out=out_1[h][:, m, :].rearrange("p m t -> p (m t)").bitcast(I32),
+                              in_=y_codes[:, h, m].bitcast(I32))
+
+        def spread_constants():
+            first = psum.tile([P, P], BF16, name="turned")
+            nc.tensor.transpose(first[:], rows[:], ident16[:])
+            nc.scalar.copy(out=cols[:], in_=first[:, 0:8])
+            nc.scalar.activation(out=neg_mass[:], in_=first[:, 8:16], func=ACT.Copy, scale=-1.0)
+            spread = psum.tile([P, DIM], BF16, name="turned")
+            for j in range(8):
+                nc.tensor.transpose(spread[:, j * P:(j + 1) * P], cols[:, j:j + 1].to_broadcast([P, P]), ident16[:])
+            nc.scalar.copy(out=gain_all[:], in_=spread[:])
+
+        for s in range(UNITS):
+            v0, v1 = V_COLS[s]
+            interleave(nc.scalar.copy, s, 0, v0, HALF)
+            interleave(nc.vector.tensor_copy, s, 0, 0, v0)
+            interleave(nc.scalar.copy, s, 1, v1, HALF)
+            interleave(nc.vector.tensor_copy, s, 1, 0, v1)
+            if s == 0:
+                spread_constants()
+            if s >= 2:
+                for ct in range(CTILES):
+                    round_y(s - 2, ct)
+            if s >= 1:
+                for ct in range(CTILES):
+                    residual(s - 1, ct)
+                for ct in range(CTILES):
+                    scale(s - 1, ct)
+                store_y(s - 1, 0, CTILES)
+                turn(s - 1, 0)
+            for g in range(PASSES):
+                quantize_x(s, g)
+                multiply(s, g)
+            if s >= 1:
+                turn(s - 1, 1)
+            if s >= 3:
+                quantize_y(s - 3, 0, CLU)
+                store_codes(s - 3, 0, CLU)
+
+        last = UNITS - 1
+        quantize_y(last - 2, 0, CLU)
+        store_codes(last - 2, 0, CLU)
+        for q in range(4):
+            store_scales(nc.sync, q, early_plane, 0, (IMG - 1) * CLU)
+        for ct in range(CTILES):
+            round_y(last - 1, ct)
+        for ct in range(CTILES):
+            residual(last, ct)
+        for ct in range(CTILES):
+            scale(last, ct)
+            store_y(last, ct, ct + 1)
+            turn(last, ct)
+            round_y(last, ct)
+        quantize_y(last - 1, 0, CLU)
+        store_codes(last - 1, 0, CLU)
+        for ct in range(CTILES):
+            quantize_y(last, ct * P, (ct + 1) * P)
+            store_codes(last, ct * P, (ct + 1) * P)
+        for q in range(4):
+            store_scales(nc.scalar if q % 2 else nc.sync, q, late_plane, (IMG - 1) * CLU, IMG * CLU)

@@ -24,7 +24,14 @@ PASSES = PTS // K_PASS
 CTILES = CLU // P
 UNITS = IMG * (DIM // HALF)
 
-V_COLS = [(352, 352), (400, 0)] + [(304, 0)] * 6
+V_COLS = [512, 256, 512, 96, 128, 128, 128, 208, 0, 128, 0, 96, 0, 96, 0, 64]
+CHUNKS = ([(b, g, h) for b in (0, 1) for g in (0, 1) for h in (0, 1)]
+          + [(b, g, h) for b in (2, 3) for h in (0, 1) for g in (0, 1)])
+ORDER = ("I0 S0 S1 K0 I1 Q0 Q1 M00 M10 S2 S3 I2 I3 Q2 M01 Q3 M11 S4 S5 I4 I5 s0 Q4 t0 s1 T0 M20 S6 Q5 S7 c0 I6 I7 Q6 M21 M30 t1 s2 T1 Q7 M31 "
+         "S8 S9 c1 q0 I9 t2 s3 T2 Q8 M40 Q9 M41 "
+         "S10 S11 c2 q1 I11 t3 s4 T3 Q10 M50 Q11 M51 "
+         "S12 S13 c3 q2 I13 t4 s5 T4 Q12 M60 Q13 M61 "
+         "S14 c4 S15 I15 q3 t5 s6 T5 Q14 M70 c5 q4 Q15 M71 q5 t6 s7 T6 c6")
 
 
 def tile_vlad_residual_sums_k2_kernel(tc, a_words, a_scales, x, mass, centres, gain, out_0, out_1, out_2):
@@ -41,7 +48,7 @@ def tile_vlad_residual_sums_k2_kernel(tc, a_words, a_scales, x, mass, centres, g
         cols = keep.tile([P, 8], BF16, name="cols", align_bytes=64)
         neg_mass = keep.tile([P, 8], F32, name="neg_mass", align_bytes=64)
         gain_all = keep.tile([P, DIM], BF16, name="gain_all", align_bytes=64)
-        cen = keep.tile([P, 2, CTILES, HALF], BF16, name="cen", align_bytes=64)
+        cen = keep.tile([P, CTILES, DIM], BF16, name="cen", align_bytes=64)
         a_codes = keep.tile([P, IMG * PASSES, CLU], U32, name="a_codes", align_bytes=64)
         a_plane = keep.tile([P, IMG * PASSES, CLU], U8, name="a_plane", align_bytes=64)
         y_codes = keep.tile([P, 2, IMG * CLU], U32, name="y_codes", align_bytes=64)
@@ -64,33 +71,25 @@ def tile_vlad_residual_sums_k2_kernel(tc, a_words, a_scales, x, mass, centres, g
         nc.vector.memset(a_plane[:].rearrange("p g n -> p (g n)").bitcast(I32), 0)
         make_identity(nc, ident32[:])
 
-        def load_centres(h):
-            cl = slice(h * HALF, (h + 1) * HALF)
-            nc.sync.dma_start(out=cen[:, h, :, :], in_=centres.rearrange("(ct p) d -> p ct d", p=P)[:, :, cl])
-
-        nc.scalar.dma_start(out=rows[0:8, :], in_=gain.rearrange("(r c) -> r c", c=P))
-        nc.scalar.dma_start(out=rows[8:16, :], in_=mass.rearrange("b (h c) -> (b h) c", c=P))
         nc.scalar.copy(out=ident16[:], in_=ident32[:])
-        load_x(0, 0, 0, HALF)
-        load_x(0, 1, 0, HALF)
+        load_x(0, 0, 0, DIM)
+        nc.sync.dma_start(out=rows[0:8, :], in_=gain.rearrange("(r c) -> r c", c=P))
+        nc.sync.dma_start(out=rows[8:16, :], in_=mass.rearrange("b (h c) -> (b h) c", c=P))
+        load_x(0, 1, 0, DIM)
         for q in range(4):
             nc.sync.dma_start(
                 out=a_plane[32 * q:32 * q + 4, :, :].bitcast(I32),
                 in_=a_scales[:, 4 * q:4 * q + 4, :].rearrange("g r n -> r g n").bitcast(I32))
-        load_x(0, 0, HALF, DIM)
         load_a(0, PASSES)
-        load_x(0, 1, HALF, DIM)
-        load_centres(0)
-        load_centres(1)
-        load_x(1, 0, 0, HALF)
-        load_x(1, 1, 0, HALF)
+        load_x(1, 0, 0, DIM)
+        nc.sync.dma_start(out=cen[:], in_=centres.rearrange("(ct p) d -> p ct d", p=P))
+        load_x(1, 1, 0, DIM)
         load_a(PASSES, 2 * PASSES)
-        load_x(1, 0, HALF, DIM)
-        load_x(1, 1, HALF, DIM)
+        load_x(2, 0, 0, DIM)
+        load_x(2, 1, 0, DIM)
         load_a(2 * PASSES, IMG * PASSES)
-        for b in range(2, IMG):
-            for g in range(PASSES):
-                load_x(b, g, 0, DIM)
+        load_x(3, 0, 0, DIM)
+        load_x(3, 1, 0, DIM)
 
         grouped = {}
         xq = {}
@@ -101,15 +100,15 @@ def tile_vlad_residual_sums_k2_kernel(tc, a_words, a_scales, x, mass, centres, g
         def interleave(engine_copy, u, g, c0, c1):
             b, h = divmod(u, 2)
             if (u, g) not in grouped:
-                grouped[u, g] = work.tile([P, HALF, PACK], BF16, name="grouped", align_bytes=64)
+                grouped[u, g] = work.tile([P, HALF, PACK], BF16, name="grouped", bufs=8, align_bytes=64)
             if c1 > c0:
                 engine_copy(
                     out=grouped[u, g][:, c0:c1, :].rearrange("p (c i) t -> p c t i", i=4),
                     in_=raw[b, g, h][:, :, c0:c1].rearrange("p t (c i) -> p c t i", i=4))
 
         def quantize_x(u, g):
-            codes = work.tile([P, HALF], U32, name="x_codes", align_bytes=64)
-            plane = work.tile([P, HALF], U8, name="x_plane", align_bytes=64)
+            codes = work.tile([P, HALF], U32, name="x_codes", bufs=8, align_bytes=64)
+            plane = work.tile([P, HALF], U8, name="x_plane", bufs=8, align_bytes=64)
             nc.vector.quantize_mx(out=codes[:].bitcast(E4M3X4), scales=plane[:],
                                   in_=grouped[u, g][:].rearrange("p c t -> p (c t)"))
             xq[u, g] = (codes, plane)
@@ -132,7 +131,7 @@ def tile_vlad_residual_sums_k2_kernel(tc, a_words, a_scales, x, mass, centres, g
             if ct == 0:
                 ys[u] = work.tile([P, CTILES, HALF], F32, name="y", bufs=UNITS, align_bytes=64)
             nc.vector.scalar_tensor_tensor(
-                out=ys[u][:, ct, :], in0=cen[:, h, ct, :],
+                out=ys[u][:, ct, :], in0=cen[:, ct, h * HALF:(h + 1) * HALF],
                 scalar=neg_mass[:, CTILES * b + ct:CTILES * b + ct + 1], in1=acc[u, ct][:],
                 op0=ALU.mult, op1=ALU.add)
 
@@ -142,23 +141,36 @@ def tile_vlad_residual_sums_k2_kernel(tc, a_words, a_scales, x, mass, centres, g
                                     in1=gain_all[:, h * HALF:(h + 1) * HALF], op=ALU.mult)
 
         turned = {}
+        y16 = {}
 
-        def turn(u, ct):
-            turned[u, ct] = psum.tile([P, PACK, P], F32, name="turned")
-            for t in range(PACK):
-                nc.tensor.transpose(turned[u, ct][:, t, :], ys[u][:, ct, t:HALF:PACK], ident32[:])
+        def rounded(u, ct):
+            if u not in y16:
+                y16[u] = work.tile([P, CTILES, HALF], BF16, name="y16", bufs=3, align_bytes=64)
+            return y16[u][:, ct, :]
 
-        def round_y(u, ct):
-            if ct == 0:
-                yb[u] = work.tile([P, CLU, PACK], BF16, name="yb", bufs=3, align_bytes=64)
-            nc.scalar.copy(out=yb[u][:, ct * P:(ct + 1) * P, :], in_=turned[u, ct][:].rearrange("p t c -> p c t"))
+        def round_on_gpsimd(u, ct):
+            nc.gpsimd.tensor_scalar(out=rounded(u, ct), in0=ys[u][:, ct, :], scalar1=1.0, scalar2=0.0,
+                                    op0=ALU.mult, op1=ALU.add)
+
+        def turn(u, ct0, ct1):
+            bank = psum.tile([P, 2, (ct1 - ct0) * P], F32, name="turned")
+            turned[u, ct0] = bank
+            for ct in range(ct0, ct1):
+                words = y16[u][:, ct, :].bitcast(F32)
+                for w in range(2):
+                    nc.tensor.transpose(bank[:, w, (ct - ct0) * P:(ct - ct0 + 1) * P], words[:, w:HALF // 2:2], ident32[:])
+
+        def gather_words(u, ct0, ct1):
+            if u not in yb:
+                yb[u] = work.tile([P, CLU, 2], F32, name="yb", bufs=3, align_bytes=64)
+            nc.scalar.copy(out=yb[u][:, ct0 * P:ct1 * P, :], in_=turned[u, ct0][:].rearrange("p w c -> p c w"))
 
         def quantize_y(u, c0, c1):
             b, h = divmod(u, 2)
             m = slice(b * CLU + c0, b * CLU + c1)
             plane = late_plane[:, h, c0:c1] if b == IMG - 1 else early_plane[:, h, m]
             nc.vector.quantize_mx(out=y_codes[:, h, m].bitcast(E4M3X4), scales=plane,
-                                  in_=yb[u][:, c0:c1, :].rearrange("p c t -> p (c t)"))
+                                  in_=yb[u][:, c0:c1, :].rearrange("p c w -> p (c w)").bitcast(BF16))
 
         def store_y(u, ct0, ct1):
             b, h = divmod(u, 2)
@@ -186,47 +198,50 @@ def tile_vlad_residual_sums_k2_kernel(tc, a_words, a_scales, x, mass, centres, g
                 nc.tensor.transpose(spread[:, j * P:(j + 1) * P], cols[:, j:j + 1].to_broadcast([P, P]), ident16[:])
             nc.scalar.copy(out=gain_all[:], in_=spread[:])
 
-        for s in range(UNITS):
-            v0, v1 = V_COLS[s]
-            interleave(nc.scalar.copy, s, 0, v0, HALF)
-            interleave(nc.vector.tensor_copy, s, 0, 0, v0)
-            interleave(nc.scalar.copy, s, 1, v1, HALF)
-            interleave(nc.vector.tensor_copy, s, 1, 0, v1)
-            if s == 0:
+        for token in ORDER.split():
+            kind, n = token[0], int(token[1:])
+            if kind in "ISQ":
+                b, g, h = CHUNKS[n]
+                if kind == "I":
+                    interleave(nc.vector.tensor_copy, 2 * b + h, g, 0, V_COLS[n])
+                elif kind == "S":
+                    interleave(nc.scalar.copy, 2 * b + h, g, V_COLS[n], HALF)
+                else:
+                    quantize_x(2 * b + h, g)
+            elif kind == "K":
                 spread_constants()
-            if s >= 2:
+            elif kind == "M":
+                multiply(n // 10, n % 10)
+            elif kind == "s":
                 for ct in range(CTILES):
-                    round_y(s - 2, ct)
-            if s >= 1:
+                    residual(n, ct)
+            elif kind == "t":
                 for ct in range(CTILES):
-                    residual(s - 1, ct)
-                for ct in range(CTILES):
-                    scale(s - 1, ct)
-                store_y(s - 1, 0, CTILES)
-                turn(s - 1, 0)
-            for g in range(PASSES):
-                quantize_x(s, g)
-                multiply(s, g)
-            if s >= 1:
-                turn(s - 1, 1)
-            if s >= 3:
-                quantize_y(s - 3, 0, CLU)
-                store_codes(s - 3, 0, CLU)
+                    scale(n, ct)
+                    round_on_gpsimd(n, ct)
+                store_y(n, 0, CTILES)
+            elif kind == "T":
+                turn(n, 0, CTILES)
+            elif kind == "c":
+                gather_words(n, 0, CTILES)
+            elif kind == "q":
+                quantize_y(n, 0, CLU)
+                store_codes(n, 0, CLU)
+                if n == 5:
+                    for q in range(4):
+                        store_scales(nc.sync, q, early_plane, 0, (IMG - 1) * CLU)
 
         last = UNITS - 1
-        quantize_y(last - 2, 0, CLU)
-        store_codes(last - 2, 0, CLU)
-        for q in range(4):
-            store_scales(nc.sync, q, early_plane, 0, (IMG - 1) * CLU)
-        for ct in range(CTILES):
-            round_y(last - 1, ct)
-        for ct in range(CTILES):
-            residual(last, ct)
-        for ct in range(CTILES):
-            scale(last, ct)
-            store_y(last, ct, ct + 1)
-            turn(last, ct)
-            round_y(last, ct)
+        scale(last, 0)
+        store_y(last, 0, 1)
+        nc.scalar.copy(out=rounded(last, 0), in_=ys[last][:, 0, :])
+        nc.vector.tensor_tensor(out=rounded(last, 1), in0=ys[last][:, 1, :], in1=gain_all[:, HALF:DIM], op=ALU.mult)
+        turn(last, 0, 1)
+        turn(last, 1, 2)
+        scale(last, 1)
+        store_y(last, 1, 2)
+        gather_words(last, 0, 1)
+        gather_words(last, 1, 2)
         quantize_y(last - 1, 0, CLU)
         store_codes(last - 1, 0, CLU)
         for ct in range(CTILES):

@@ -24,14 +24,16 @@ PASSES = PTS // K_PASS
 CTILES = CLU // P
 UNITS = IMG * (DIM // HALF)
 
-V_COLS = [512, 256, 512, 96, 128, 128, 128, 208, 0, 128, 0, 96, 0, 96, 0, 64]
+V_COLS = [448, 384, 512, 0, 384, 0, 192, 192, 0, 384, 192, 0, 0, 0, 0, 0]
 CHUNKS = ([(b, g, h) for b in (0, 1) for g in (0, 1) for h in (0, 1)]
           + [(b, g, h) for b in (2, 3) for h in (0, 1) for g in (0, 1)])
-ORDER = ("I0 S0 S1 K0 I1 Q0 Q1 M00 M10 S2 S3 I2 I3 Q2 M01 Q3 M11 S4 S5 I4 I5 s0 Q4 t0 s1 T0 M20 S6 Q5 S7 c0 I6 I7 Q6 M21 M30 t1 s2 T1 Q7 M31 "
-         "S8 S9 c1 q0 I9 t2 s3 T2 Q8 M40 Q9 M41 "
-         "S10 S11 c2 q1 I11 t3 s4 T3 Q10 M50 Q11 M51 "
-         "S12 S13 c3 q2 I13 t4 s5 T4 Q12 M60 Q13 M61 "
-         "S14 c4 S15 I15 q3 t5 s6 T5 Q14 M70 c5 q4 Q15 M71 q5 t6 s7 T6 c6")
+ORDER = ("I0 S0 S1 K0 I1 Q0 Q1 M00 M10 I2 S3 Q2 M01 Q3 M11 S4 S5 I4 Q4 s0 M20 "
+         "t00 Q5 t01 y0 S6 S7 s1 T0 M30 I6 I7 Q6 M21 S8 S9 "
+         "t10 Q7 M31 t11 y1 s2 T1 I9 S10 S11 I10 "
+         "t20 Q8 M40 t21 y2 s3 T2 Q9 M41 c0 S12 "
+         "t30 Q10 M50 t31 y3 s4 T3 q0 Q11 M51 S13 c1 S14 "
+         "t40 Q12 M60 t41 y4 s5 T4 q1 Q13 M61 c2 S15 "
+         "t50 Q14 M70 t51 y5 s6 T5 t60 z60 q2 Q15 M71 c3 c4 c5 q3 q4 q5 t61 z61 s7 T6")
 
 
 def tile_vlad_residual_sums_k2_kernel(tc, a_words, a_scales, x, mass, centres, gain, out_0, out_1, out_2):
@@ -47,11 +49,11 @@ def tile_vlad_residual_sums_k2_kernel(tc, a_words, a_scales, x, mass, centres, g
         rows = keep.tile([P, P], BF16, name="rows", align_bytes=64)
         cols = keep.tile([P, 8], BF16, name="cols", align_bytes=64)
         neg_mass = keep.tile([P, 8], F32, name="neg_mass", align_bytes=64)
-        gain_all = keep.tile([P, DIM], BF16, name="gain_all", align_bytes=64)
+        gain_all = psum.tile([P, DIM], BF16, name="gain_all", bufs=1)
         cen = keep.tile([P, CTILES, DIM], BF16, name="cen", align_bytes=64)
         a_codes = keep.tile([P, IMG * PASSES, CLU], U32, name="a_codes", align_bytes=64)
         a_plane = keep.tile([P, IMG * PASSES, CLU], U8, name="a_plane", align_bytes=64)
-        y_codes = keep.tile([P, 2, IMG * CLU], U32, name="y_codes", align_bytes=64)
+        y_codes = [keep.tile([P, 2, CLU], U32, name="y_codes%d" % b, align_bytes=64) for b in range(IMG)]
         early_plane = keep.tile([P, 2, (IMG - 1) * CLU], U8, name="early_plane", align_bytes=64)
         late_plane = keep.tile([P, 2, CLU], U8, name="late_plane", align_bytes=64)
         raw = {}
@@ -153,7 +155,7 @@ def tile_vlad_residual_sums_k2_kernel(tc, a_words, a_scales, x, mass, centres, g
                                     op0=ALU.mult, op1=ALU.add)
 
         def turn(u, ct0, ct1):
-            bank = psum.tile([P, 2, (ct1 - ct0) * P], F32, name="turned")
+            bank = psum.tile([P, 2, (ct1 - ct0) * P], F32, name="turned", bufs=3)
             turned[u, ct0] = bank
             for ct in range(ct0, ct1):
                 words = y16[u][:, ct, :].bitcast(F32)
@@ -162,14 +164,14 @@ def tile_vlad_residual_sums_k2_kernel(tc, a_words, a_scales, x, mass, centres, g
 
         def gather_words(u, ct0, ct1):
             if u not in yb:
-                yb[u] = work.tile([P, CLU, 2], F32, name="yb", bufs=3, align_bytes=64)
+                yb[u] = work.tile([P, CLU, 2], F32, name="yb", bufs=4, align_bytes=64)
             nc.scalar.copy(out=yb[u][:, ct0 * P:ct1 * P, :], in_=turned[u, ct0][:].rearrange("p w c -> p c w"))
 
         def quantize_y(u, c0, c1):
             b, h = divmod(u, 2)
             m = slice(b * CLU + c0, b * CLU + c1)
             plane = late_plane[:, h, c0:c1] if b == IMG - 1 else early_plane[:, h, m]
-            nc.vector.quantize_mx(out=y_codes[:, h, m].bitcast(E4M3X4), scales=plane,
+            nc.vector.quantize_mx(out=y_codes[b][:, h, c0:c1].bitcast(E4M3X4), scales=plane,
                                   in_=yb[u][:, c0:c1, :].rearrange("p c w -> p (c w)").bitcast(BF16))
 
         def store_y(u, ct0, ct1):
@@ -186,17 +188,15 @@ def tile_vlad_residual_sums_k2_kernel(tc, a_words, a_scales, x, mass, centres, g
             b, h = divmod(u, 2)
             m = slice(b * CLU + c0, b * CLU + c1)
             nc.sync.dma_start(out=out_1[h][:, m, :].rearrange("p m t -> p (m t)").bitcast(I32),
-                              in_=y_codes[:, h, m].bitcast(I32))
+                              in_=y_codes[b][:, h, c0:c1].bitcast(I32))
 
         def spread_constants():
-            first = psum.tile([P, P], BF16, name="turned")
+            first = psum.tile([P, P], BF16, name="turned", bufs=3)
             nc.tensor.transpose(first[:], rows[:], ident16[:])
             nc.scalar.copy(out=cols[:], in_=first[:, 0:8])
             nc.scalar.activation(out=neg_mass[:], in_=first[:, 8:16], func=ACT.Copy, scale=-1.0)
-            spread = psum.tile([P, DIM], BF16, name="turned")
             for j in range(8):
-                nc.tensor.transpose(spread[:, j * P:(j + 1) * P], cols[:, j:j + 1].to_broadcast([P, P]), ident16[:])
-            nc.scalar.copy(out=gain_all[:], in_=spread[:])
+                nc.tensor.transpose(gain_all[:, j * P:(j + 1) * P], cols[:, j:j + 1].to_broadcast([P, P]), ident16[:])
 
         for token in ORDER.split():
             kind, n = token[0], int(token[1:])
@@ -216,17 +216,22 @@ def tile_vlad_residual_sums_k2_kernel(tc, a_words, a_scales, x, mass, centres, g
                 for ct in range(CTILES):
                     residual(n, ct)
             elif kind == "t":
-                for ct in range(CTILES):
-                    scale(n, ct)
-                    round_on_gpsimd(n, ct)
+                scale(n // 10, n % 10)
+                round_on_gpsimd(n // 10, n % 10)
+            elif kind == "y":
                 store_y(n, 0, CTILES)
+            elif kind == "z":
+                store_y(n // 10, n % 10, n % 10 + 1)
             elif kind == "T":
                 turn(n, 0, CTILES)
             elif kind == "c":
                 gather_words(n, 0, CTILES)
             elif kind == "q":
                 quantize_y(n, 0, CLU)
-                store_codes(n, 0, CLU)
+                if n % 2:
+                    m = slice(n // 2 * CLU, (n // 2 + 1) * CLU)
+                    nc.sync.dma_start(out=out_1[:, :, m, :].rearrange("g p m t -> p g (m t)").bitcast(I32),
+                                      in_=y_codes[n // 2][:].bitcast(I32))
                 if n == 5:
                     for q in range(4):
                         store_scales(nc.sync, q, early_plane, 0, (IMG - 1) * CLU)
@@ -236,15 +241,16 @@ def tile_vlad_residual_sums_k2_kernel(tc, a_words, a_scales, x, mass, centres, g
         store_y(last, 0, 1)
         nc.scalar.copy(out=rounded(last, 0), in_=ys[last][:, 0, :])
         nc.vector.tensor_tensor(out=rounded(last, 1), in0=ys[last][:, 1, :], in1=gain_all[:, HALF:DIM], op=ALU.mult)
-        turn(last, 0, 1)
         turn(last, 1, 2)
+        turn(last, 0, 1)
         scale(last, 1)
         store_y(last, 1, 2)
-        gather_words(last, 0, 1)
+        gather_words(last - 1, 0, CTILES)
         gather_words(last, 1, 2)
+        gather_words(last, 0, 1)
         quantize_y(last - 1, 0, CLU)
         store_codes(last - 1, 0, CLU)
-        for ct in range(CTILES):
+        for ct in (1, 0):
             quantize_y(last, ct * P, (ct + 1) * P)
             store_codes(last, ct * P, (ct + 1) * P)
         for q in range(4):

@@ -14,7 +14,6 @@ U8 = mybir.dt.uint8
 E4M3X4 = mybir.dt.float8_e4m3fn_x4
 E5M2X4 = mybir.dt.float8_e5m2_x4
 ALU = mybir.AluOpType
-ACT = mybir.ActivationFunctionType
 
 P = 128
 PACK = 4
@@ -24,16 +23,7 @@ PASSES = PTS // K_PASS
 CTILES = CLU // P
 UNITS = IMG * (DIM // HALF)
 
-V_COLS = [448, 384, 512, 0, 384, 0, 192, 192, 0, 384, 192, 0, 0, 0, 0, 0]
-CHUNKS = ([(b, g, h) for b in (0, 1) for g in (0, 1) for h in (0, 1)]
-          + [(b, g, h) for b in (2, 3) for h in (0, 1) for g in (0, 1)])
-ORDER = ("I0 S0 S1 K0 I1 Q0 Q1 M00 M10 I2 S3 Q2 M01 Q3 M11 S4 S5 I4 Q4 s0 M20 "
-         "t00 Q5 t01 y0 S6 S7 s1 T0 M30 I6 I7 Q6 M21 S8 S9 "
-         "t10 Q7 M31 t11 y1 s2 T1 I9 S10 S11 I10 "
-         "t20 Q8 M40 t21 y2 s3 T2 Q9 M41 c0 S12 "
-         "t30 Q10 M50 t31 y3 s4 T3 q0 Q11 M51 S13 c1 S14 "
-         "t40 Q12 M60 t41 y4 s5 T4 q1 Q13 M61 c2 S15 "
-         "t50 Q14 M70 t51 y5 s6 T5 t60 z60 q2 Q15 M71 c3 c4 c5 q3 q4 q5 t61 z61 s7 T6")
+SHARE_FIRST, SHARE_SECOND, SHARE_CATCH_UP, SHARE_UNIT3, SHARE_STEADY = 288, 224, 448, 128, 192
 
 
 def tile_vlad_residual_sums_k2_kernel(tc, a_words, a_scales, x, mass, centres, gain, out_0, out_1, out_2):
@@ -50,54 +40,67 @@ def tile_vlad_residual_sums_k2_kernel(tc, a_words, a_scales, x, mass, centres, g
         cols = keep.tile([P, 8], BF16, name="cols", align_bytes=64)
         neg_mass = keep.tile([P, 8], F32, name="neg_mass", align_bytes=64)
         gain_all = psum.tile([P, DIM], BF16, name="gain_all", bufs=1)
-        cen = keep.tile([P, CTILES, DIM], BF16, name="cen", align_bytes=64)
-        a_codes = keep.tile([P, IMG * PASSES, CLU], U32, name="a_codes", align_bytes=64)
-        a_plane = keep.tile([P, IMG * PASSES, CLU], U8, name="a_plane", align_bytes=64)
+        cen = [keep.tile([P, CTILES, HALF], BF16, name="cen%d" % h, align_bytes=64) for h in range(2)]
+        a_codes = [keep.tile([P, PASSES, CLU], U32, name="a_codes%d" % b, align_bytes=64) for b in range(IMG)]
+        a_planes = [keep.tile([P, n * PASSES, CLU], U8, name="a_plane%d" % n, align_bytes=64) for n in (1, IMG - 1)]
         y_codes = [keep.tile([P, 2, CLU], U32, name="y_codes%d" % b, align_bytes=64) for b in range(IMG)]
-        early_plane = keep.tile([P, 2, (IMG - 1) * CLU], U8, name="early_plane", align_bytes=64)
-        late_plane = keep.tile([P, 2, CLU], U8, name="late_plane", align_bytes=64)
+        y_planes = [keep.tile([P, 2, 2 * CLU], U8, name="y_plane%d" % n, align_bytes=64) for n in range(2)]
         raw = {}
 
-        def load_x(b, g, c0, c1):
-            src = x[b, g * K_PASS:(g + 1) * K_PASS, c0:c1].rearrange("(p j) d -> p j d", j=PACK)
-            piece = keep.tile([P, PACK, c1 - c0], BF16, name="raw%d%d%d" % (b, g, c0), align_bytes=64)
-            nc.sync.dma_start(out=piece[:], in_=src)
-            for c in range(c0, c1, HALF):
-                raw[b, g, c // HALF] = piece[:, :, c - c0:c - c0 + HALF]
+        def load_x(b, g):
+            raw[b, g] = keep.tile([P, PACK, DIM], BF16, name="raw%d%d" % (b, g), align_bytes=64)
+            nc.sync.dma_start(out=raw[b, g][:], in_=x[b, g * K_PASS:(g + 1) * K_PASS, :].rearrange("(p j) d -> p j d", j=PACK))
 
-        def load_a(g0, g1):
-            src = a_words[g0:g1].rearrange("g p n t -> p g (n t)").bitcast(I32)
-            nc.sync.dma_start(out=a_codes[:, g0:g1, :].bitcast(I32), in_=src)
+        def load_a(b):
+            src = a_words[PASSES * b:PASSES * (b + 1)].rearrange("g p n t -> p g (n t)").bitcast(I32)
+            nc.sync.dma_start(out=a_codes[b][:].bitcast(I32), in_=src)
+
+        def load_centres(h):
+            nc.sync.dma_start(out=cen[h][:], in_=centres[:, h * HALF:(h + 1) * HALF].rearrange("(ct p) d -> p ct d", p=P))
+
+        def load_scales(plane, g0, g1):
+            for q in range(4):
+                nc.sync.dma_start(
+                    out=plane[32 * q:32 * q + 4, :, :].bitcast(I32),
+                    in_=a_scales[g0:g1, 4 * q:4 * q + 4, :].rearrange("g r n -> r g n").bitcast(I32))
 
         nc.vector.memset(rows[:], 0.0)
-        nc.vector.memset(a_plane[:].rearrange("p g n -> p (g n)").bitcast(I32), 0)
+        for plane in a_planes:
+            nc.vector.memset(plane[:].rearrange("p g n -> p (g n)").bitcast(I32), 0)
         make_identity(nc, ident32[:])
 
-        nc.scalar.copy(out=ident16[:], in_=ident32[:])
-        load_x(0, 0, 0, DIM)
+        load_x(0, 0)
         nc.sync.dma_start(out=rows[0:8, :], in_=gain.rearrange("(r c) -> r c", c=P))
         nc.sync.dma_start(out=rows[8:16, :], in_=mass.rearrange("b (h c) -> (b h) c", c=P))
-        load_x(0, 1, 0, DIM)
-        for q in range(4):
-            nc.sync.dma_start(
-                out=a_plane[32 * q:32 * q + 4, :, :].bitcast(I32),
-                in_=a_scales[:, 4 * q:4 * q + 4, :].rearrange("g r n -> r g n").bitcast(I32))
-        load_a(0, PASSES)
-        load_x(1, 0, 0, DIM)
-        nc.sync.dma_start(out=cen[:], in_=centres.rearrange("(ct p) d -> p ct d", p=P))
-        load_x(1, 1, 0, DIM)
-        load_a(PASSES, 2 * PASSES)
-        load_x(2, 0, 0, DIM)
-        load_x(2, 1, 0, DIM)
-        load_a(2 * PASSES, IMG * PASSES)
-        load_x(3, 0, 0, DIM)
-        load_x(3, 1, 0, DIM)
+        nc.scalar.copy(out=ident16[:], in_=ident32[:])
+        load_x(0, 1)
+        load_scales(a_planes[0], 0, PASSES)
+        load_a(0)
+        load_centres(0)
+        load_x(1, 0)
+        load_centres(1)
+        load_x(1, 1)
+        load_scales(a_planes[1], PASSES, IMG * PASSES)
+        load_a(1)
+        for b in range(2, IMG):
+            load_x(b, 0)
+            load_x(b, 1)
+            load_a(b)
 
         grouped = {}
         xq = {}
         acc = {}
         ys = {}
         yb = {}
+        turned = {}
+        y16 = {}
+
+        def vector_share(u, g):
+            if u < 2:
+                return SHARE_FIRST if g == 0 else SHARE_SECOND
+            if g == 0 or u == UNITS - 1:
+                return 0
+            return SHARE_CATCH_UP if u == 2 else SHARE_UNIT3 if u == 3 else SHARE_STEADY
 
         def interleave(engine_copy, u, g, c0, c1):
             b, h = divmod(u, 2)
@@ -106,11 +109,17 @@ def tile_vlad_residual_sums_k2_kernel(tc, a_words, a_scales, x, mass, centres, g
             if c1 > c0:
                 engine_copy(
                     out=grouped[u, g][:, c0:c1, :].rearrange("p (c i) t -> p c t i", i=4),
-                    in_=raw[b, g, h][:, :, c0:c1].rearrange("p t (c i) -> p c t i", i=4))
+                    in_=raw[b, g][:, :, h * HALF + c0:h * HALF + c1].rearrange("p t (c i) -> p c t i", i=4))
+
+        def interleave_on_vector(u, g):
+            interleave(nc.vector.tensor_copy, u, g, 0, vector_share(u, g))
+
+        def interleave_on_scalar(u, g):
+            interleave(nc.scalar.copy, u, g, vector_share(u, g), HALF)
 
         def quantize_x(u, g):
-            codes = work.tile([P, HALF], U32, name="x_codes", bufs=8, align_bytes=64)
-            plane = work.tile([P, HALF], U8, name="x_plane", bufs=8, align_bytes=64)
+            codes = work.tile([P, HALF], U32, name="x_codes", bufs=6, align_bytes=64)
+            plane = work.tile([P, HALF], U8, name="x_plane", bufs=6, align_bytes=64)
             nc.vector.quantize_mx(out=codes[:].bitcast(E4M3X4), scales=plane[:],
                                   in_=grouped[u, g][:].rearrange("p c t -> p (c t)"))
             xq[u, g] = (codes, plane)
@@ -118,13 +127,14 @@ def tile_vlad_residual_sums_k2_kernel(tc, a_words, a_scales, x, mass, centres, g
         def multiply(u, g):
             b = u // 2
             codes, plane = xq[u, g]
+            a_scale = a_planes[0][:, g, :] if b == 0 else a_planes[1][:, PASSES * (b - 1) + g, :]
             for ct in range(CTILES):
                 if g == 0:
                     acc[u, ct] = psum.tile([P, HALF], F32, name="acc")
                 cl = slice(ct * P, (ct + 1) * P)
                 nc.tensor.matmul_mx(
                     out=acc[u, ct][:],
-                    lhsT=a_codes[:, PASSES * b + g, cl].bitcast(E5M2X4), lhsT_scale=a_plane[:, PASSES * b + g, cl],
+                    lhsT=a_codes[b][:, g, cl].bitcast(E5M2X4), lhsT_scale=a_scale[:, cl],
                     rhs=codes[:].bitcast(E4M3X4), rhs_scale=plane[:],
                     start=(g == 0), stop=(g == PASSES - 1))
 
@@ -133,24 +143,21 @@ def tile_vlad_residual_sums_k2_kernel(tc, a_words, a_scales, x, mass, centres, g
             if ct == 0:
                 ys[u] = work.tile([P, CTILES, HALF], F32, name="y", bufs=UNITS, align_bytes=64)
             nc.vector.scalar_tensor_tensor(
-                out=ys[u][:, ct, :], in0=cen[:, ct, h * HALF:(h + 1) * HALF],
+                out=ys[u][:, ct, :], in0=cen[h][:, ct, :],
                 scalar=neg_mass[:, CTILES * b + ct:CTILES * b + ct + 1], in1=acc[u, ct][:],
                 op0=ALU.mult, op1=ALU.add)
 
-        def scale(u, ct):
+        def scale(u, ct, out):
             h = u % 2
-            nc.vector.tensor_tensor(out=ys[u][:, ct, :], in0=ys[u][:, ct, :],
-                                    in1=gain_all[:, h * HALF:(h + 1) * HALF], op=ALU.mult)
-
-        turned = {}
-        y16 = {}
+            nc.vector.tensor_tensor(out=out, in0=ys[u][:, ct, :], in1=gain_all[:, h * HALF:(h + 1) * HALF], op=ALU.mult)
 
         def rounded(u, ct):
             if u not in y16:
                 y16[u] = work.tile([P, CTILES, HALF], BF16, name="y16", bufs=3, align_bytes=64)
             return y16[u][:, ct, :]
 
-        def round_on_gpsimd(u, ct):
+        def scale_and_round(u, ct):
+            scale(u, ct, ys[u][:, ct, :])
             nc.gpsimd.tensor_scalar(out=rounded(u, ct), in0=ys[u][:, ct, :], scalar1=1.0, scalar2=0.0,
                                     op0=ALU.mult, op1=ALU.add)
 
@@ -169,8 +176,7 @@ def tile_vlad_residual_sums_k2_kernel(tc, a_words, a_scales, x, mass, centres, g
 
         def quantize_y(u, c0, c1):
             b, h = divmod(u, 2)
-            m = slice(b * CLU + c0, b * CLU + c1)
-            plane = late_plane[:, h, c0:c1] if b == IMG - 1 else early_plane[:, h, m]
+            plane = y_planes[b // 2][:, h, b % 2 * CLU + c0:b % 2 * CLU + c1]
             nc.vector.quantize_mx(out=y_codes[b][:, h, c0:c1].bitcast(E4M3X4), scales=plane,
                                   in_=yb[u][:, c0:c1, :].rearrange("p c w -> p (c w)").bitcast(BF16))
 
@@ -190,68 +196,79 @@ def tile_vlad_residual_sums_k2_kernel(tc, a_words, a_scales, x, mass, centres, g
             nc.sync.dma_start(out=out_1[h][:, m, :].rearrange("p m t -> p (m t)").bitcast(I32),
                               in_=y_codes[b][:, h, c0:c1].bitcast(I32))
 
+        def finish_planes(u):
+            quantize_y(u, 0, CLU)
+            b = u // 2
+            if u % 2:
+                m = slice(b * CLU, (b + 1) * CLU)
+                nc.sync.dma_start(out=out_1[:, :, m, :].rearrange("g p m t -> p g (m t)").bitcast(I32),
+                                  in_=y_codes[b][:].bitcast(I32))
+            if u == UNITS // 2 - 1:
+                for q in range(4):
+                    store_scales(nc.sync, q, y_planes[0], 0, 2 * CLU)
+
         def spread_constants():
             first = psum.tile([P, P], BF16, name="turned", bufs=3)
             nc.tensor.transpose(first[:], rows[:], ident16[:])
-            nc.scalar.copy(out=cols[:], in_=first[:, 0:8])
-            nc.scalar.activation(out=neg_mass[:], in_=first[:, 8:16], func=ACT.Copy, scale=-1.0)
+            nc.vector.tensor_copy(out=cols[:], in_=first[:, 0:8])
+            nc.vector.tensor_scalar(out=neg_mass[:], in0=first[:, 8:16], scalar1=-1.0, scalar2=None, op0=ALU.mult)
             for j in range(8):
                 nc.tensor.transpose(gain_all[:, j * P:(j + 1) * P], cols[:, j:j + 1].to_broadcast([P, P]), ident16[:])
 
-        for token in ORDER.split():
-            kind, n = token[0], int(token[1:])
-            if kind in "ISQ":
-                b, g, h = CHUNKS[n]
-                if kind == "I":
-                    interleave(nc.vector.tensor_copy, 2 * b + h, g, 0, V_COLS[n])
-                elif kind == "S":
-                    interleave(nc.scalar.copy, 2 * b + h, g, V_COLS[n], HALF)
-                else:
-                    quantize_x(2 * b + h, g)
-            elif kind == "K":
-                spread_constants()
-            elif kind == "M":
-                multiply(n // 10, n % 10)
-            elif kind == "s":
-                for ct in range(CTILES):
-                    residual(n, ct)
-            elif kind == "t":
-                scale(n // 10, n % 10)
-                round_on_gpsimd(n // 10, n % 10)
-            elif kind == "y":
-                store_y(n, 0, CTILES)
-            elif kind == "z":
-                store_y(n // 10, n % 10, n % 10 + 1)
-            elif kind == "T":
-                turn(n, 0, CTILES)
-            elif kind == "c":
-                gather_words(n, 0, CTILES)
-            elif kind == "q":
-                quantize_y(n, 0, CLU)
-                if n % 2:
-                    m = slice(n // 2 * CLU, (n // 2 + 1) * CLU)
-                    nc.sync.dma_start(out=out_1[:, :, m, :].rearrange("g p m t -> p g (m t)").bitcast(I32),
-                                      in_=y_codes[n // 2][:].bitcast(I32))
-                if n == 5:
-                    for q in range(4):
-                        store_scales(nc.sync, q, early_plane, 0, (IMG - 1) * CLU)
-
         last = UNITS - 1
-        scale(last, 0)
-        store_y(last, 0, 1)
-        nc.scalar.copy(out=rounded(last, 0), in_=ys[last][:, 0, :])
-        nc.vector.tensor_tensor(out=rounded(last, 1), in0=ys[last][:, 1, :], in1=gain_all[:, HALF:DIM], op=ALU.mult)
-        turn(last, 1, 2)
-        turn(last, 0, 1)
-        scale(last, 1)
-        store_y(last, 1, 2)
+
+        for g in range(PASSES):
+            for u in range(2):
+                interleave_on_vector(u, g)
+                interleave_on_scalar(u, g)
+            if g == 0:
+                spread_constants()
+            for u in range(2):
+                quantize_x(u, g)
+        for u in range(2):
+            for g in range(PASSES):
+                multiply(u, g)
+        interleave_on_scalar(2, 0)
+        interleave_on_scalar(3, 0)
+        for ct in range(CTILES):
+            residual(0, ct)
+
+        for u in range(last):
+            if u >= 1:
+                quantize_x(u + 1, 1)
+                multiply(u + 1, 1)
+            if 2 <= u <= last - 2:
+                interleave_on_scalar(u + 2, 0)
+            scale_and_round(u, 0)
+            if u >= 2:
+                finish_planes(u - 2)
+            scale_and_round(u, 1)
+            store_y(u, 0, CTILES)
+            for ct in range(CTILES):
+                residual(u + 1, ct)
+            if u >= 1:
+                gather_words(u - 1, 0, CTILES)
+            turn(u, 0, CTILES)
+            if u + 2 <= last:
+                interleave_on_scalar(u + 2, 1)
+                interleave_on_vector(u + 2, 1)
+                quantize_x(u + 2, 0)
+                multiply(u + 2, 0)
+
+        finish_planes(last - 2)
+        for ct in range(CTILES):
+            scale(last, ct, rounded(last, ct))
         gather_words(last - 1, 0, CTILES)
-        gather_words(last, 1, 2)
-        gather_words(last, 0, 1)
+        for ct in range(CTILES):
+            turn(last, ct, ct + 1)
+            gather_words(last, ct, ct + 1)
+        scale(last, 0, ys[last][:, 0, :])
+        store_y(last, 0, 1)
         quantize_y(last - 1, 0, CLU)
         store_codes(last - 1, 0, CLU)
-        for ct in (1, 0):
-            quantize_y(last, ct * P, (ct + 1) * P)
-            store_codes(last, ct * P, (ct + 1) * P)
+        scale(last, 1, ys[last][:, 1, :])
+        store_y(last, 1, 2)
+        quantize_y(last, 0, CLU)
+        store_codes(last, 0, CLU)
         for q in range(4):
-            store_scales(nc.scalar if q % 2 else nc.sync, q, late_plane, (IMG - 1) * CLU, IMG * CLU)
+            store_scales(nc.scalar if q % 2 else nc.sync, q, y_planes[1], 2 * CLU, IMG * CLU)

@@ -23,7 +23,7 @@ PASSES = PTS // K_PASS
 CTILES = CLU // P
 UNITS = IMG * (DIM // HALF)
 
-SHARE_FIRST, SHARE_SECOND, SHARE_CATCH_UP, SHARE_UNIT3, SHARE_STEADY = 288, 224, 448, 128, 192
+SHARE_FIRST, SHARE_SECOND, SHARE_CATCH_UP, SHARE_UNIT3, SHARE_STEADY = 0, 0, 0, 0, 0
 
 
 def tile_vlad_residual_sums_k2_kernel(tc, a_words, a_scales, x, mass, centres, gain, out_0, out_1, out_2):

@@ -108,8 +108,8 @@ def tile_vlad_residual_sums_k2_kernel(tc, a_words, a_scales, x, mass, centres, g
                 grouped[u, g] = work.tile([P, HALF, PACK], BF16, name="grouped", bufs=8, align_bytes=64)
             if c1 > c0:
                 engine_copy(
-                    out=grouped[u, g][:, c0:c1, :].rearrange("p (c i) t -> p c t i", i=4),
-                    in_=raw[b, g][:, :, h * HALF + c0:h * HALF + c1].rearrange("p t (c i) -> p c t i", i=4))
+                    out=grouped[u, g][:, c0:c1, :].rearrange("p (c i) t -> p c t i", i=8),
+                    in_=raw[b, g][:, :, h * HALF + c0:h * HALF + c1].rearrange("p t (c i) -> p c t i", i=8))
 
         def interleave_on_vector(u, g):
             interleave(nc.vector.tensor_copy, u, g, 0, vector_share(u, g))

@@ -108,8 +108,8 @@ def tile_vlad_residual_sums_k2_kernel(tc, a_words, a_scales, x, mass, centres, g
                 grouped[u, g] = work.tile([P, HALF, PACK], BF16, name="grouped", bufs=8, align_bytes=64)
             if c1 > c0:
                 engine_copy(
-                    out=grouped[u, g][:, c0:c1, :].rearrange("p (c i) t -> p c t i", i=8),
-                    in_=raw[b, g][:, :, h * HALF + c0:h * HALF + c1].rearrange("p t (c i) -> p c t i", i=8))
+                    out=grouped[u, g][:, c0:c1, :].rearrange("p (c i) (s t) -> p c s i t", i=8, t=2),
+                    in_=raw[b, g][:, :, h * HALF + c0:h * HALF + c1].rearrange("p (s t) (c i) -> p c s i t", i=8, t=2))
 
         def interleave_on_vector(u, g):
             interleave(nc.vector.tensor_copy, u, g, 0, vector_share(u, g))

@@ -23,7 +23,9 @@ PASSES = PTS // K_PASS
 CTILES = CLU // P
 UNITS = IMG * (DIM // HALF)
 
-SHARE_FIRST, SHARE_SECOND, SHARE_CATCH_UP, SHARE_UNIT3, SHARE_STEADY = 0, 0, 0, 0, 0
+SHARE_FIRST, SHARE_SECOND, SHARE_CATCH_UP, SHARE_STEADY = 288, 224, 448, 128
+SHARE_GPSIMD = 96
+SLIVER = 64
 
 
 def tile_vlad_residual_sums_k2_kernel(tc, a_words, a_scales, x, mass, centres, gain, out_0, out_1, out_2):
@@ -98,24 +100,37 @@ def tile_vlad_residual_sums_k2_kernel(tc, a_words, a_scales, x, mass, centres, g
         def vector_share(u, g):
             if u < 2:
                 return SHARE_FIRST if g == 0 else SHARE_SECOND
-            if g == 0 or u == UNITS - 1:
-                return 0
-            return SHARE_CATCH_UP if u == 2 else SHARE_UNIT3 if u == 3 else SHARE_STEADY
+            if (u, g) == (2, 1):
+                return SHARE_CATCH_UP
+            return SHARE_STEADY if g == 0 and 4 <= u <= 5 else 0
 
-        def interleave(engine_copy, u, g, c0, c1):
+        def interleave(engine_copy, u, g, c0, c1, rows_at_a_time=2):
             b, h = divmod(u, 2)
             if (u, g) not in grouped:
                 grouped[u, g] = work.tile([P, HALF, PACK], BF16, name="grouped", bufs=8, align_bytes=64)
             if c1 > c0:
-                engine_copy(
-                    out=grouped[u, g][:, c0:c1, :].rearrange("p (c i) (s t) -> p c s i t", i=8, t=2),
-                    in_=raw[b, g][:, :, h * HALF + c0:h * HALF + c1].rearrange("p (s t) (c i) -> p c s i t", i=8, t=2))
+                src = raw[b, g][:, :, h * HALF + c0:h * HALF + c1]
+                dst = grouped[u, g][:, c0:c1, :]
+                if rows_at_a_time == 1:
+                    engine_copy(out=dst.rearrange("p (c i) t -> p c t i", i=8), in_=src.rearrange("p t (c i) -> p c t i", i=8))
+                else:
+                    engine_copy(out=dst.rearrange("p (c i) (s t) -> p c s i t", i=8, t=2),
+                                in_=src.rearrange("p (s t) (c i) -> p c s i t", i=8, t=2))
 
         def interleave_on_vector(u, g):
             interleave(nc.vector.tensor_copy, u, g, 0, vector_share(u, g))
 
+        def gpsimd_share(u, g):
+            return SHARE_GPSIMD if g == 1 and u >= 3 else 0
+
+        def gpsimd_copy(out, in_):
+            nc.gpsimd.tensor_scalar(out=out, in0=in_, scalar1=1.0, scalar2=0.0, op0=ALU.mult, op1=ALU.add)
+
+        def interleave_on_gpsimd(u, g):
+            interleave(gpsimd_copy, u, g, HALF - gpsimd_share(u, g), HALF, 1)
+
         def interleave_on_scalar(u, g):
-            interleave(nc.scalar.copy, u, g, vector_share(u, g), HALF)
+            interleave(nc.scalar.copy, u, g, vector_share(u, g), HALF - gpsimd_share(u, g))
 
         def quantize_x(u, g):
             codes = work.tile([P, HALF], U32, name="x_codes", bufs=6, align_bytes=64)
@@ -147,19 +162,19 @@ def tile_vlad_residual_sums_k2_kernel(tc, a_words, a_scales, x, mass, centres, g
                 scalar=neg_mass[:, CTILES * b + ct:CTILES * b + ct + 1], in1=acc[u, ct][:],
                 op0=ALU.mult, op1=ALU.add)
 
-        def scale(u, ct, out):
+        def scale(u, ct, out, c0=0, c1=HALF):
             h = u % 2
-            nc.vector.tensor_tensor(out=out, in0=ys[u][:, ct, :], in1=gain_all[:, h * HALF:(h + 1) * HALF], op=ALU.mult)
+            nc.vector.tensor_tensor(out=out[:, c0:c1], in0=ys[u][:, ct, c0:c1],
+                                    in1=gain_all[:, h * HALF + c0:h * HALF + c1], op=ALU.mult)
 
         def rounded(u, ct):
             if u not in y16:
                 y16[u] = work.tile([P, CTILES, HALF], BF16, name="y16", bufs=3, align_bytes=64)
             return y16[u][:, ct, :]
 
-        def scale_and_round(u, ct):
-            scale(u, ct, ys[u][:, ct, :])
-            nc.gpsimd.tensor_scalar(out=rounded(u, ct), in0=ys[u][:, ct, :], scalar1=1.0, scalar2=0.0,
-                                    op0=ALU.mult, op1=ALU.add)
+        def round_on_gpsimd(u, ct0, ct1):
+            rounded(u, ct0)
+            gpsimd_copy(y16[u][:, ct0:ct1, :], ys[u][:, ct0:ct1, :])
 
         def turn(u, ct0, ct1):
             bank = psum.tile([P, 2, (ct1 - ct0) * P], F32, name="turned", bufs=3)
@@ -230,44 +245,76 @@ def tile_vlad_residual_sums_k2_kernel(tc, a_words, a_scales, x, mass, centres, g
                 multiply(u, g)
         interleave_on_scalar(2, 0)
         interleave_on_scalar(3, 0)
+        interleave_on_scalar(2, 1)
         for ct in range(CTILES):
             residual(0, ct)
 
-        for u in range(last):
-            if u >= 1:
-                quantize_x(u + 1, 1)
-                multiply(u + 1, 1)
-            if 2 <= u <= last - 2:
-                interleave_on_scalar(u + 2, 0)
-            scale_and_round(u, 0)
-            if u >= 2:
-                finish_planes(u - 2)
-            scale_and_round(u, 1)
+        def sliver(u):
+            scale(u, 1, ys[u][:, 1, :], HALF - SLIVER, HALF)
             store_y(u, 0, CTILES)
+
+        def one_port_block(u):
+            scale(u, 0, ys[u][:, 0, :])
+            scale(u, 1, ys[u][:, 1, :], 0, HALF - SLIVER)
             for ct in range(CTILES):
                 residual(u + 1, ct)
-            if u >= 1:
-                gather_words(u - 1, 0, CTILES)
-            turn(u, 0, CTILES)
-            if u + 2 <= last:
-                interleave_on_scalar(u + 2, 1)
-                interleave_on_vector(u + 2, 1)
-                quantize_x(u + 2, 0)
-                multiply(u + 2, 0)
 
-        finish_planes(last - 2)
+        one_port_block(0)
+        for u in range(1, last - 1):
+            if u == 1:
+                interleave_on_vector(2, 1)
+            quantize_x(u + 1, 0)
+            multiply(u + 1, 0)
+            quantize_x(u + 1, 1)
+            multiply(u + 1, 1)
+            interleave_on_vector(u + 2, 0)
+            sliver(u - 1)
+            if u >= 3:
+                finish_planes(u - 3)
+            round_on_gpsimd(u - 1, 0, CTILES)
+            turn(u - 1, 0, CTILES)
+            interleave_on_gpsimd(u + 2, 1)
+            if u >= 2:
+                interleave_on_scalar(u + 2, 0)
+                gather_words(u - 2, 0, CTILES)
+            interleave_on_scalar(u + 2, 1)
+            if u < last - 2:
+                one_port_block(u)
+
         for ct in range(CTILES):
-            scale(last, ct, rounded(last, ct))
+            scale(last - 2, ct, ys[last - 2][:, ct, :])
+        store_y(last - 2, 0, CTILES)
+        round_on_gpsimd(last - 2, 0, CTILES)
+        gather_words(last - 3, 0, CTILES)
+        turn(last - 2, 0, CTILES)
+        gather_words(last - 2, 0, CTILES)
+        for ct in range(CTILES):
+            residual(last - 1, ct)
+        for ct in range(CTILES):
+            scale(last - 1, ct, ys[last - 1][:, ct, :])
+        store_y(last - 1, 0, CTILES)
+        quantize_x(last, 0)
+        multiply(last, 0)
+        finish_planes(last - 4)
+        quantize_x(last, 1)
+        multiply(last, 1)
+        finish_planes(last - 3)
+        finish_planes(last - 2)
+        rounded(last - 1, 0)
+        nc.scalar.copy(out=y16[last - 1][:], in_=ys[last - 1][:])
+        turn(last - 1, 0, CTILES)
         gather_words(last - 1, 0, CTILES)
         for ct in range(CTILES):
+            residual(last, ct)
+        for ct in range(CTILES):
+            scale(last, ct, rounded(last, ct))
             turn(last, ct, ct + 1)
             gather_words(last, ct, ct + 1)
-        scale(last, 0, ys[last][:, 0, :])
-        store_y(last, 0, 1)
+        for ct in range(CTILES):
+            scale(last, ct, ys[last][:, ct, :])
+            store_y(last, ct, ct + 1)
         quantize_y(last - 1, 0, CLU)
         store_codes(last - 1, 0, CLU)
-        scale(last, 1, ys[last][:, 1, :])
-        store_y(last, 1, 2)
         quantize_y(last, 0, CLU)
         store_codes(last, 0, CLU)
         for q in range(4):

@@ -21,10 +21,10 @@ K_PASS = P * PACK
 HALF = 512
 PASSES = PTS // K_PASS
 CTILES = CLU // P
-UNITS = IMG * (DIM // HALF)
+UNITS = IMG * CTILES
 
-SHARE_FIRST, SHARE_SECOND, SHARE_CATCH_UP, SHARE_STEADY = 288, 224, 448, 128
-SHARE_GPSIMD = 96
+SHARE_HEAD, SHARE_CATCH_UP, SHARE_STEADY = 288, 304, 112
+SHARE_GPSIMD, SHARE_GPSIMD_FIRST = 88, 384
 SLIVER = 64
 
 
@@ -42,11 +42,11 @@ def tile_vlad_residual_sums_k2_kernel(tc, a_words, a_scales, x, mass, centres, g
         cols = keep.tile([P, 8], BF16, name="cols", align_bytes=64)
         neg_mass = keep.tile([P, 8], F32, name="neg_mass", align_bytes=64)
         gain_all = psum.tile([P, DIM], BF16, name="gain_all", bufs=1)
-        cen = [keep.tile([P, CTILES, HALF], BF16, name="cen%d" % h, align_bytes=64) for h in range(2)]
+        cen = [keep.tile([P, DIM], BF16, name="cen%d" % ct, align_bytes=64) for ct in range(CTILES)]
         a_codes = [keep.tile([P, PASSES, CLU], U32, name="a_codes%d" % b, align_bytes=64) for b in range(IMG)]
         a_planes = [keep.tile([P, n * PASSES, CLU], U8, name="a_plane%d" % n, align_bytes=64) for n in (1, IMG - 1)]
         y_codes = [keep.tile([P, 2, CLU], U32, name="y_codes%d" % b, align_bytes=64) for b in range(IMG)]
-        y_planes = [keep.tile([P, 2, 2 * CLU], U8, name="y_plane%d" % n, align_bytes=64) for n in range(2)]
+        y_planes = [keep.tile([P, IMG * CLU], U8, name="y_plane%d" % n, align_bytes=64) for n in range(1)]
         raw = {}
 
         def load_x(b, g):
@@ -57,14 +57,11 @@ def tile_vlad_residual_sums_k2_kernel(tc, a_words, a_scales, x, mass, centres, g
             src = a_words[PASSES * b:PASSES * (b + 1)].rearrange("g p n t -> p g (n t)").bitcast(I32)
             nc.sync.dma_start(out=a_codes[b][:].bitcast(I32), in_=src)
 
-        def load_centres(h):
-            nc.sync.dma_start(out=cen[h][:], in_=centres[:, h * HALF:(h + 1) * HALF].rearrange("(ct p) d -> p ct d", p=P))
-
-        def load_scales(plane, g0, g1):
+        def load_scales(plane, b0, b1):
             for q in range(4):
                 nc.sync.dma_start(
                     out=plane[32 * q:32 * q + 4, :, :].bitcast(I32),
-                    in_=a_scales[g0:g1, 4 * q:4 * q + 4, :].rearrange("g r n -> r g n").bitcast(I32))
+                    in_=a_scales[PASSES * b0:PASSES * b1, 4 * q:4 * q + 4, :].rearrange("g r n -> r g n").bitcast(I32))
 
         nc.vector.memset(rows[:], 0.0)
         for plane in a_planes:
@@ -76,13 +73,13 @@ def tile_vlad_residual_sums_k2_kernel(tc, a_words, a_scales, x, mass, centres, g
         nc.sync.dma_start(out=rows[8:16, :], in_=mass.rearrange("b (h c) -> (b h) c", c=P))
         nc.scalar.copy(out=ident16[:], in_=ident32[:])
         load_x(0, 1)
-        load_scales(a_planes[0], 0, PASSES)
+        load_scales(a_planes[0], 0, 1)
         load_a(0)
-        load_centres(0)
+        nc.sync.dma_start(out=cen[0][:], in_=centres[0:P, :])
         load_x(1, 0)
-        load_centres(1)
+        nc.sync.dma_start(out=cen[1][:], in_=centres[P:2 * P, :])
         load_x(1, 1)
-        load_scales(a_planes[1], PASSES, IMG * PASSES)
+        load_scales(a_planes[1], 1, IMG)
         load_a(1)
         for b in range(2, IMG):
             load_x(b, 0)
@@ -97,130 +94,110 @@ def tile_vlad_residual_sums_k2_kernel(tc, a_words, a_scales, x, mass, centres, g
         turned = {}
         y16 = {}
 
-        def vector_share(u, g):
-            if u < 2:
-                return SHARE_FIRST if g == 0 else SHARE_SECOND
-            if (u, g) == (2, 1):
+        def vector_share(b, g, h):
+            if b == 0:
+                return SHARE_HEAD
+            if (b, g, h) in ((1, 1, 0), (2, 0, 1)):
                 return SHARE_CATCH_UP
-            return SHARE_STEADY if g == 0 and 4 <= u <= 5 else 0
+            return SHARE_STEADY if b >= 2 and h == 1 else 0
 
-        def interleave(engine_copy, u, g, c0, c1, rows_at_a_time=2):
-            b, h = divmod(u, 2)
-            if (u, g) not in grouped:
-                grouped[u, g] = work.tile([P, HALF, PACK], BF16, name="grouped", bufs=8, align_bytes=64)
-            if c1 > c0:
-                src = raw[b, g][:, :, h * HALF + c0:h * HALF + c1]
-                dst = grouped[u, g][:, c0:c1, :]
-                if rows_at_a_time == 1:
-                    engine_copy(out=dst.rearrange("p (c i) t -> p c t i", i=8), in_=src.rearrange("p t (c i) -> p c t i", i=8))
-                else:
-                    engine_copy(out=dst.rearrange("p (c i) (s t) -> p c s i t", i=8, t=2),
-                                in_=src.rearrange("p (s t) (c i) -> p c s i t", i=8, t=2))
+        def gpsimd_share(b, g, h):
+            if (b, g, h) == (1, 0, 1):
+                return SHARE_GPSIMD_FIRST
+            return SHARE_GPSIMD if b >= 2 and h == 1 else 0
 
-        def interleave_on_vector(u, g):
-            interleave(nc.vector.tensor_copy, u, g, 0, vector_share(u, g))
+        def chunk_views(b, g, h, c0, c1):
+            if (b, g, h) not in grouped:
+                grouped[b, g, h] = work.tile([P, HALF, PACK], BF16, name="grouped", bufs=8, align_bytes=64)
+            return grouped[b, g, h][:, c0:c1, :], raw[b, g][:, :, h * HALF + c0:h * HALF + c1]
 
-        def gpsimd_share(u, g):
-            return SHARE_GPSIMD if g == 1 and u >= 3 else 0
+        def interleave_on_vector(b, g, h):
+            dst, src = chunk_views(b, g, h, 0, vector_share(b, g, h))
+            nc.vector.tensor_copy(out=dst.rearrange("p (c i) t -> p c t i", i=4), in_=src.rearrange("p t (c i) -> p c t i", i=4))
 
         def gpsimd_copy(out, in_):
             nc.gpsimd.tensor_scalar(out=out, in0=in_, scalar1=1.0, scalar2=0.0, op0=ALU.mult, op1=ALU.add)
 
-        def interleave_on_gpsimd(u, g):
-            interleave(gpsimd_copy, u, g, HALF - gpsimd_share(u, g), HALF, 1)
+        def interleave_on_gpsimd(b, g, h):
+            dst, src = chunk_views(b, g, h, HALF - gpsimd_share(b, g, h), HALF)
+            gpsimd_copy(dst, src.rearrange("p t c -> p c t"))
 
-        def interleave_on_scalar(u, g):
-            interleave(nc.scalar.copy, u, g, vector_share(u, g), HALF - gpsimd_share(u, g))
+        def interleave_on_scalar(b, g, h):
+            dst, src = chunk_views(b, g, h, vector_share(b, g, h), HALF - gpsimd_share(b, g, h))
+            nc.scalar.copy(out=dst.rearrange("p (c i) (s t) -> p c s i t", i=8, t=2),
+                           in_=src.rearrange("p (s t) (c i) -> p c s i t", i=8, t=2))
 
-        def quantize_x(u, g):
-            codes = work.tile([P, HALF], U32, name="x_codes", bufs=6, align_bytes=64)
-            plane = work.tile([P, HALF], U8, name="x_plane", bufs=6, align_bytes=64)
+        def quantize_x(b, g, h):
+            codes = work.tile([P, HALF], U32, name="x_codes", bufs=8, align_bytes=64)
+            plane = work.tile([P, HALF], U8, name="x_plane", bufs=8, align_bytes=64)
             nc.vector.quantize_mx(out=codes[:].bitcast(E4M3X4), scales=plane[:],
-                                  in_=grouped[u, g][:].rearrange("p c t -> p (c t)"))
-            xq[u, g] = (codes, plane)
+                                  in_=grouped[b, g, h][:].rearrange("p c t -> p (c t)"))
+            xq[b, g, h] = (codes, plane)
 
-        def multiply(u, g):
-            b = u // 2
-            codes, plane = xq[u, g]
+        def multiply(u, g, h0=0, h1=2):
+            b, ct = divmod(u, CTILES)
             a_scale = a_planes[0][:, g, :] if b == 0 else a_planes[1][:, PASSES * (b - 1) + g, :]
-            for ct in range(CTILES):
+            cl = slice(ct * P, (ct + 1) * P)
+            for h in range(h0, h1):
+                codes, plane = xq[b, g, h]
                 if g == 0:
-                    acc[u, ct] = psum.tile([P, HALF], F32, name="acc")
-                cl = slice(ct * P, (ct + 1) * P)
+                    acc[u, h] = psum.tile([P, HALF], F32, name="acc")
                 nc.tensor.matmul_mx(
-                    out=acc[u, ct][:],
+                    out=acc[u, h][:],
                     lhsT=a_codes[b][:, g, cl].bitcast(E5M2X4), lhsT_scale=a_scale[:, cl],
                     rhs=codes[:].bitcast(E4M3X4), rhs_scale=plane[:],
                     start=(g == 0), stop=(g == PASSES - 1))
 
-        def residual(u, ct):
-            b, h = divmod(u, 2)
-            if ct == 0:
-                ys[u] = work.tile([P, CTILES, HALF], F32, name="y", bufs=UNITS, align_bytes=64)
-            nc.vector.scalar_tensor_tensor(
-                out=ys[u][:, ct, :], in0=cen[h][:, ct, :],
-                scalar=neg_mass[:, CTILES * b + ct:CTILES * b + ct + 1], in1=acc[u, ct][:],
-                op0=ALU.mult, op1=ALU.add)
+        def residual(u, h0=0, h1=2):
+            if u not in ys:
+                ys[u] = work.tile([P, DIM], F32, name="y", bufs=UNITS, align_bytes=64)
+            for h in range(h0, h1):
+                d = slice(h * HALF, (h + 1) * HALF)
+                nc.vector.scalar_tensor_tensor(
+                    out=ys[u][:, d], in0=cen[u % CTILES][:, d], scalar=neg_mass[:, u:u + 1], in1=acc[u, h][:],
+                    op0=ALU.mult, op1=ALU.add)
 
-        def scale(u, ct, out, c0=0, c1=HALF):
-            h = u % 2
-            nc.vector.tensor_tensor(out=out[:, c0:c1], in0=ys[u][:, ct, c0:c1],
-                                    in1=gain_all[:, h * HALF + c0:h * HALF + c1], op=ALU.mult)
+        def scale(u, out, d0, d1):
+            nc.vector.tensor_tensor(out=out[:, d0:d1], in0=ys[u][:, d0:d1], in1=gain_all[:, d0:d1], op=ALU.mult)
 
-        def rounded(u, ct):
+        def rounded(u):
             if u not in y16:
-                y16[u] = work.tile([P, CTILES, HALF], BF16, name="y16", bufs=3, align_bytes=64)
-            return y16[u][:, ct, :]
+                y16[u] = work.tile([P, DIM], BF16, name="y16", bufs=3, align_bytes=64)
+            return y16[u]
 
-        def round_on_gpsimd(u, ct0, ct1):
-            rounded(u, ct0)
-            gpsimd_copy(y16[u][:, ct0:ct1, :], ys[u][:, ct0:ct1, :])
-
-        def turn(u, ct0, ct1):
-            bank = psum.tile([P, 2, (ct1 - ct0) * P], F32, name="turned", bufs=3)
-            turned[u, ct0] = bank
-            for ct in range(ct0, ct1):
-                words = y16[u][:, ct, :].bitcast(F32)
+        def turn(u, h0=0, h1=2):
+            bank = psum.tile([P, h1 - h0, 2, P], F32, name="turned", bufs=3)
+            turned[u, h0] = bank
+            for h in range(h0, h1):
+                words = y16[u][:, h * HALF:(h + 1) * HALF].bitcast(F32)
                 for w in range(2):
-                    nc.tensor.transpose(bank[:, w, (ct - ct0) * P:(ct - ct0 + 1) * P], words[:, w:HALF // 2:2], ident32[:])
+                    nc.tensor.transpose(bank[:, h - h0, w, :], words[:, w:HALF // 2:2], ident32[:])
 
-        def gather_words(u, ct0, ct1):
-            if u not in yb:
-                yb[u] = work.tile([P, CLU, 2], F32, name="yb", bufs=4, align_bytes=64)
-            nc.scalar.copy(out=yb[u][:, ct0 * P:ct1 * P, :], in_=turned[u, ct0][:].rearrange("p w c -> p c w"))
+        def gather_words(u, h0=0, h1=2):
+            b, ct = divmod(u, CTILES)
+            if b not in yb:
+                yb[b] = work.tile([P, 2, CLU, 2], F32, name="yb", bufs=3, align_bytes=64)
+            nc.scalar.copy(out=yb[b][:, h0:h1, ct * P:(ct + 1) * P, :],
+                           in_=turned[u, h0][:].rearrange("p h w c -> p h c w"))
 
-        def quantize_y(u, c0, c1):
-            b, h = divmod(u, 2)
-            plane = y_planes[b // 2][:, h, b % 2 * CLU + c0:b % 2 * CLU + c1]
-            nc.vector.quantize_mx(out=y_codes[b][:, h, c0:c1].bitcast(E4M3X4), scales=plane,
-                                  in_=yb[u][:, c0:c1, :].rearrange("p c w -> p (c w)").bitcast(BF16))
+        def store_y(u, d0=0, d1=DIM):
+            b, ct = divmod(u, CTILES)
+            nc.sync.dma_start(out=out_0[b, ct * P:(ct + 1) * P, d0:d1], in_=ys[u][:, d0:d1])
 
-        def store_y(u, ct0, ct1):
-            b, h = divmod(u, 2)
-            nc.sync.dma_start(out=out_0[b].rearrange("(ct p) d -> p ct d", p=P)[:, ct0:ct1, h * HALF:(h + 1) * HALF],
-                              in_=ys[u][:, ct0:ct1, :])
+        def store_scales(queue, q, n):
+            queue.dma_start(out=out_2[:, 4 * q:4 * q + 4, :].bitcast(I32),
+                            in_=y_planes[n][32 * q:32 * q + 8, :].bitcast(I32))
 
-        def store_scales(queue, q, plane, m0, m1):
-            queue.dma_start(
-                out=out_2[:, 4 * q:4 * q + 4, m0:m1].rearrange("g r m -> r g m").bitcast(I32),
-                in_=plane[32 * q:32 * q + 4, :, :].bitcast(I32))
-
-        def store_codes(u, c0, c1):
-            b, h = divmod(u, 2)
-            m = slice(b * CLU + c0, b * CLU + c1)
-            nc.sync.dma_start(out=out_1[h][:, m, :].rearrange("p m t -> p (m t)").bitcast(I32),
-                              in_=y_codes[b][:, h, c0:c1].bitcast(I32))
-
-        def finish_planes(u):
-            quantize_y(u, 0, CLU)
-            b = u // 2
-            if u % 2:
-                m = slice(b * CLU, (b + 1) * CLU)
-                nc.sync.dma_start(out=out_1[:, :, m, :].rearrange("g p m t -> p g (m t)").bitcast(I32),
+        def finish_planes(b, h):
+            nc.vector.quantize_mx(out=y_codes[b][:, h, :].bitcast(E4M3X4),
+                                  scales=y_planes[0][4 * h:, b * CLU:(b + 1) * CLU],
+                                  in_=yb[b][:, h, :, :].rearrange("p c w -> p (c w)").bitcast(BF16))
+            if b == IMG - 1:
+                nc.sync.dma_start(out=out_1[h][:, b * CLU:(b + 1) * CLU, :].rearrange("p m t -> p (m t)").bitcast(I32),
+                                  in_=y_codes[b][:, h, :].bitcast(I32))
+            elif h == 1:
+                nc.sync.dma_start(out=out_1[:, :, b * CLU:(b + 1) * CLU, :].rearrange("g p m t -> p g (m t)").bitcast(I32),
                                   in_=y_codes[b][:].bitcast(I32))
-            if u == UNITS // 2 - 1:
-                for q in range(4):
-                    store_scales(nc.sync, q, y_planes[0], 0, 2 * CLU)
 
         def spread_constants():
             first = psum.tile([P, P], BF16, name="turned", bufs=3)
@@ -230,92 +207,103 @@ def tile_vlad_residual_sums_k2_kernel(tc, a_words, a_scales, x, mass, centres, g
             for j in range(8):
                 nc.tensor.transpose(gain_all[:, j * P:(j + 1) * P], cols[:, j:j + 1].to_broadcast([P, P]), ident16[:])
 
+        def sliver(u):
+            scale(u, ys[u], DIM - SLIVER, DIM)
+            store_y(u)
+
         last = UNITS - 1
 
         for g in range(PASSES):
-            for u in range(2):
-                interleave_on_vector(u, g)
-                interleave_on_scalar(u, g)
+            for h in range(2):
+                interleave_on_vector(0, g, h)
+                interleave_on_scalar(0, g, h)
             if g == 0:
                 spread_constants()
-            for u in range(2):
-                quantize_x(u, g)
+            for h in range(2):
+                quantize_x(0, g, h)
         for u in range(2):
             for g in range(PASSES):
                 multiply(u, g)
-        interleave_on_scalar(2, 0)
-        interleave_on_scalar(3, 0)
-        interleave_on_scalar(2, 1)
-        for ct in range(CTILES):
-            residual(0, ct)
+        interleave_on_scalar(1, 0, 0)
+        interleave_on_gpsimd(1, 0, 1)
+        interleave_on_scalar(1, 0, 1)
+        interleave_on_scalar(1, 1, 0)
+        interleave_on_scalar(1, 1, 1)
+        residual(0)
+        scale(0, ys[0], 0, HALF)
+        scale(0, ys[0], HALF, DIM - SLIVER)
+        residual(1)
 
-        def sliver(u):
-            scale(u, 1, ys[u][:, 1, :], HALF - SLIVER, HALF)
-            store_y(u, 0, CTILES)
+        def round_on_scalar(u, d0=0, d1=DIM):
+            nc.scalar.copy(out=rounded(u)[:, d0:d1], in_=ys[u][:, d0:d1])
 
-        def one_port_block(u):
-            scale(u, 0, ys[u][:, 0, :])
-            scale(u, 1, ys[u][:, 1, :], 0, HALF - SLIVER)
-            for ct in range(CTILES):
-                residual(u + 1, ct)
-
-        one_port_block(0)
-        for u in range(1, last - 1):
+        for u in range(1, last - 2):
+            b, g = divmod(u, 2)
+            nb, ng = divmod(u + 3, 2)
             if u == 1:
-                interleave_on_vector(2, 1)
-            quantize_x(u + 1, 0)
-            multiply(u + 1, 0)
-            quantize_x(u + 1, 1)
-            multiply(u + 1, 1)
-            interleave_on_vector(u + 2, 0)
+                interleave_on_vector(1, 1, 0)
+                for h in range(2):
+                    quantize_x(1, 0, h)
+                multiply(2, 0)
+            quantize_x(b + 1, g, 0)
+            if u == last - 3:
+                finish_planes(0, 0)
+            quantize_x(b + 1, g, 1)
+            multiply(2 * b + 2, g)
+            if g == 1:
+                for k in range(PASSES):
+                    multiply(2 * b + 3, k)
             sliver(u - 1)
-            if u >= 3:
-                finish_planes(u - 3)
-            round_on_gpsimd(u - 1, 0, CTILES)
-            turn(u - 1, 0, CTILES)
-            interleave_on_gpsimd(u + 2, 1)
+            interleave_on_vector(nb, ng, 1)
+            gpsimd_copy(rounded(u - 1)[:], ys[u - 1][:])
+            turn(u - 1)
+            interleave_on_gpsimd(nb, ng, 1)
+            interleave_on_scalar(nb, ng, 1)
+            interleave_on_scalar(nb, ng, 0)
             if u >= 2:
-                interleave_on_scalar(u + 2, 0)
-                gather_words(u - 2, 0, CTILES)
-            interleave_on_scalar(u + 2, 1)
-            if u < last - 2:
-                one_port_block(u)
-
-        for ct in range(CTILES):
-            scale(last - 2, ct, ys[last - 2][:, ct, :])
-        store_y(last - 2, 0, CTILES)
-        round_on_gpsimd(last - 2, 0, CTILES)
-        gather_words(last - 3, 0, CTILES)
-        turn(last - 2, 0, CTILES)
-        gather_words(last - 2, 0, CTILES)
-        for ct in range(CTILES):
-            residual(last - 1, ct)
-        for ct in range(CTILES):
-            scale(last - 1, ct, ys[last - 1][:, ct, :])
-        store_y(last - 1, 0, CTILES)
-        quantize_x(last, 0)
-        multiply(last, 0)
-        finish_planes(last - 4)
-        quantize_x(last, 1)
-        multiply(last, 1)
-        finish_planes(last - 3)
-        finish_planes(last - 2)
-        rounded(last - 1, 0)
-        nc.scalar.copy(out=y16[last - 1][:], in_=ys[last - 1][:])
-        turn(last - 1, 0, CTILES)
-        gather_words(last - 1, 0, CTILES)
-        for ct in range(CTILES):
-            residual(last, ct)
-        for ct in range(CTILES):
-            scale(last, ct, rounded(last, ct))
-            turn(last, ct, ct + 1)
-            gather_words(last, ct, ct + 1)
-        for ct in range(CTILES):
-            scale(last, ct, ys[last][:, ct, :])
-            store_y(last, ct, ct + 1)
-        quantize_y(last - 1, 0, CLU)
-        store_codes(last - 1, 0, CLU)
-        quantize_y(last, 0, CLU)
-        store_codes(last, 0, CLU)
+                gather_words(u - 2)
+            scale(u, ys[u], 0, DIM - SLIVER if u < last - 3 else DIM)
+            residual(u + 1)
+        store_y(4)
+        round_on_scalar(4)
+        gather_words(3)
+        quantize_x(3, 1, 0)
+        multiply(6, 1, 0, 1)
+        multiply(7, 0, 0, 1)
+        finish_planes(0, 1)
+        quantize_x(3, 1, 1)
+        multiply(6, 1, 1, 2)
+        turn(4)
+        multiply(7, 0, 1, 2)
+        multiply(7, 1)
+        scale(5, ys[5], 0, DIM)
+        store_y(5)
+        round_on_scalar(5)
+        gather_words(4)
+        turn(5)
+        residual(6)
+        finish_planes(1, 0)
+        scale(6, ys[6], 0, DIM)
+        store_y(6)
+        for h in (1, 0):
+            round_on_scalar(6, h * HALF, (h + 1) * HALF)
+            turn(6, h, h + 1)
+        gather_words(5)
+        residual(last)
+        scale(last, ys[last], 0, HALF)
+        store_y(last, 0, HALF)
+        round_on_scalar(last, 0, HALF)
+        scale(last, rounded(last), HALF, DIM)
+        finish_planes(1, 1)
+        scale(last, ys[last], HALF, DIM)
+        store_y(last, HALF, DIM)
+        finish_planes(2, 0)
+        finish_planes(2, 1)
+        for h in (1, 0):
+            gather_words(6, h, h + 1)
+            turn(last, h, h + 1)
+            gather_words(last, h, h + 1)
+        finish_planes(IMG - 1, 1)
+        finish_planes(IMG - 1, 0)
         for q in range(4):
-            store_scales(nc.scalar if q % 2 else nc.sync, q, y_planes[1], 2 * CLU, IMG * CLU)
+            store_scales(nc.scalar if q % 2 else nc.sync, q, 0)

@@ -23,8 +23,8 @@ PASSES = PTS // K_PASS
 CTILES = CLU // P
 UNITS = IMG * CTILES
 
-SHARE_HEAD, SHARE_CATCH_UP, SHARE_STEADY = 288, 304, 112
-SHARE_GPSIMD, SHARE_GPSIMD_FIRST = 88, 384
+SHARE_HEAD, SHARE_CATCH_UP, SHARE_STEADY = 256, 336, 112
+SHARE_GPSIMD, SHARE_GPSIMD_FIRST = 80, 256
 SLIVER = 64
 
 
@@ -97,12 +97,12 @@ def tile_vlad_residual_sums_k2_kernel(tc, a_words, a_scales, x, mass, centres, g
         def vector_share(b, g, h):
             if b == 0:
                 return SHARE_HEAD
-            if (b, g, h) in ((1, 1, 0), (2, 0, 1)):
+            if (b, g, h) == (1, 1, 0):
                 return SHARE_CATCH_UP
-            return SHARE_STEADY if b >= 2 and h == 1 else 0
+            return SHARE_STEADY if h == 1 and (b, g) in ((2, 0), (2, 1), (3, 0)) else 0
 
         def gpsimd_share(b, g, h):
-            if (b, g, h) == (1, 0, 1):
+            if (b, g, h) in ((1, 0, 1), (2, 0, 1)):
                 return SHARE_GPSIMD_FIRST
             return SHARE_GPSIMD if b >= 2 and h == 1 else 0
 
@@ -177,8 +177,8 @@ def tile_vlad_residual_sums_k2_kernel(tc, a_words, a_scales, x, mass, centres, g
             b, ct = divmod(u, CTILES)
             if b not in yb:
                 yb[b] = work.tile([P, 2, CLU, 2], F32, name="yb", bufs=3, align_bytes=64)
-            nc.scalar.copy(out=yb[b][:, h0:h1, ct * P:(ct + 1) * P, :],
-                           in_=turned[u, h0][:].rearrange("p h w c -> p h c w"))
+            nc.scalar.copy(out=yb[b][:, h0:h1, ct * P:(ct + 1) * P, :].rearrange("p h (c i) w -> p h c w i", i=2),
+                           in_=turned[u, h0][:].rearrange("p h w (c i) -> p h c w i", i=2))
 
         def store_y(u, d0=0, d1=DIM):
             b, ct = divmod(u, CTILES)
@@ -213,25 +213,31 @@ def tile_vlad_residual_sums_k2_kernel(tc, a_words, a_scales, x, mass, centres, g
 
         last = UNITS - 1
 
-        for g in range(PASSES):
-            for h in range(2):
-                interleave_on_vector(0, g, h)
-                interleave_on_scalar(0, g, h)
-            if g == 0:
-                spread_constants()
-            for h in range(2):
-                quantize_x(0, g, h)
+        for h in range(2):
+            interleave_on_vector(0, 0, h)
+            interleave_on_scalar(0, 0, h)
+        spread_constants()
+        quantize_x(0, 0, 0)
+        interleave_on_vector(0, 1, 0)
+        interleave_on_scalar(0, 1, 0)
+        quantize_x(0, 0, 1)
+        quantize_x(0, 1, 0)
+        interleave_on_vector(0, 1, 1)
+        interleave_on_scalar(0, 1, 1)
+        quantize_x(0, 1, 1)
         for u in range(2):
-            for g in range(PASSES):
-                multiply(u, g)
+            for h in range(2):
+                for g in range(PASSES):
+                    multiply(u, g, h, h + 1)
         interleave_on_scalar(1, 0, 0)
         interleave_on_gpsimd(1, 0, 1)
         interleave_on_scalar(1, 0, 1)
         interleave_on_scalar(1, 1, 0)
         interleave_on_scalar(1, 1, 1)
         residual(0)
-        scale(0, ys[0], 0, HALF)
-        scale(0, ys[0], HALF, DIM - SLIVER)
+        for d0, d1 in ((0, HALF), (HALF, DIM - SLIVER)):
+            scale(0, ys[0], d0, d1)
+            gpsimd_copy(rounded(0)[:, d0:d1], ys[0][:, d0:d1])
         residual(1)
 
         def round_on_scalar(u, d0=0, d1=DIM):
@@ -254,12 +260,14 @@ def tile_vlad_residual_sums_k2_kernel(tc, a_words, a_scales, x, mass, centres, g
                 for k in range(PASSES):
                     multiply(2 * b + 3, k)
             sliver(u - 1)
-            interleave_on_vector(nb, ng, 1)
-            gpsimd_copy(rounded(u - 1)[:], ys[u - 1][:])
+            if u < last - 3:
+                interleave_on_vector(nb, ng, 1)
+            d0 = DIM - SLIVER if u == 1 else 0
+            gpsimd_copy(rounded(u - 1)[:, d0:DIM], ys[u - 1][:, d0:DIM])
             turn(u - 1)
             interleave_on_gpsimd(nb, ng, 1)
-            interleave_on_scalar(nb, ng, 1)
-            interleave_on_scalar(nb, ng, 0)
+            for h in ((1, 0) if u < last - 3 else (0, 1)):
+                interleave_on_scalar(nb, ng, h)
             if u >= 2:
                 gather_words(u - 2)
             scale(u, ys[u], 0, DIM - SLIVER if u < last - 3 else DIM)

@@ -23,8 +23,8 @@ PASSES = PTS // K_PASS
 CTILES = CLU // P
 UNITS = IMG * CTILES
 
-SHARE_HEAD, SHARE_CATCH_UP, SHARE_STEADY = 256, 336, 112
-SHARE_GPSIMD, SHARE_GPSIMD_FIRST = 80, 256
+SHARE_HEAD, SHARE_CATCH_UP, SHARE_STEADY = 256, 368, 120
+SHARE_GPSIMD, SHARE_GPSIMD_FIRST = 80, 384
 SLIVER = 64
 
 
@@ -44,7 +44,8 @@ def tile_vlad_residual_sums_k2_kernel(tc, a_words, a_scales, x, mass, centres, g
         gain_all = psum.tile([P, DIM], BF16, name="gain_all", bufs=1)
         cen = [keep.tile([P, DIM], BF16, name="cen%d" % ct, align_bytes=64) for ct in range(CTILES)]
         a_codes = [keep.tile([P, PASSES, CLU], U32, name="a_codes%d" % b, align_bytes=64) for b in range(IMG)]
-        a_planes = [keep.tile([P, n * PASSES, CLU], U8, name="a_plane%d" % n, align_bytes=64) for n in (1, IMG - 1)]
+        a_planes = [keep.tile([P, n * PASSES, CLU], U8, name="a_plane%d" % n, align_bytes=64) for n in (1, 2)]
+        a_planes.insert(1, keep.tile([P, PASSES, CLU], U8, name="a_plane_second", align_bytes=64))
         y_codes = [keep.tile([P, 2, CLU], U32, name="y_codes%d" % b, align_bytes=64) for b in range(IMG)]
         y_planes = [keep.tile([P, IMG * CLU], U8, name="y_plane%d" % n, align_bytes=64) for n in range(1)]
         raw = {}
@@ -79,11 +80,15 @@ def tile_vlad_residual_sums_k2_kernel(tc, a_words, a_scales, x, mass, centres, g
         load_x(1, 0)
         nc.sync.dma_start(out=cen[1][:], in_=centres[P:2 * P, :])
         load_x(1, 1)
-        load_scales(a_planes[1], 1, IMG)
+        load_x(2, 0)
+        load_scales(a_planes[1], 1, 2)
         load_a(1)
         for b in range(2, IMG):
-            load_x(b, 0)
+            if b > 2:
+                load_x(b, 0)
             load_x(b, 1)
+            if b == 2:
+                load_scales(a_planes[2], 2, IMG)
             load_a(b)
 
         grouped = {}
@@ -102,8 +107,10 @@ def tile_vlad_residual_sums_k2_kernel(tc, a_words, a_scales, x, mass, centres, g
             return SHARE_STEADY if h == 1 and (b, g) in ((2, 0), (2, 1), (3, 0)) else 0
 
         def gpsimd_share(b, g, h):
-            if (b, g, h) in ((1, 0, 1), (2, 0, 1)):
+            if (b, g, h) == (1, 0, 1):
                 return SHARE_GPSIMD_FIRST
+            if (b, g, h) == (2, 0, 1):
+                return SHARE_GPSIMD_FIRST // 2
             return SHARE_GPSIMD if b >= 2 and h == 1 else 0
 
         def chunk_views(b, g, h, c0, c1):
@@ -136,7 +143,7 @@ def tile_vlad_residual_sums_k2_kernel(tc, a_words, a_scales, x, mass, centres, g
 
         def multiply(u, g, h0=0, h1=2):
             b, ct = divmod(u, CTILES)
-            a_scale = a_planes[0][:, g, :] if b == 0 else a_planes[1][:, PASSES * (b - 1) + g, :]
+            a_scale = a_planes[b][:, g, :] if b < 2 else a_planes[2][:, PASSES * (b - 2) + g, :]
             cl = slice(ct * P, (ct + 1) * P)
             for h in range(h0, h1):
                 codes, plane = xq[b, g, h]
@@ -225,20 +232,24 @@ def tile_vlad_residual_sums_k2_kernel(tc, a_words, a_scales, x, mass, centres, g
         interleave_on_vector(0, 1, 1)
         interleave_on_scalar(0, 1, 1)
         quantize_x(0, 1, 1)
+        for g in range(PASSES):
+            for u in range(2):
+                multiply(u, g, 0, 1)
         for u in range(2):
-            for h in range(2):
-                for g in range(PASSES):
-                    multiply(u, g, h, h + 1)
+            for g in range(PASSES):
+                multiply(u, g, 1, 2)
         interleave_on_scalar(1, 0, 0)
         interleave_on_gpsimd(1, 0, 1)
         interleave_on_scalar(1, 0, 1)
         interleave_on_scalar(1, 1, 0)
         interleave_on_scalar(1, 1, 1)
-        residual(0)
-        for d0, d1 in ((0, HALF), (HALF, DIM - SLIVER)):
-            scale(0, ys[0], d0, d1)
-            gpsimd_copy(rounded(0)[:, d0:d1], ys[0][:, d0:d1])
-        residual(1)
+        for u in range(2):
+            residual(u, 0, 1)
+        scale(0, ys[0], 0, HALF)
+        gpsimd_copy(rounded(0)[:, 0:HALF], ys[0][:, 0:HALF])
+        for u in range(2):
+            residual(u, 1, 2)
+        scale(0, ys[0], HALF, DIM - SLIVER)
 
         def round_on_scalar(u, d0=0, d1=DIM):
             nc.scalar.copy(out=rounded(u)[:, d0:d1], in_=ys[u][:, d0:d1])
@@ -250,19 +261,23 @@ def tile_vlad_residual_sums_k2_kernel(tc, a_words, a_scales, x, mass, centres, g
                 interleave_on_vector(1, 1, 0)
                 for h in range(2):
                     quantize_x(1, 0, h)
-                multiply(2, 0)
             quantize_x(b + 1, g, 0)
             if u == last - 3:
                 finish_planes(0, 0)
             quantize_x(b + 1, g, 1)
-            multiply(2 * b + 2, g)
+            if u == 1:
+                for h in range(2):
+                    for k in range(PASSES):
+                        multiply(2, k, h, h + 1)
+            else:
+                multiply(2 * b + 2, g)
             if g == 1:
                 for k in range(PASSES):
                     multiply(2 * b + 3, k)
             sliver(u - 1)
             if u < last - 3:
                 interleave_on_vector(nb, ng, 1)
-            d0 = DIM - SLIVER if u == 1 else 0
+            d0 = HALF if u == 1 else 0
             gpsimd_copy(rounded(u - 1)[:, d0:DIM], ys[u - 1][:, d0:DIM])
             turn(u - 1)
             interleave_on_gpsimd(nb, ng, 1)

@@ -23,8 +23,8 @@ PASSES = PTS // K_PASS
 CTILES = CLU // P
 UNITS = IMG * CTILES
 
-SHARE_HEAD, SHARE_CATCH_UP, SHARE_STEADY = 256, 368, 120
-SHARE_GPSIMD, SHARE_GPSIMD_FIRST = 80, 384
+SHARE_HEAD, SHARE_CATCH_UP, SHARE_STEADY = 256, 384, 120
+SHARE_GPSIMD, SHARE_GPSIMD_FIRST = 80, 352
 SLIVER = 64
 
 
@@ -264,6 +264,10 @@ def tile_vlad_residual_sums_k2_kernel(tc, a_words, a_scales, x, mass, centres, g
             quantize_x(b + 1, g, 0)
             if u == last - 3:
                 finish_planes(0, 0)
+            elif u > 1:
+                interleave_on_vector(nb, ng, 1)
+            if u > 1:
+                sliver(u - 1)
             quantize_x(b + 1, g, 1)
             if u == 1:
                 for h in range(2):
@@ -274,8 +278,8 @@ def tile_vlad_residual_sums_k2_kernel(tc, a_words, a_scales, x, mass, centres, g
             if g == 1:
                 for k in range(PASSES):
                     multiply(2 * b + 3, k)
-            sliver(u - 1)
-            if u < last - 3:
+            if u == 1:
+                sliver(0)
                 interleave_on_vector(nb, ng, 1)
             d0 = HALF if u == 1 else 0
             gpsimd_copy(rounded(u - 1)[:, d0:DIM], ys[u - 1][:, d0:DIM])

@@ -21,11 +21,15 @@ K_PASS = P * PACK
 HALF = 512
 PASSES = PTS // K_PASS
 CTILES = CLU // P
-UNITS = IMG * CTILES
 
-SHARE_HEAD, SHARE_CATCH_UP, SHARE_STEADY = 256, 384, 120
-SHARE_GPSIMD, SHARE_GPSIMD_FIRST = 80, 352
-SLIVER = 64
+HEAD_FIRST = 256
+HEAD_SECOND = 336
+HEAD_THIRD = 144
+CATCH_UP = 320
+STEADY = 32
+GPSIMD_FIRST = 64
+GPSIMD_SECOND = 160
+GPSIMD_THIRD = 384
 
 
 def tile_vlad_residual_sums_k2_kernel(tc, a_words, a_scales, x, mass, centres, gain, out_0, out_1, out_2):
@@ -33,7 +37,7 @@ def tile_vlad_residual_sums_k2_kernel(tc, a_words, a_scales, x, mass, centres, g
     with ExitStack() as ctx:
         keep = ctx.enter_context(tc.tile_pool(name="keep", bufs=1))
         work = ctx.enter_context(tc.tile_pool(name="work", bufs=4))
-        psum = ctx.enter_context(tc.psum_pool(name="psum", bufs=4))
+        psum = ctx.enter_context(tc.psum_pool(name="psum", bufs=1))
         ctx.enter_context(tc.manual_schedule())
 
         ident32 = keep.tile([P, P], F32, name="ident32", align_bytes=64)
@@ -41,13 +45,14 @@ def tile_vlad_residual_sums_k2_kernel(tc, a_words, a_scales, x, mass, centres, g
         rows = keep.tile([P, P], BF16, name="rows", align_bytes=64)
         cols = keep.tile([P, 8], BF16, name="cols", align_bytes=64)
         neg_mass = keep.tile([P, 8], F32, name="neg_mass", align_bytes=64)
-        gain_all = psum.tile([P, DIM], BF16, name="gain_all", bufs=1)
-        cen = [keep.tile([P, DIM], BF16, name="cen%d" % ct, align_bytes=64) for ct in range(CTILES)]
+        gain_all = psum.tile([P, DIM], BF16, name="gain_all")
+        cen = [keep.tile([P, CTILES, HALF], BF16, name="cen%d" % h, align_bytes=64) for h in range(2)]
         a_codes = [keep.tile([P, PASSES, CLU], U32, name="a_codes%d" % b, align_bytes=64) for b in range(IMG)]
-        a_planes = [keep.tile([P, n * PASSES, CLU], U8, name="a_plane%d" % n, align_bytes=64) for n in (1, 2)]
-        a_planes.insert(1, keep.tile([P, PASSES, CLU], U8, name="a_plane_second", align_bytes=64))
+        a_planes = [keep.tile([P, n * PASSES, CLU], U8, name="a_plane%d" % k, align_bytes=64) for k, n in enumerate((1, 1, 2))]
         y_codes = [keep.tile([P, 2, CLU], U32, name="y_codes%d" % b, align_bytes=64) for b in range(IMG)]
-        y_planes = [keep.tile([P, IMG * CLU], U8, name="y_plane%d" % n, align_bytes=64) for n in range(1)]
+        y_plane = keep.tile([P, IMG * CLU], U8, name="y_plane", align_bytes=64)
+        handed = [keep.tile([P, HALF * PACK], BF16, name="handed%d" % k, align_bytes=64) for k in range(2)]
+        ys = [keep.tile([P, CTILES, DIM], F32, name="y%d" % b, align_bytes=64) for b in range(IMG)]
         raw = {}
 
         def load_x(b, g):
@@ -57,6 +62,9 @@ def tile_vlad_residual_sums_k2_kernel(tc, a_words, a_scales, x, mass, centres, g
         def load_a(b):
             src = a_words[PASSES * b:PASSES * (b + 1)].rearrange("g p n t -> p g (n t)").bitcast(I32)
             nc.sync.dma_start(out=a_codes[b][:].bitcast(I32), in_=src)
+
+        def load_centres(h):
+            nc.sync.dma_start(out=cen[h][:], in_=centres[:, h * HALF:(h + 1) * HALF].rearrange("(k p) d -> p k d", p=P))
 
         def load_scales(plane, b0, b1):
             for q in range(4):
@@ -76,133 +84,132 @@ def tile_vlad_residual_sums_k2_kernel(tc, a_words, a_scales, x, mass, centres, g
         load_x(0, 1)
         load_scales(a_planes[0], 0, 1)
         load_a(0)
-        nc.sync.dma_start(out=cen[0][:], in_=centres[0:P, :])
+        load_centres(0)
         load_x(1, 0)
-        nc.sync.dma_start(out=cen[1][:], in_=centres[P:2 * P, :])
+        load_centres(1)
         load_x(1, 1)
-        load_x(2, 0)
         load_scales(a_planes[1], 1, 2)
         load_a(1)
         for b in range(2, IMG):
-            if b > 2:
-                load_x(b, 0)
+            load_x(b, 0)
             load_x(b, 1)
             if b == 2:
                 load_scales(a_planes[2], 2, IMG)
             load_a(b)
 
-        grouped = {}
+        grouped = {(0, 1, 1): handed[0], (1, 0, 1): handed[0], (1, 1, 1): handed[1], (2, 0, 1): handed[1], (2, 1, 1): handed[0], (3, 1, 1): handed[1]}
+        y16 = {(0, 0): handed[0], (1, 0): handed[1]}
         xq = {}
         acc = {}
-        ys = {}
         yb = {}
         turned = {}
-        y16 = {}
-
-        def vector_share(b, g, h):
-            if b == 0:
-                return SHARE_HEAD
-            if (b, g, h) == (1, 1, 0):
-                return SHARE_CATCH_UP
-            return SHARE_STEADY if h == 1 and (b, g) in ((2, 0), (2, 1), (3, 0)) else 0
-
-        def gpsimd_share(b, g, h):
-            if (b, g, h) == (1, 0, 1):
-                return SHARE_GPSIMD_FIRST
-            if (b, g, h) == (2, 0, 1):
-                return SHARE_GPSIMD_FIRST // 2
-            return SHARE_GPSIMD if b >= 2 and h == 1 else 0
 
         def chunk_views(b, g, h, c0, c1):
             if (b, g, h) not in grouped:
-                grouped[b, g, h] = work.tile([P, HALF, PACK], BF16, name="grouped", bufs=8, align_bytes=64)
-            return grouped[b, g, h][:, c0:c1, :], raw[b, g][:, :, h * HALF + c0:h * HALF + c1]
+                grouped[b, g, h] = work.tile([P, HALF * PACK], BF16, name="grouped", bufs=6, align_bytes=64)
+            dst = grouped[b, g, h][:].rearrange("p (c t) -> p c t", t=PACK)
+            return dst[:, c0:c1, :], raw[b, g][:, :, h * HALF + c0:h * HALF + c1]
 
-        def interleave_on_vector(b, g, h):
-            dst, src = chunk_views(b, g, h, 0, vector_share(b, g, h))
+        def interleave_on_vector(b, g, h, c0, c1):
+            dst, src = chunk_views(b, g, h, c0, c1)
             nc.vector.tensor_copy(out=dst.rearrange("p (c i) t -> p c t i", i=4), in_=src.rearrange("p t (c i) -> p c t i", i=4))
 
         def gpsimd_copy(out, in_):
             nc.gpsimd.tensor_scalar(out=out, in0=in_, scalar1=1.0, scalar2=0.0, op0=ALU.mult, op1=ALU.add)
 
-        def interleave_on_gpsimd(b, g, h):
-            dst, src = chunk_views(b, g, h, HALF - gpsimd_share(b, g, h), HALF)
+        def interleave_on_gpsimd(b, g, h, c0, c1):
+            dst, src = chunk_views(b, g, h, c0, c1)
             gpsimd_copy(dst, src.rearrange("p t c -> p c t"))
 
-        def interleave_on_scalar(b, g, h):
-            dst, src = chunk_views(b, g, h, vector_share(b, g, h), HALF - gpsimd_share(b, g, h))
+        def interleave_on_scalar(b, g, h, c0=0, c1=HALF):
+            dst, src = chunk_views(b, g, h, c0, c1)
             nc.scalar.copy(out=dst.rearrange("p (c i) (s t) -> p c s i t", i=8, t=2),
                            in_=src.rearrange("p (s t) (c i) -> p c s i t", i=8, t=2))
 
         def quantize_x(b, g, h):
-            codes = work.tile([P, HALF], U32, name="x_codes", bufs=8, align_bytes=64)
-            plane = work.tile([P, HALF], U8, name="x_plane", bufs=8, align_bytes=64)
-            nc.vector.quantize_mx(out=codes[:].bitcast(E4M3X4), scales=plane[:],
-                                  in_=grouped[b, g, h][:].rearrange("p c t -> p (c t)"))
+            codes = work.tile([P, HALF], U32, name="x_codes", bufs=6, align_bytes=64)
+            plane = work.tile([P, HALF], U8, name="x_plane", bufs=6, align_bytes=64)
+            nc.vector.quantize_mx(out=codes[:].bitcast(E4M3X4), scales=plane[:], in_=grouped[b, g, h][:])
             xq[b, g, h] = (codes, plane)
 
-        def multiply(u, g, h0=0, h1=2):
-            b, ct = divmod(u, CTILES)
-            a_scale = a_planes[b][:, g, :] if b < 2 else a_planes[2][:, PASSES * (b - 2) + g, :]
+        def multiply(b, h, ct, g):
             cl = slice(ct * P, (ct + 1) * P)
+            if g == 0:
+                acc[ct, h] = psum.tile([P, HALF], F32, name="acc%d%d" % (ct, h))
+            a_scale = a_planes[b][:, g, :] if b < 2 else a_planes[2][:, PASSES * (b - 2) + g, :]
+            codes, plane = xq[b, g, h]
+            nc.tensor.matmul_mx(
+                out=acc[ct, h][:],
+                lhsT=a_codes[b][:, g, cl].bitcast(E5M2X4), lhsT_scale=a_scale[:, cl],
+                rhs=codes[:].bitcast(E4M3X4), rhs_scale=plane[:],
+                start=(g == 0), stop=(g == PASSES - 1))
+
+        def multiply_by_bank(b, h):
+            for ct in range(CTILES):
+                for g in range(PASSES):
+                    multiply(b, h, ct, g)
+
+        def multiply_by_pass(b, g, h0=0, h1=2):
             for h in range(h0, h1):
-                codes, plane = xq[b, g, h]
-                if g == 0:
-                    acc[u, h] = psum.tile([P, HALF], F32, name="acc")
-                nc.tensor.matmul_mx(
-                    out=acc[u, h][:],
-                    lhsT=a_codes[b][:, g, cl].bitcast(E5M2X4), lhsT_scale=a_scale[:, cl],
-                    rhs=codes[:].bitcast(E4M3X4), rhs_scale=plane[:],
-                    start=(g == 0), stop=(g == PASSES - 1))
+                for ct in range(CTILES):
+                    multiply(b, h, ct, g)
 
-        def residual(u, h0=0, h1=2):
-            if u not in ys:
-                ys[u] = work.tile([P, DIM], F32, name="y", bufs=UNITS, align_bytes=64)
-            for h in range(h0, h1):
-                d = slice(h * HALF, (h + 1) * HALF)
-                nc.vector.scalar_tensor_tensor(
-                    out=ys[u][:, d], in0=cen[u % CTILES][:, d], scalar=neg_mass[:, u:u + 1], in1=acc[u, h][:],
-                    op0=ALU.mult, op1=ALU.add)
+        def residual(b, ct, h):
+            d = slice(h * HALF, (h + 1) * HALF)
+            u = b * CTILES + ct
+            nc.vector.scalar_tensor_tensor(
+                out=ys[b][:, ct, d], in0=cen[h][:, ct, :], scalar=neg_mass[:, u:u + 1], in1=acc[ct, h][:],
+                op0=ALU.mult, op1=ALU.add)
 
-        def scale(u, out, d0, d1):
-            nc.vector.tensor_tensor(out=out[:, d0:d1], in0=ys[u][:, d0:d1], in1=gain_all[:, d0:d1], op=ALU.mult)
+        def scale(b, ct, h, out=None):
+            d = slice(h * HALF, (h + 1) * HALF)
+            nc.vector.tensor_tensor(out=ys[b][:, ct, d] if out is None else out, in0=ys[b][:, ct, d], in1=gain_all[:, d], op=ALU.mult)
 
-        def rounded(u):
-            if u not in y16:
-                y16[u] = work.tile([P, DIM], BF16, name="y16", bufs=3, align_bytes=64)
-            return y16[u]
+        def epilogue(b, h):
+            for ct in range(CTILES):
+                residual(b, ct, h)
+            for ct in range(CTILES):
+                scale(b, ct, h)
 
-        def turn(u, h0=0, h1=2):
-            bank = psum.tile([P, h1 - h0, 2, P], F32, name="turned", bufs=3)
-            turned[u, h0] = bank
-            for h in range(h0, h1):
-                words = y16[u][:, h * HALF:(h + 1) * HALF].bitcast(F32)
+        def rounded(b, h):
+            if (b, h) not in y16:
+                y16[b, h] = work.tile([P, CTILES * HALF], BF16, name="y16", bufs=6, align_bytes=64)
+            return y16[b, h][:, 0:CTILES * HALF].rearrange("p (k d) -> p k d", k=CTILES)
+
+        def round_on_gpsimd(b, h, c0=0, c1=CTILES):
+            gpsimd_copy(rounded(b, h)[:, c0:c1, :], ys[b][:, c0:c1, h * HALF:(h + 1) * HALF])
+
+        def round_on_scalar(b, h, c0=0, c1=CTILES):
+            nc.scalar.copy(out=rounded(b, h)[:, c0:c1, :], in_=ys[b][:, c0:c1, h * HALF:(h + 1) * HALF])
+
+        def turn(b, h, c0=0, c1=CTILES, freed=None):
+            if freed is None:
+                bank = psum.tile([P, c1 - c0, 2, P], F32, name="turned", bufs=3)
+            else:
+                bank = psum.tile([P, c1 - c0, 2, P], F32, name="acc%d%d" % freed)
+            turned[b, h, c0] = bank
+            for ct in range(c0, c1):
+                words = rounded(b, h)[:, ct, :].bitcast(F32)
                 for w in range(2):
-                    nc.tensor.transpose(bank[:, h - h0, w, :], words[:, w:HALF // 2:2], ident32[:])
+                    nc.tensor.transpose(bank[:, ct - c0, w, :], words[:, w:HALF // 2:2], ident32[:])
 
-        def gather_words(u, h0=0, h1=2):
-            b, ct = divmod(u, CTILES)
-            if b not in yb:
-                yb[b] = work.tile([P, 2, CLU, 2], F32, name="yb", bufs=3, align_bytes=64)
-            nc.scalar.copy(out=yb[b][:, h0:h1, ct * P:(ct + 1) * P, :].rearrange("p h (c i) w -> p h c w i", i=2),
-                           in_=turned[u, h0][:].rearrange("p h w (c i) -> p h c w i", i=2))
+        def gather_words(b, h, c0=0, c1=CTILES):
+            if (b, h) not in yb:
+                yb[b, h] = work.tile([P, CLU, 2], F32, name="yb", bufs=8, align_bytes=64)
+            nc.scalar.copy(out=yb[b, h][:, c0 * P:c1 * P, :].rearrange("p (k c i) w -> p k c w i", k=c1 - c0, i=2),
+                           in_=turned[b, h, c0][:].rearrange("p k w (c i) -> p k c w i", i=2))
 
-        def store_y(u, d0=0, d1=DIM):
-            b, ct = divmod(u, CTILES)
-            nc.sync.dma_start(out=out_0[b, ct * P:(ct + 1) * P, d0:d1], in_=ys[u][:, d0:d1])
-
-        def store_scales(queue, q, n):
-            queue.dma_start(out=out_2[:, 4 * q:4 * q + 4, :].bitcast(I32),
-                            in_=y_planes[n][32 * q:32 * q + 8, :].bitcast(I32))
+        def store_y(b, ct, d0=0, d1=DIM):
+            nc.sync.dma_start(out=out_0[b, ct * P:(ct + 1) * P, d0:d1], in_=ys[b][:, ct, d0:d1])
 
         def finish_planes(b, h):
             nc.vector.quantize_mx(out=y_codes[b][:, h, :].bitcast(E4M3X4),
-                                  scales=y_planes[0][4 * h:, b * CLU:(b + 1) * CLU],
-                                  in_=yb[b][:, h, :, :].rearrange("p c w -> p (c w)").bitcast(BF16))
+                                  scales=y_plane[4 * h:, b * CLU:(b + 1) * CLU],
+                                  in_=yb[b, h][:].rearrange("p c w -> p (c w)").bitcast(BF16))
             if b == IMG - 1:
                 nc.sync.dma_start(out=out_1[h][:, b * CLU:(b + 1) * CLU, :].rearrange("p m t -> p (m t)").bitcast(I32),
                                   in_=y_codes[b][:, h, :].bitcast(I32))
-            elif h == 1:
+            elif (h == 1) == (b == 0):
                 nc.sync.dma_start(out=out_1[:, :, b * CLU:(b + 1) * CLU, :].rearrange("g p m t -> p g (m t)").bitcast(I32),
                                   in_=y_codes[b][:].bitcast(I32))
 
@@ -214,123 +221,116 @@ def tile_vlad_residual_sums_k2_kernel(tc, a_words, a_scales, x, mass, centres, g
             for j in range(8):
                 nc.tensor.transpose(gain_all[:, j * P:(j + 1) * P], cols[:, j:j + 1].to_broadcast([P, P]), ident16[:])
 
-        def sliver(u):
-            scale(u, ys[u], DIM - SLIVER, DIM)
-            store_y(u)
-
-        last = UNITS - 1
+        def window(b, held_in, held_out):
+            if held_in:
+                scale(b - 1, 1, 1)
+                store_y(b - 1, 1)
+            epilogue(b, 0)
+            for ct in range(CTILES):
+                residual(b, ct, 1)
+            scale(b, 0, 1)
+            store_y(b, 0)
+            if not held_out:
+                scale(b, 1, 1)
+                store_y(b, 1)
 
         for h in range(2):
-            interleave_on_vector(0, 0, h)
-            interleave_on_scalar(0, 0, h)
+            interleave_on_vector(0, 0, h, 0, HEAD_FIRST)
+            interleave_on_scalar(0, 0, h, HEAD_FIRST, HALF)
         spread_constants()
         quantize_x(0, 0, 0)
-        interleave_on_vector(0, 1, 0)
-        interleave_on_scalar(0, 1, 0)
-        quantize_x(0, 0, 1)
+        interleave_on_vector(0, 1, 0, 0, HEAD_SECOND)
+        interleave_on_scalar(0, 1, 0, HEAD_SECOND, HALF)
         quantize_x(0, 1, 0)
-        interleave_on_vector(0, 1, 1)
-        interleave_on_scalar(0, 1, 1)
+        interleave_on_vector(0, 1, 1, 0, HEAD_THIRD)
+        interleave_on_scalar(0, 1, 1, HEAD_THIRD, HALF)
+        quantize_x(0, 0, 1)
         quantize_x(0, 1, 1)
-        for g in range(PASSES):
-            for u in range(2):
-                multiply(u, g, 0, 1)
-        for u in range(2):
+        for h in range(2):
             for g in range(PASSES):
-                multiply(u, g, 1, 2)
+                multiply_by_pass(0, g, h, h + 1)
+
+        window(0, False, False)
+        interleave_on_gpsimd(1, 0, 1, 0, HALF)
+        interleave_on_gpsimd(1, 1, 0, HALF - GPSIMD_FIRST, HALF)
         interleave_on_scalar(1, 0, 0)
-        interleave_on_gpsimd(1, 0, 1)
-        interleave_on_scalar(1, 0, 1)
-        interleave_on_scalar(1, 1, 0)
-        interleave_on_scalar(1, 1, 1)
-        for u in range(2):
-            residual(u, 0, 1)
-        scale(0, ys[0], 0, HALF)
-        gpsimd_copy(rounded(0)[:, 0:HALF], ys[0][:, 0:HALF])
-        for u in range(2):
-            residual(u, 1, 2)
-        scale(0, ys[0], HALF, DIM - SLIVER)
+        interleave_on_scalar(1, 1, 0, 0, HALF - GPSIMD_FIRST)
+        interleave_on_scalar(1, 1, 1, CATCH_UP, HALF)
+        quantize_x(1, 0, 0)
+        interleave_on_vector(1, 1, 1, 0, CATCH_UP)
+        quantize_x(1, 1, 0)
+        quantize_x(1, 1, 1)
+        quantize_x(1, 0, 1)
+        for g in range(PASSES):
+            multiply_by_pass(1, g, 0, 1)
+        multiply_by_bank(1, 1)
 
-        def round_on_scalar(u, d0=0, d1=DIM):
-            nc.scalar.copy(out=rounded(u)[:, d0:d1], in_=ys[u][:, d0:d1])
+        window(1, False, True)
+        interleave_on_gpsimd(2, 0, 1, 0, HALF)
+        interleave_on_gpsimd(2, 1, 1, HALF - GPSIMD_SECOND, HALF)
+        interleave_on_scalar(2, 0, 0)
+        interleave_on_scalar(2, 1, 0)
+        interleave_on_scalar(2, 1, 1, 0, HALF - GPSIMD_SECOND)
+        for g, h in ((0, 0), (1, 0), (1, 1), (0, 1)):
+            quantize_x(2, g, h)
+        for h in range(2):
+            multiply_by_bank(2, h)
 
-        for u in range(1, last - 2):
-            b, g = divmod(u, 2)
-            nb, ng = divmod(u + 3, 2)
-            if u == 1:
-                interleave_on_vector(1, 1, 0)
-                for h in range(2):
-                    quantize_x(1, 0, h)
-            quantize_x(b + 1, g, 0)
-            if u == last - 3:
-                finish_planes(0, 0)
-            elif u > 1:
-                interleave_on_vector(nb, ng, 1)
-            if u > 1:
-                sliver(u - 1)
-            quantize_x(b + 1, g, 1)
-            if u == 1:
-                for h in range(2):
-                    for k in range(PASSES):
-                        multiply(2, k, h, h + 1)
-            else:
-                multiply(2 * b + 2, g)
-            if g == 1:
-                for k in range(PASSES):
-                    multiply(2 * b + 3, k)
-            if u == 1:
-                sliver(0)
-                interleave_on_vector(nb, ng, 1)
-            d0 = HALF if u == 1 else 0
-            gpsimd_copy(rounded(u - 1)[:, d0:DIM], ys[u - 1][:, d0:DIM])
-            turn(u - 1)
-            interleave_on_gpsimd(nb, ng, 1)
-            for h in ((1, 0) if u < last - 3 else (0, 1)):
-                interleave_on_scalar(nb, ng, h)
-            if u >= 2:
-                gather_words(u - 2)
-            scale(u, ys[u], 0, DIM - SLIVER if u < last - 3 else DIM)
-            residual(u + 1)
-        store_y(4)
-        round_on_scalar(4)
-        gather_words(3)
+        window(2, True, False)
+        for b, h in ((0, 0), (0, 1)):
+            round_on_gpsimd(b, h)
+            turn(b, h)
+        interleave_on_gpsimd(3, 0, 1, HALF - GPSIMD_THIRD, HALF)
+        interleave_on_scalar(3, 0, 0)
+        interleave_on_scalar(3, 1, 0)
+        interleave_on_scalar(3, 0, 1, 0, HALF - GPSIMD_THIRD)
+        for h in range(2):
+            gather_words(0, h)
+        interleave_on_scalar(3, 1, 1, STEADY, HALF)
+        quantize_x(3, 0, 0)
         quantize_x(3, 1, 0)
-        multiply(6, 1, 0, 1)
-        multiply(7, 0, 0, 1)
+        finish_planes(0, 0)
+        interleave_on_vector(3, 1, 1, 0, STEADY)
         finish_planes(0, 1)
         quantize_x(3, 1, 1)
-        multiply(6, 1, 1, 2)
-        turn(4)
-        multiply(7, 0, 1, 2)
-        multiply(7, 1)
-        scale(5, ys[5], 0, DIM)
-        store_y(5)
-        round_on_scalar(5)
-        gather_words(4)
-        turn(5)
-        residual(6)
-        finish_planes(1, 0)
-        scale(6, ys[6], 0, DIM)
-        store_y(6)
-        for h in (1, 0):
-            round_on_scalar(6, h * HALF, (h + 1) * HALF)
-            turn(6, h, h + 1)
-        gather_words(5)
-        residual(last)
-        scale(last, ys[last], 0, HALF)
-        store_y(last, 0, HALF)
-        round_on_scalar(last, 0, HALF)
-        scale(last, rounded(last), HALF, DIM)
+        quantize_x(3, 0, 1)
+        for h in range(2):
+            multiply_by_bank(3, h)
+
+        last = IMG - 1
+        round_on_gpsimd(1, 0)
+        round_on_scalar(1, 1)
+        round_on_scalar(2, 1)
+        turn(1, 1)
+        turn(1, 0)
+        turn(2, 1)
+        round_on_gpsimd(2, 0)
+        epilogue(last, 0)
+        for ct in range(CTILES):
+            store_y(last, ct, 0, HALF)
+        turn(2, 0, freed=(0, 0))
+        round_on_scalar(last, 0, 0, 1)
+        round_on_gpsimd(last, 0, 1, 2)
+        gather_words(1, 1)
+        gather_words(1, 0)
+        turn(last, 0, freed=(1, 0))
+        for ct in range(CTILES):
+            residual(last, ct, 1)
+        scale(last, 0, 1)
+        store_y(last, 0, HALF, DIM)
+        gather_words(2, 1)
+        round_on_scalar(last, 1, 0, 1)
+        scale(last, 1, 1, rounded(last, 1)[:, 1, :])
         finish_planes(1, 1)
-        scale(last, ys[last], HALF, DIM)
-        store_y(last, HALF, DIM)
-        finish_planes(2, 0)
-        finish_planes(2, 1)
-        for h in (1, 0):
-            gather_words(6, h, h + 1)
-            turn(last, h, h + 1)
-            gather_words(last, h, h + 1)
-        finish_planes(IMG - 1, 1)
-        finish_planes(IMG - 1, 0)
+        scale(last, 1, 1)
+        store_y(last, 1, HALF, DIM)
+        gather_words(2, 0)
+        gather_words(last, 0)
+        for ct in (1, 0):
+            turn(last, 1, ct, ct + 1)
+            gather_words(last, 1, ct, ct + 1)
+        for b, h in ((2, 1), (1, 0), (2, 0), (3, 0), (3, 1)):
+            finish_planes(b, h)
         for q in range(4):
-            store_scales(nc.scalar if q % 2 else nc.sync, q, 0)
+            queue = nc.scalar if q % 2 else nc.sync
+            queue.dma_start(out=out_2[:, 4 * q:4 * q + 4, :].bitcast(I32), in_=y_plane[32 * q:32 * q + 8, :].bitcast(I32))

@@ -26,10 +26,11 @@ HEAD_FIRST = 256
 HEAD_SECOND = 336
 HEAD_THIRD = 144
 CATCH_UP = 320
-STEADY = 32
+SECOND = 96
+STEADY = 96
 GPSIMD_FIRST = 64
-GPSIMD_SECOND = 160
-GPSIMD_THIRD = 384
+GPSIMD_SECOND = 64
+GPSIMD_THIRD = 288
 
 
 def tile_vlad_residual_sums_k2_kernel(tc, a_words, a_scales, x, mass, centres, gain, out_0, out_1, out_2):
@@ -132,9 +133,9 @@ def tile_vlad_residual_sums_k2_kernel(tc, a_words, a_scales, x, mass, centres, g
             nc.vector.quantize_mx(out=codes[:].bitcast(E4M3X4), scales=plane[:], in_=grouped[b, g, h][:])
             xq[b, g, h] = (codes, plane)
 
-        def multiply(b, h, ct, g):
+        def multiply(b, h, ct, g, first=0):
             cl = slice(ct * P, (ct + 1) * P)
-            if g == 0:
+            if g == first:
                 acc[ct, h] = psum.tile([P, HALF], F32, name="acc%d%d" % (ct, h))
             a_scale = a_planes[b][:, g, :] if b < 2 else a_planes[2][:, PASSES * (b - 2) + g, :]
             codes, plane = xq[b, g, h]
@@ -142,12 +143,12 @@ def tile_vlad_residual_sums_k2_kernel(tc, a_words, a_scales, x, mass, centres, g
                 out=acc[ct, h][:],
                 lhsT=a_codes[b][:, g, cl].bitcast(E5M2X4), lhsT_scale=a_scale[:, cl],
                 rhs=codes[:].bitcast(E4M3X4), rhs_scale=plane[:],
-                start=(g == 0), stop=(g == PASSES - 1))
+                start=(g == first), stop=(g != first))
 
         def multiply_by_bank(b, h):
             for ct in range(CTILES):
-                for g in range(PASSES):
-                    multiply(b, h, ct, g)
+                for g in (h, 1 - h):
+                    multiply(b, h, ct, g, h)
 
         def multiply_by_pass(b, g, h0=0, h1=2):
             for h in range(h0, h1):
@@ -270,8 +271,10 @@ def tile_vlad_residual_sums_k2_kernel(tc, a_words, a_scales, x, mass, centres, g
         interleave_on_gpsimd(2, 1, 1, HALF - GPSIMD_SECOND, HALF)
         interleave_on_scalar(2, 0, 0)
         interleave_on_scalar(2, 1, 0)
-        interleave_on_scalar(2, 1, 1, 0, HALF - GPSIMD_SECOND)
-        for g, h in ((0, 0), (1, 0), (1, 1), (0, 1)):
+        interleave_on_scalar(2, 1, 1, SECOND, HALF - GPSIMD_SECOND)
+        quantize_x(2, 0, 0)
+        interleave_on_vector(2, 1, 1, 0, SECOND)
+        for g, h in ((1, 0), (1, 1), (0, 1)):
             quantize_x(2, g, h)
         for h in range(2):
             multiply_by_bank(2, h)
@@ -284,9 +287,10 @@ def tile_vlad_residual_sums_k2_kernel(tc, a_words, a_scales, x, mass, centres, g
         interleave_on_scalar(3, 0, 0)
         interleave_on_scalar(3, 1, 0)
         interleave_on_scalar(3, 0, 1, 0, HALF - GPSIMD_THIRD)
+        interleave_on_scalar(3, 1, 1, STEADY, HALF // 2)
         for h in range(2):
             gather_words(0, h)
-        interleave_on_scalar(3, 1, 1, STEADY, HALF)
+        interleave_on_scalar(3, 1, 1, HALF // 2, HALF)
         quantize_x(3, 0, 0)
         quantize_x(3, 1, 0)
         finish_planes(0, 0)

@@ -29,8 +29,8 @@ CATCH_UP = 320
 SECOND = 96
 STEADY = 96
 GPSIMD_FIRST = 64
-GPSIMD_SECOND = 64
-GPSIMD_THIRD = 288
+GPSIMD_SECOND = 160
+GPSIMD_THIRD = 384
 
 
 def tile_vlad_residual_sums_k2_kernel(tc, a_words, a_scales, x, mass, centres, gain, out_0, out_1, out_2):
@@ -49,11 +49,11 @@ def tile_vlad_residual_sums_k2_kernel(tc, a_words, a_scales, x, mass, centres, g
         gain_all = psum.tile([P, DIM], BF16, name="gain_all")
         cen = [keep.tile([P, CTILES, HALF], BF16, name="cen%d" % h, align_bytes=64) for h in range(2)]
         a_codes = [keep.tile([P, PASSES, CLU], U32, name="a_codes%d" % b, align_bytes=64) for b in range(IMG)]
-        a_planes = [keep.tile([P, n * PASSES, CLU], U8, name="a_plane%d" % k, align_bytes=64) for k, n in enumerate((1, 1, 2))]
+        a_planes = [keep.tile([P, n * PASSES, CLU], U8, name="a_plane%d" % k, align_bytes=64) for k, n in enumerate((2, 2))]
         y_codes = [keep.tile([P, 2, CLU], U32, name="y_codes%d" % b, align_bytes=64) for b in range(IMG)]
         y_plane = keep.tile([P, IMG * CLU], U8, name="y_plane", align_bytes=64)
         handed = [keep.tile([P, HALF * PACK], BF16, name="handed%d" % k, align_bytes=64) for k in range(2)]
-        ys = [keep.tile([P, CTILES, DIM], F32, name="y%d" % b, align_bytes=64) for b in range(IMG)]
+        ys = [[keep.tile([P, CTILES, HALF], F32, name="y%d%d" % (b, h), align_bytes=64) for h in range(2)] for b in range(IMG)]
         raw = {}
 
         def load_x(b, g):
@@ -68,10 +68,10 @@ def tile_vlad_residual_sums_k2_kernel(tc, a_words, a_scales, x, mass, centres, g
             nc.sync.dma_start(out=cen[h][:], in_=centres[:, h * HALF:(h + 1) * HALF].rearrange("(k p) d -> p k d", p=P))
 
         def load_scales(plane, b0, b1):
-            for q in range(4):
+            for r in range(4):
                 nc.sync.dma_start(
-                    out=plane[32 * q:32 * q + 4, :, :].bitcast(I32),
-                    in_=a_scales[PASSES * b0:PASSES * b1, 4 * q:4 * q + 4, :].rearrange("g r n -> r g n").bitcast(I32))
+                    out=plane[r:P:32, :, :].bitcast(I32),
+                    in_=a_scales[PASSES * b0:PASSES * b1, r:16:4, :].rearrange("g q n -> q g n").bitcast(I32))
 
         nc.vector.memset(rows[:], 0.0)
         for plane in a_planes:
@@ -83,20 +83,20 @@ def tile_vlad_residual_sums_k2_kernel(tc, a_words, a_scales, x, mass, centres, g
         nc.sync.dma_start(out=rows[8:16, :], in_=mass.rearrange("b (h c) -> (b h) c", c=P))
         nc.scalar.copy(out=ident16[:], in_=ident32[:])
         load_x(0, 1)
-        load_scales(a_planes[0], 0, 1)
+        load_scales(a_planes[0], 0, 2)
         load_a(0)
         load_centres(0)
         load_x(1, 0)
         load_centres(1)
         load_x(1, 1)
-        load_scales(a_planes[1], 1, 2)
         load_a(1)
-        for b in range(2, IMG):
-            load_x(b, 0)
-            load_x(b, 1)
-            if b == 2:
-                load_scales(a_planes[2], 2, IMG)
-            load_a(b)
+        load_x(2, 0)
+        load_x(2, 1)
+        load_x(3, 0)
+        load_scales(a_planes[1], 2, IMG)
+        load_a(2)
+        load_x(3, 1)
+        load_a(3)
 
         grouped = {(0, 1, 1): handed[0], (1, 0, 1): handed[0], (1, 1, 1): handed[1], (2, 0, 1): handed[1], (2, 1, 1): handed[0], (3, 1, 1): handed[1]}
         y16 = {(0, 0): handed[0], (1, 0): handed[1]}
@@ -137,7 +137,7 @@ def tile_vlad_residual_sums_k2_kernel(tc, a_words, a_scales, x, mass, centres, g
             cl = slice(ct * P, (ct + 1) * P)
             if g == first:
                 acc[ct, h] = psum.tile([P, HALF], F32, name="acc%d%d" % (ct, h))
-            a_scale = a_planes[b][:, g, :] if b < 2 else a_planes[2][:, PASSES * (b - 2) + g, :]
+            a_scale = a_planes[b // 2][:, PASSES * (b % 2) + g, :]
             codes, plane = xq[b, g, h]
             nc.tensor.matmul_mx(
                 out=acc[ct, h][:],
@@ -156,15 +156,18 @@ def tile_vlad_residual_sums_k2_kernel(tc, a_words, a_scales, x, mass, centres, g
                     multiply(b, h, ct, g)
 
         def residual(b, ct, h):
-            d = slice(h * HALF, (h + 1) * HALF)
             u = b * CTILES + ct
             nc.vector.scalar_tensor_tensor(
-                out=ys[b][:, ct, d], in0=cen[h][:, ct, :], scalar=neg_mass[:, u:u + 1], in1=acc[ct, h][:],
+                out=ys[b][h][:, ct, :], in0=cen[h][:, ct, :], scalar=neg_mass[:, u:u + 1], in1=acc[ct, h][:],
                 op0=ALU.mult, op1=ALU.add)
 
-        def scale(b, ct, h, out=None):
-            d = slice(h * HALF, (h + 1) * HALF)
-            nc.vector.tensor_tensor(out=ys[b][:, ct, d] if out is None else out, in0=ys[b][:, ct, d], in1=gain_all[:, d], op=ALU.mult)
+        def scale(b, ct, h):
+            nc.vector.tensor_tensor(out=ys[b][h][:, ct, :], in0=ys[b][h][:, ct, :], in1=gain_all[:, h * HALF:(h + 1) * HALF], op=ALU.mult)
+
+        def scale_rounded(b, ct, h):
+            nc.vector.tensor_tensor(out=rounded(b, h)[:, :, ct * P:(ct + 1) * P, :],
+                                    in0=ys[b][h][:, ct, :].rearrange("p (q w e) -> p w q e", w=2, e=2),
+                                    in1=gain_all[:, h * HALF:(h + 1) * HALF].rearrange("p (q w e) -> p w q e", w=2, e=2), op=ALU.mult)
 
         def epilogue(b, h):
             for ct in range(CTILES):
@@ -175,13 +178,18 @@ def tile_vlad_residual_sums_k2_kernel(tc, a_words, a_scales, x, mass, centres, g
         def rounded(b, h):
             if (b, h) not in y16:
                 y16[b, h] = work.tile([P, CTILES * HALF], BF16, name="y16", bufs=6, align_bytes=64)
-            return y16[b, h][:, 0:CTILES * HALF].rearrange("p (k d) -> p k d", k=CTILES)
+            return y16[b, h][:, 0:CTILES * HALF].rearrange("p (w q e) -> p w q e", w=2, e=2)
+
+        def round_views(b, h, c0, c1):
+            src = ys[b][h][:, c0:c1, :].rearrange("p k (q w e) -> p w (k q) e", w=2, e=2)
+            return rounded(b, h)[:, :, c0 * P:c1 * P, :], src
 
         def round_on_gpsimd(b, h, c0=0, c1=CTILES):
-            gpsimd_copy(rounded(b, h)[:, c0:c1, :], ys[b][:, c0:c1, h * HALF:(h + 1) * HALF])
+            gpsimd_copy(*round_views(b, h, c0, c1))
 
         def round_on_scalar(b, h, c0=0, c1=CTILES):
-            nc.scalar.copy(out=rounded(b, h)[:, c0:c1, :], in_=ys[b][:, c0:c1, h * HALF:(h + 1) * HALF])
+            dst, src = round_views(b, h, c0, c1)
+            nc.scalar.copy(out=dst, in_=src)
 
         def turn(b, h, c0=0, c1=CTILES, freed=None):
             if freed is None:
@@ -190,9 +198,9 @@ def tile_vlad_residual_sums_k2_kernel(tc, a_words, a_scales, x, mass, centres, g
                 bank = psum.tile([P, c1 - c0, 2, P], F32, name="acc%d%d" % freed)
             turned[b, h, c0] = bank
             for ct in range(c0, c1):
-                words = rounded(b, h)[:, ct, :].bitcast(F32)
                 for w in range(2):
-                    nc.tensor.transpose(bank[:, ct - c0, w, :], words[:, w:HALF // 2:2], ident32[:])
+                    words = rounded(b, h)[:, w, ct * P:(ct + 1) * P, :].rearrange("p q e -> p (q e)").bitcast(F32)
+                    nc.tensor.transpose(bank[:, ct - c0, w, :], words, ident32[:])
 
         def gather_words(b, h, c0=0, c1=CTILES):
             if (b, h) not in yb:
@@ -200,8 +208,9 @@ def tile_vlad_residual_sums_k2_kernel(tc, a_words, a_scales, x, mass, centres, g
             nc.scalar.copy(out=yb[b, h][:, c0 * P:c1 * P, :].rearrange("p (k c i) w -> p k c w i", k=c1 - c0, i=2),
                            in_=turned[b, h, c0][:].rearrange("p k w (c i) -> p k c w i", i=2))
 
-        def store_y(b, ct, d0=0, d1=DIM):
-            nc.sync.dma_start(out=out_0[b, ct * P:(ct + 1) * P, d0:d1], in_=ys[b][:, ct, d0:d1])
+        def store_y(b, h, c0=0, c1=CTILES):
+            dst = out_0[b, c0 * P:c1 * P, h * HALF:(h + 1) * HALF].rearrange("(k p) d -> p k d", p=P)
+            nc.sync.dma_start(out=dst, in_=ys[b][h][:, c0:c1, :])
 
         def finish_planes(b, h):
             nc.vector.quantize_mx(out=y_codes[b][:, h, :].bitcast(E4M3X4),
@@ -227,10 +236,10 @@ def tile_vlad_residual_sums_k2_kernel(tc, a_words, a_scales, x, mass, centres, g
                 scale(b - 1, 1, 1)
                 store_y(b - 1, 1)
             epilogue(b, 0)
+            store_y(b, 0)
             for ct in range(CTILES):
                 residual(b, ct, 1)
             scale(b, 0, 1)
-            store_y(b, 0)
             if not held_out:
                 scale(b, 1, 1)
                 store_y(b, 1)
@@ -253,7 +262,8 @@ def tile_vlad_residual_sums_k2_kernel(tc, a_words, a_scales, x, mass, centres, g
 
         window(0, False, False)
         interleave_on_gpsimd(1, 0, 1, 0, HALF)
-        interleave_on_gpsimd(1, 1, 0, HALF - GPSIMD_FIRST, HALF)
+        if GPSIMD_FIRST:
+            interleave_on_gpsimd(1, 1, 0, HALF - GPSIMD_FIRST, HALF)
         interleave_on_scalar(1, 0, 0)
         interleave_on_scalar(1, 1, 0, 0, HALF - GPSIMD_FIRST)
         interleave_on_scalar(1, 1, 1, CATCH_UP, HALF)
@@ -310,8 +320,7 @@ def tile_vlad_residual_sums_k2_kernel(tc, a_words, a_scales, x, mass, centres, g
         turn(2, 1)
         round_on_gpsimd(2, 0)
         epilogue(last, 0)
-        for ct in range(CTILES):
-            store_y(last, ct, 0, HALF)
+        store_y(last, 0)
         turn(2, 0, freed=(0, 0))
         round_on_scalar(last, 0, 0, 1)
         round_on_gpsimd(last, 0, 1, 2)
@@ -321,13 +330,13 @@ def tile_vlad_residual_sums_k2_kernel(tc, a_words, a_scales, x, mass, centres, g
         for ct in range(CTILES):
             residual(last, ct, 1)
         scale(last, 0, 1)
-        store_y(last, 0, HALF, DIM)
+        store_y(last, 1, 0, 1)
         gather_words(2, 1)
         round_on_scalar(last, 1, 0, 1)
-        scale(last, 1, 1, rounded(last, 1)[:, 1, :])
+        scale_rounded(last, 1, 1)
         finish_planes(1, 1)
         scale(last, 1, 1)
-        store_y(last, 1, HALF, DIM)
+        store_y(last, 1, 1, 2)
         gather_words(2, 0)
         gather_words(last, 0)
         for ct in (1, 0):

@@ -26,11 +26,13 @@ HEAD_FIRST = 256
 HEAD_SECOND = 336
 HEAD_THIRD = 144
 CATCH_UP = 320
-SECOND = 96
-STEADY = 96
+SECOND = 0
+STEADY = 0
 GPSIMD_FIRST = 64
 GPSIMD_SECOND = 160
-GPSIMD_THIRD = 384
+GPSIMD_THIRD = 352
+HELD0, HELD1, HELD2 = 0, 1, 0
+WARM = 0
 
 
 def tile_vlad_residual_sums_k2_kernel(tc, a_words, a_scales, x, mass, centres, gain, out_0, out_1, out_2):
@@ -231,17 +233,25 @@ def tile_vlad_residual_sums_k2_kernel(tc, a_words, a_scales, x, mass, centres, g
             for j in range(8):
                 nc.tensor.transpose(gain_all[:, j * P:(j + 1) * P], cols[:, j:j + 1].to_broadcast([P, P]), ident16[:])
 
+        def warm_up(b, ct):
+            idle = psum.tile([P, HALF], F32, name="acc%d1" % ct)
+            codes, plane = xq[b, 1, 1]
+            nc.tensor.matmul_mx(
+                out=idle[:], lhsT=a_codes[0][:, 0, 0:P].bitcast(E5M2X4), lhsT_scale=a_planes[0][:, 0, 0:P],
+                rhs=codes[:].bitcast(E4M3X4), rhs_scale=plane[:], start=True, stop=True)
+
         def window(b, held_in, held_out):
+            for ct in range(CTILES - held_in, CTILES):
+                scale(b - 1, ct, 1)
             if held_in:
-                scale(b - 1, 1, 1)
                 store_y(b - 1, 1)
             epilogue(b, 0)
             store_y(b, 0)
             for ct in range(CTILES):
                 residual(b, ct, 1)
-            scale(b, 0, 1)
+            for ct in range(CTILES - held_out):
+                scale(b, ct, 1)
             if not held_out:
-                scale(b, 1, 1)
                 store_y(b, 1)
 
         for h in range(2):
@@ -260,7 +270,9 @@ def tile_vlad_residual_sums_k2_kernel(tc, a_words, a_scales, x, mass, centres, g
             for g in range(PASSES):
                 multiply_by_pass(0, g, h, h + 1)
 
-        window(0, False, False)
+        window(0, 0, HELD0)
+        for ct in range(WARM):
+            warm_up(0, ct)
         interleave_on_gpsimd(1, 0, 1, 0, HALF)
         if GPSIMD_FIRST:
             interleave_on_gpsimd(1, 1, 0, HALF - GPSIMD_FIRST, HALF)
@@ -276,23 +288,28 @@ def tile_vlad_residual_sums_k2_kernel(tc, a_words, a_scales, x, mass, centres, g
             multiply_by_pass(1, g, 0, 1)
         multiply_by_bank(1, 1)
 
-        window(1, False, True)
+        window(1, HELD0, HELD1)
+        for ct in range(WARM):
+            warm_up(1, ct)
         interleave_on_gpsimd(2, 0, 1, 0, HALF)
         interleave_on_gpsimd(2, 1, 1, HALF - GPSIMD_SECOND, HALF)
         interleave_on_scalar(2, 0, 0)
         interleave_on_scalar(2, 1, 0)
         interleave_on_scalar(2, 1, 1, SECOND, HALF - GPSIMD_SECOND)
         quantize_x(2, 0, 0)
-        interleave_on_vector(2, 1, 1, 0, SECOND)
+        if SECOND:
+            interleave_on_vector(2, 1, 1, 0, SECOND)
         for g, h in ((1, 0), (1, 1), (0, 1)):
             quantize_x(2, g, h)
         for h in range(2):
             multiply_by_bank(2, h)
 
-        window(2, True, False)
+        window(2, HELD1, HELD2)
         for b, h in ((0, 0), (0, 1)):
             round_on_gpsimd(b, h)
             turn(b, h)
+        for ct in range(WARM):
+            warm_up(2, ct)
         interleave_on_gpsimd(3, 0, 1, HALF - GPSIMD_THIRD, HALF)
         interleave_on_scalar(3, 0, 0)
         interleave_on_scalar(3, 1, 0)
@@ -304,7 +321,8 @@ def tile_vlad_residual_sums_k2_kernel(tc, a_words, a_scales, x, mass, centres, g
         quantize_x(3, 0, 0)
         quantize_x(3, 1, 0)
         finish_planes(0, 0)
-        interleave_on_vector(3, 1, 1, 0, STEADY)
+        if STEADY:
+            interleave_on_vector(3, 1, 1, 0, STEADY)
         finish_planes(0, 1)
         quantize_x(3, 1, 1)
         quantize_x(3, 0, 1)
@@ -312,6 +330,10 @@ def tile_vlad_residual_sums_k2_kernel(tc, a_words, a_scales, x, mass, centres, g
             multiply_by_bank(3, h)
 
         last = IMG - 1
+        for ct in range(CTILES - HELD2, CTILES):
+            scale(2, ct, 1)
+        if HELD2:
+            store_y(2, 1)
         round_on_gpsimd(1, 0)
         round_on_scalar(1, 1)
         round_on_scalar(2, 1)

@@ -30,9 +30,10 @@ SECOND = 0
 STEADY = 0
 GPSIMD_FIRST = 64
 GPSIMD_SECOND = 160
-GPSIMD_THIRD = 352
-HELD0, HELD1, HELD2 = 0, 1, 0
+GPSIMD_THIRD = 288
+HELD0, HELD1, HELD2 = 0, 1, 1
 WARM = 0
+DOUBLE = 0
 
 
 def tile_vlad_residual_sums_k2_kernel(tc, a_words, a_scales, x, mass, centres, gain, out_0, out_1, out_2):
@@ -221,7 +222,7 @@ def tile_vlad_residual_sums_k2_kernel(tc, a_words, a_scales, x, mass, centres, g
             if b == IMG - 1:
                 nc.sync.dma_start(out=out_1[h][:, b * CLU:(b + 1) * CLU, :].rearrange("p m t -> p (m t)").bitcast(I32),
                                   in_=y_codes[b][:, h, :].bitcast(I32))
-            elif (h == 1) == (b == 0):
+            elif (h == 1) == (b % 2 == 0):
                 nc.sync.dma_start(out=out_1[:, :, b * CLU:(b + 1) * CLU, :].rearrange("g p m t -> p g (m t)").bitcast(I32),
                                   in_=y_codes[b][:].bitcast(I32))
 
@@ -314,20 +315,21 @@ def tile_vlad_residual_sums_k2_kernel(tc, a_words, a_scales, x, mass, centres, g
         interleave_on_scalar(3, 0, 0)
         interleave_on_scalar(3, 1, 0)
         interleave_on_scalar(3, 0, 1, 0, HALF - GPSIMD_THIRD)
-        interleave_on_scalar(3, 1, 1, STEADY, HALF // 2)
+        interleave_on_scalar(3, 1, 1, STEADY, HALF)
+        round_on_scalar(1, 1)
         for h in range(2):
             gather_words(0, h)
-        interleave_on_scalar(3, 1, 1, HALF // 2, HALF)
+        round_on_scalar(2, 0)
         quantize_x(3, 0, 0)
         quantize_x(3, 1, 0)
-        finish_planes(0, 0)
         if STEADY:
             interleave_on_vector(3, 1, 1, 0, STEADY)
-        finish_planes(0, 1)
         quantize_x(3, 1, 1)
         quantize_x(3, 0, 1)
-        for h in range(2):
-            multiply_by_bank(3, h)
+        multiply_by_bank(3, 0)
+        turn(1, 1)
+        turn(2, 0)
+        multiply_by_bank(3, 1)
 
         last = IMG - 1
         for ct in range(CTILES - HELD2, CTILES):
@@ -335,36 +337,39 @@ def tile_vlad_residual_sums_k2_kernel(tc, a_words, a_scales, x, mass, centres, g
         if HELD2:
             store_y(2, 1)
         round_on_gpsimd(1, 0)
-        round_on_scalar(1, 1)
-        round_on_scalar(2, 1)
-        turn(1, 1)
+        round_on_gpsimd(2, 1)
+        gather_words(1, 1)
+        gather_words(2, 0)
         turn(1, 0)
         turn(2, 1)
-        round_on_gpsimd(2, 0)
         epilogue(last, 0)
         store_y(last, 0)
-        turn(2, 0, freed=(0, 0))
         round_on_scalar(last, 0, 0, 1)
         round_on_gpsimd(last, 0, 1, 2)
-        gather_words(1, 1)
         gather_words(1, 0)
-        turn(last, 0, freed=(1, 0))
+        gather_words(2, 1)
+        turn(last, 0)
         for ct in range(CTILES):
             residual(last, ct, 1)
-        scale(last, 0, 1)
-        store_y(last, 1, 0, 1)
-        gather_words(2, 1)
-        round_on_scalar(last, 1, 0, 1)
-        scale_rounded(last, 1, 1)
-        finish_planes(1, 1)
-        scale(last, 1, 1)
-        store_y(last, 1, 1, 2)
-        gather_words(2, 0)
+        if DOUBLE:
+            scale(last, 0, 1)
+            store_y(last, 1, 0, 1)
+            round_on_scalar(last, 1, 0, 1)
+            scale_rounded(last, 1, 1)
+            finish_planes(0, 0)
+            scale(last, 1, 1)
+            store_y(last, 1, 1, 2)
+        else:
+            for ct in range(CTILES):
+                scale(last, ct, 1)
+                store_y(last, 1, ct, ct + 1)
+                round_on_scalar(last, 1, ct, ct + 1)
+            finish_planes(0, 0)
         gather_words(last, 0)
-        for ct in (1, 0):
+        for ct in ((1, 0) if DOUBLE else (0, 1)):
             turn(last, 1, ct, ct + 1)
             gather_words(last, 1, ct, ct + 1)
-        for b, h in ((2, 1), (1, 0), (2, 0), (3, 0), (3, 1)):
+        for b, h in ((1, 1), (0, 1), (2, 0), (1, 0), (2, 1), (3, 0), (3, 1)):
             finish_planes(b, h)
         for q in range(4):
             queue = nc.scalar if q % 2 else nc.sync

@@ -50,7 +50,7 @@ def tile_vlad_residual_sums_k2_kernel(tc, a_words, a_scales, x, mass, centres, g
         cols = keep.tile([P, 8], BF16, name="cols", align_bytes=64)
         neg_mass = keep.tile([P, 8], F32, name="neg_mass", align_bytes=64)
         gain_all = psum.tile([P, DIM], BF16, name="gain_all")
-        cen = [keep.tile([P, CTILES, HALF], BF16, name="cen%d" % h, align_bytes=64) for h in range(2)]
+        cen = [keep.tile([P, DIM], BF16, name="cen%d" % ct, align_bytes=64) for ct in range(CTILES)]
         a_codes = [keep.tile([P, PASSES, CLU], U32, name="a_codes%d" % b, align_bytes=64) for b in range(IMG)]
         a_planes = [keep.tile([P, n * PASSES, CLU], U8, name="a_plane%d" % k, align_bytes=64) for k, n in enumerate((2, 2))]
         y_codes = [keep.tile([P, 2, CLU], U32, name="y_codes%d" % b, align_bytes=64) for b in range(IMG)]
@@ -67,8 +67,8 @@ def tile_vlad_residual_sums_k2_kernel(tc, a_words, a_scales, x, mass, centres, g
             src = a_words[PASSES * b:PASSES * (b + 1)].rearrange("g p n t -> p g (n t)").bitcast(I32)
             nc.sync.dma_start(out=a_codes[b][:].bitcast(I32), in_=src)
 
-        def load_centres(h):
-            nc.sync.dma_start(out=cen[h][:], in_=centres[:, h * HALF:(h + 1) * HALF].rearrange("(k p) d -> p k d", p=P))
+        def load_centres(ct):
+            nc.sync.dma_start(out=cen[ct][:], in_=centres[ct * P:(ct + 1) * P, :])
 
         def load_scales(plane, b0, b1):
             for r in range(4):
@@ -161,7 +161,7 @@ def tile_vlad_residual_sums_k2_kernel(tc, a_words, a_scales, x, mass, centres, g
         def residual(b, ct, h):
             u = b * CTILES + ct
             nc.vector.scalar_tensor_tensor(
-                out=ys[b][h][:, ct, :], in0=cen[h][:, ct, :], scalar=neg_mass[:, u:u + 1], in1=acc[ct, h][:],
+                out=ys[b][h][:, ct, :], in0=cen[ct][:, h * HALF:(h + 1) * HALF], scalar=neg_mass[:, u:u + 1], in1=acc[ct, h][:],
                 op0=ALU.mult, op1=ALU.add)
 
         def scale(b, ct, h):

@@ -33,7 +33,6 @@ GPSIMD_SECOND = 160
 GPSIMD_THIRD = 288
 HELD0, HELD1, HELD2 = 0, 1, 1
 WARM = 0
-DOUBLE = 0
 
 
 def tile_vlad_residual_sums_k2_kernel(tc, a_words, a_scales, x, mass, centres, gain, out_0, out_1, out_2):
@@ -53,7 +52,7 @@ def tile_vlad_residual_sums_k2_kernel(tc, a_words, a_scales, x, mass, centres, g
         cen = [keep.tile([P, DIM], BF16, name="cen%d" % ct, align_bytes=64) for ct in range(CTILES)]
         a_codes = [keep.tile([P, PASSES, CLU], U32, name="a_codes%d" % b, align_bytes=64) for b in range(IMG)]
         a_planes = [keep.tile([P, n * PASSES, CLU], U8, name="a_plane%d" % k, align_bytes=64) for k, n in enumerate((2, 2))]
-        y_codes = [keep.tile([P, 2, CLU], U32, name="y_codes%d" % b, align_bytes=64) for b in range(IMG)]
+        y_codes = [keep.tile([P, IMG * CLU], U32, name="y_codes%d" % h, align_bytes=64) for h in range(2)]
         y_plane = keep.tile([P, IMG * CLU], U8, name="y_plane", align_bytes=64)
         handed = [keep.tile([P, HALF * PACK], BF16, name="handed%d" % k, align_bytes=64) for k in range(2)]
         ys = [[keep.tile([P, CTILES, HALF], F32, name="y%d%d" % (b, h), align_bytes=64) for h in range(2)] for b in range(IMG)]
@@ -216,15 +215,13 @@ def tile_vlad_residual_sums_k2_kernel(tc, a_words, a_scales, x, mass, centres, g
             nc.sync.dma_start(out=dst, in_=ys[b][h][:, c0:c1, :])
 
         def finish_planes(b, h):
-            nc.vector.quantize_mx(out=y_codes[b][:, h, :].bitcast(E4M3X4),
+            nc.vector.quantize_mx(out=y_codes[h][:, b * CLU:(b + 1) * CLU].bitcast(E4M3X4),
                                   scales=y_plane[4 * h:, b * CLU:(b + 1) * CLU],
                                   in_=yb[b, h][:].rearrange("p c w -> p (c w)").bitcast(BF16))
-            if b == IMG - 1:
-                nc.sync.dma_start(out=out_1[h][:, b * CLU:(b + 1) * CLU, :].rearrange("p m t -> p (m t)").bitcast(I32),
-                                  in_=y_codes[b][:, h, :].bitcast(I32))
-            elif (h == 1) == (b % 2 == 0):
-                nc.sync.dma_start(out=out_1[:, :, b * CLU:(b + 1) * CLU, :].rearrange("g p m t -> p g (m t)").bitcast(I32),
-                                  in_=y_codes[b][:].bitcast(I32))
+
+        def store_codes(h, b0, b1):
+            dst = out_1[h][:, b0 * CLU:b1 * CLU, :].rearrange("p m t -> p (m t)").bitcast(I32)
+            nc.sync.dma_start(out=dst, in_=y_codes[h][:, b0 * CLU:b1 * CLU].bitcast(I32))
 
         def spread_constants():
             first = psum.tile([P, P], BF16, name="turned", bufs=3)
@@ -341,36 +338,31 @@ def tile_vlad_residual_sums_k2_kernel(tc, a_words, a_scales, x, mass, centres, g
         gather_words(1, 1)
         gather_words(2, 0)
         turn(1, 0)
-        turn(2, 1)
         epilogue(last, 0)
         store_y(last, 0)
         round_on_scalar(last, 0, 0, 1)
         round_on_gpsimd(last, 0, 1, 2)
         gather_words(1, 0)
-        gather_words(2, 1)
         turn(last, 0)
         for ct in range(CTILES):
             residual(last, ct, 1)
-        if DOUBLE:
-            scale(last, 0, 1)
-            store_y(last, 1, 0, 1)
-            round_on_scalar(last, 1, 0, 1)
-            scale_rounded(last, 1, 1)
-            finish_planes(0, 0)
-            scale(last, 1, 1)
-            store_y(last, 1, 1, 2)
-        else:
-            for ct in range(CTILES):
-                scale(last, ct, 1)
-                store_y(last, 1, ct, ct + 1)
-                round_on_scalar(last, 1, ct, ct + 1)
-            finish_planes(0, 0)
+        turn(2, 1)
         gather_words(last, 0)
-        for ct in ((1, 0) if DOUBLE else (0, 1)):
+        for ct in range(CTILES):
+            scale(last, ct, 1)
+            store_y(last, 1, ct, ct + 1)
+            round_on_scalar(last, 1, ct, ct + 1)
+        gather_words(2, 1)
+        for ct in range(CTILES):
             turn(last, 1, ct, ct + 1)
             gather_words(last, 1, ct, ct + 1)
-        for b, h in ((1, 1), (0, 1), (2, 0), (1, 0), (2, 1), (3, 0), (3, 1)):
-            finish_planes(b, h)
+        for b in range(IMG):
+            finish_planes(b, 0)
+        store_codes(0, 0, IMG)
+        for b in range(IMG):
+            finish_planes(b, 1)
+            if b % 2:
+                store_codes(1, b - 1, b + 1)
         for q in range(4):
             queue = nc.scalar if q % 2 else nc.sync
             queue.dma_start(out=out_2[:, 4 * q:4 * q + 4, :].bitcast(I32), in_=y_plane[32 * q:32 * q + 8, :].bitcast(I32))

@@ -24,14 +24,14 @@ CTILES = CLU // P
 
 HEAD_FIRST = 256
 HEAD_SECOND = 336
-HEAD_THIRD = 144
-CATCH_UP = 320
+HEAD_THIRD = 160
+CATCH_UP = 304
 SECOND = 0
 STEADY = 0
 GPSIMD_FIRST = 64
-GPSIMD_SECOND = 160
-GPSIMD_THIRD = 288
-HELD0, HELD1, HELD2 = 0, 1, 1
+GPSIMD_SECOND = 128
+GPSIMD_THIRD = 432
+HELD0, HELD1, HELD2 = 0, 1, 2
 WARM = 0
 
 
@@ -101,10 +101,10 @@ def tile_vlad_residual_sums_k2_kernel(tc, a_words, a_scales, x, mass, centres, g
         load_a(3)
 
         grouped = {(0, 1, 1): handed[0], (1, 0, 1): handed[0], (1, 1, 1): handed[1], (2, 0, 1): handed[1], (2, 1, 1): handed[0], (3, 1, 1): handed[1]}
-        y16 = {(0, 0): handed[0], (1, 0): handed[1]}
+        y16 = {(0, 0): handed[0], (0, 1): handed[1]}
         xq = {}
         acc = {}
-        yb = {}
+        yb = [keep.tile([P, IMG * CLU, 2], F32, name="yb%d" % h, align_bytes=64) for h in range(2)]
         turned = {}
 
         def chunk_views(b, g, h, c0, c1):
@@ -166,6 +166,16 @@ def tile_vlad_residual_sums_k2_kernel(tc, a_words, a_scales, x, mass, centres, g
         def scale(b, ct, h):
             nc.vector.tensor_tensor(out=ys[b][h][:, ct, :], in0=ys[b][h][:, ct, :], in1=gain_all[:, h * HALF:(h + 1) * HALF], op=ALU.mult)
 
+        def scale_both(b, h):
+            spread = gain_all[:, h * HALF:(h + 1) * HALF].unsqueeze(1).to_broadcast([P, CTILES, HALF])
+            nc.vector.tensor_tensor(out=ys[b][h][:], in0=ys[b][h][:], in1=spread, op=ALU.mult)
+
+        def scale_held(b, held):
+            if held == CTILES:
+                scale_both(b, 1)
+            elif held:
+                scale(b, 1, 1)
+
         def scale_rounded(b, ct, h):
             nc.vector.tensor_tensor(out=rounded(b, h)[:, :, ct * P:(ct + 1) * P, :],
                                     in0=ys[b][h][:, ct, :].rearrange("p (q w e) -> p w q e", w=2, e=2),
@@ -205,19 +215,17 @@ def tile_vlad_residual_sums_k2_kernel(tc, a_words, a_scales, x, mass, centres, g
                     nc.tensor.transpose(bank[:, ct - c0, w, :], words, ident32[:])
 
         def gather_words(b, h, c0=0, c1=CTILES):
-            if (b, h) not in yb:
-                yb[b, h] = work.tile([P, CLU, 2], F32, name="yb", bufs=8, align_bytes=64)
-            nc.scalar.copy(out=yb[b, h][:, c0 * P:c1 * P, :].rearrange("p (k c i) w -> p k c w i", k=c1 - c0, i=2),
+            nc.scalar.copy(out=yb[h][:, b * CLU + c0 * P:b * CLU + c1 * P, :].rearrange("p (k c i) w -> p k c w i", k=c1 - c0, i=2),
                            in_=turned[b, h, c0][:].rearrange("p k w (c i) -> p k c w i", i=2))
 
         def store_y(b, h, c0=0, c1=CTILES):
             dst = out_0[b, c0 * P:c1 * P, h * HALF:(h + 1) * HALF].rearrange("(k p) d -> p k d", p=P)
             nc.sync.dma_start(out=dst, in_=ys[b][h][:, c0:c1, :])
 
-        def finish_planes(b, h):
-            nc.vector.quantize_mx(out=y_codes[h][:, b * CLU:(b + 1) * CLU].bitcast(E4M3X4),
-                                  scales=y_plane[4 * h:, b * CLU:(b + 1) * CLU],
-                                  in_=yb[b, h][:].rearrange("p c w -> p (c w)").bitcast(BF16))
+        def finish_planes(h, b0, b1):
+            cl = slice(b0 * CLU, b1 * CLU)
+            nc.vector.quantize_mx(out=y_codes[h][:, cl].bitcast(E4M3X4), scales=y_plane[4 * h:, cl],
+                                  in_=yb[h][:, cl, :].rearrange("p c w -> p (c w)").bitcast(BF16))
 
         def store_codes(h, b0, b1):
             dst = out_1[h][:, b0 * CLU:b1 * CLU, :].rearrange("p m t -> p (m t)").bitcast(I32)
@@ -239,8 +247,7 @@ def tile_vlad_residual_sums_k2_kernel(tc, a_words, a_scales, x, mass, centres, g
                 rhs=codes[:].bitcast(E4M3X4), rhs_scale=plane[:], start=True, stop=True)
 
         def window(b, held_in, held_out):
-            for ct in range(CTILES - held_in, CTILES):
-                scale(b - 1, ct, 1)
+            scale_held(b - 1, held_in)
             if held_in:
                 store_y(b - 1, 1)
             epilogue(b, 0)
@@ -259,9 +266,9 @@ def tile_vlad_residual_sums_k2_kernel(tc, a_words, a_scales, x, mass, centres, g
         quantize_x(0, 0, 0)
         interleave_on_vector(0, 1, 0, 0, HEAD_SECOND)
         interleave_on_scalar(0, 1, 0, HEAD_SECOND, HALF)
-        quantize_x(0, 1, 0)
         interleave_on_vector(0, 1, 1, 0, HEAD_THIRD)
         interleave_on_scalar(0, 1, 1, HEAD_THIRD, HALF)
+        quantize_x(0, 1, 0)
         quantize_x(0, 0, 1)
         quantize_x(0, 1, 1)
         for h in range(2):
@@ -303,19 +310,18 @@ def tile_vlad_residual_sums_k2_kernel(tc, a_words, a_scales, x, mass, centres, g
             multiply_by_bank(2, h)
 
         window(2, HELD1, HELD2)
-        for b, h in ((0, 0), (0, 1)):
-            round_on_gpsimd(b, h)
-            turn(b, h)
+        round_on_gpsimd(0, 0)
+        turn(0, 0)
         for ct in range(WARM):
             warm_up(2, ct)
         interleave_on_gpsimd(3, 0, 1, HALF - GPSIMD_THIRD, HALF)
         interleave_on_scalar(3, 0, 0)
         interleave_on_scalar(3, 1, 0)
-        interleave_on_scalar(3, 0, 1, 0, HALF - GPSIMD_THIRD)
+        if GPSIMD_THIRD < HALF:
+            interleave_on_scalar(3, 0, 1, 0, HALF - GPSIMD_THIRD)
         interleave_on_scalar(3, 1, 1, STEADY, HALF)
         round_on_scalar(1, 1)
-        for h in range(2):
-            gather_words(0, h)
+        gather_words(0, 0)
         round_on_scalar(2, 0)
         quantize_x(3, 0, 0)
         quantize_x(3, 1, 0)
@@ -329,10 +335,12 @@ def tile_vlad_residual_sums_k2_kernel(tc, a_words, a_scales, x, mass, centres, g
         multiply_by_bank(3, 1)
 
         last = IMG - 1
-        for ct in range(CTILES - HELD2, CTILES):
-            scale(2, ct, 1)
+        scale_held(2, HELD2)
         if HELD2:
             store_y(2, 1)
+        round_on_gpsimd(0, 1, 1, 2)
+        round_on_scalar(0, 1, 0, 1)
+        turn(0, 1)
         round_on_gpsimd(1, 0)
         round_on_gpsimd(2, 1)
         gather_words(1, 1)
@@ -342,27 +350,26 @@ def tile_vlad_residual_sums_k2_kernel(tc, a_words, a_scales, x, mass, centres, g
         store_y(last, 0)
         round_on_scalar(last, 0, 0, 1)
         round_on_gpsimd(last, 0, 1, 2)
+        gather_words(0, 1)
+        turn(2, 1)
         gather_words(1, 0)
         turn(last, 0)
         for ct in range(CTILES):
             residual(last, ct, 1)
-        turn(2, 1)
-        gather_words(last, 0)
+        gather_words(2, 1)
         for ct in range(CTILES):
             scale(last, ct, 1)
             store_y(last, 1, ct, ct + 1)
             round_on_scalar(last, 1, ct, ct + 1)
-        gather_words(2, 1)
+        gather_words(last, 0)
         for ct in range(CTILES):
             turn(last, 1, ct, ct + 1)
             gather_words(last, 1, ct, ct + 1)
-        for b in range(IMG):
-            finish_planes(b, 0)
-        store_codes(0, 0, IMG)
-        for b in range(IMG):
-            finish_planes(b, 1)
-            if b % 2:
-                store_codes(1, b - 1, b + 1)
+        for h, b0, b1 in ((0, 0, 2), (1, 2, 3), (1, 0, 2), (0, 2, 3), (0, 3, 4), (1, 3, 4)):
+            finish_planes(h, b0, b1)
+            if (h, b0) == (0, 2):
+                continue
+            store_codes(h, 2 if (h, b0) == (0, 3) else b0, b1)
         for q in range(4):
             queue = nc.scalar if q % 2 else nc.sync
             queue.dma_start(out=out_2[:, 4 * q:4 * q + 4, :].bitcast(I32), in_=y_plane[32 * q:32 * q + 8, :].bitcast(I32))

@@ -25,14 +25,15 @@ CTILES = CLU // P
 HEAD_FIRST = 256
 HEAD_SECOND = 336
 HEAD_THIRD = 160
-CATCH_UP = 304
+CATCH_UP = 256
 SECOND = 0
 STEADY = 0
-GPSIMD_FIRST = 64
+GPSIMD_FIRST = 96
 GPSIMD_SECOND = 128
 GPSIMD_THIRD = 432
 HELD0, HELD1, HELD2 = 0, 1, 2
 WARM = 0
+SPLIT = 1
 
 
 def tile_vlad_residual_sums_k2_kernel(tc, a_words, a_scales, x, mass, centres, gain, out_0, out_1, out_2):
@@ -330,17 +331,23 @@ def tile_vlad_residual_sums_k2_kernel(tc, a_words, a_scales, x, mass, centres, g
         quantize_x(3, 1, 1)
         quantize_x(3, 0, 1)
         multiply_by_bank(3, 0)
+        for g in (1, 0):
+            multiply(3, 1, 0, g, 1)
         turn(1, 1)
         turn(2, 0)
-        multiply_by_bank(3, 1)
+        if SPLIT:
+            round_on_gpsimd(0, 1, 1, 2)
+            round_on_scalar(0, 1, 0, 1)
+        else:
+            round_on_scalar(0, 1)
+        turn(0, 1)
+        for g in (1, 0):
+            multiply(3, 1, 1, g, 1)
 
         last = IMG - 1
         scale_held(2, HELD2)
         if HELD2:
             store_y(2, 1)
-        round_on_gpsimd(0, 1, 1, 2)
-        round_on_scalar(0, 1, 0, 1)
-        turn(0, 1)
         round_on_gpsimd(1, 0)
         round_on_gpsimd(2, 1)
         gather_words(1, 1)
@@ -349,8 +356,8 @@ def tile_vlad_residual_sums_k2_kernel(tc, a_words, a_scales, x, mass, centres, g
         epilogue(last, 0)
         store_y(last, 0)
         round_on_scalar(last, 0, 0, 1)
-        round_on_gpsimd(last, 0, 1, 2)
         gather_words(0, 1)
+        round_on_gpsimd(last, 0, 1, 2)
         turn(2, 1)
         gather_words(1, 0)
         turn(last, 0)

@@ -24,16 +24,17 @@ CTILES = CLU // P
 
 HEAD_FIRST = 256
 HEAD_SECOND = 336
-HEAD_THIRD = 160
-CATCH_UP = 256
+HEAD_THIRD = 192
+CATCH_UP = 128
 SECOND = 0
 STEADY = 0
-GPSIMD_FIRST = 96
+GPSIMD_FIRST = 256
 GPSIMD_SECOND = 128
 GPSIMD_THIRD = 432
 HELD0, HELD1, HELD2 = 0, 1, 2
 WARM = 0
 SPLIT = 1
+GAP = 96
 
 
 def tile_vlad_residual_sums_k2_kernel(tc, a_words, a_scales, x, mass, centres, gain, out_0, out_1, out_2):
@@ -279,10 +280,11 @@ def tile_vlad_residual_sums_k2_kernel(tc, a_words, a_scales, x, mass, centres, g
         window(0, 0, HELD0)
         for ct in range(WARM):
             warm_up(0, ct)
-        interleave_on_gpsimd(1, 0, 1, 0, HALF)
+        interleave_on_gpsimd(1, 0, 1, GAP, HALF)
         if GPSIMD_FIRST:
             interleave_on_gpsimd(1, 1, 0, HALF - GPSIMD_FIRST, HALF)
         interleave_on_scalar(1, 0, 0)
+        interleave_on_scalar(1, 0, 1, 0, GAP)
         interleave_on_scalar(1, 1, 0, 0, HALF - GPSIMD_FIRST)
         interleave_on_scalar(1, 1, 1, CATCH_UP, HALF)
         quantize_x(1, 0, 0)

@@ -30,9 +30,9 @@ SECOND = 0
 STEADY = 0
 GPSIMD_FIRST = 256
 GPSIMD_SECOND = 128
-GPSIMD_THIRD = 432
+GPSIMD_THIRD = 400
 HELD0, HELD1, HELD2 = 0, 1, 2
-WARM = 0
+WARM = 2
 SPLIT = 1
 GAP = 96
 
@@ -337,14 +337,11 @@ def tile_vlad_residual_sums_k2_kernel(tc, a_words, a_scales, x, mass, centres, g
             multiply(3, 1, 0, g, 1)
         turn(1, 1)
         turn(2, 0)
-        if SPLIT:
-            round_on_gpsimd(0, 1, 1, 2)
-            round_on_scalar(0, 1, 0, 1)
-        else:
-            round_on_scalar(0, 1)
-        turn(0, 1)
+        round_on_gpsimd(0, 1, 1, 2)
+        round_on_scalar(0, 1, 0, 1)
         for g in (1, 0):
             multiply(3, 1, 1, g, 1)
+        turn(0, 1)
 
         last = IMG - 1
         scale_held(2, HELD2)

@@ -21,20 +21,14 @@ K_PASS = P * PACK
 HALF = 512
 PASSES = PTS // K_PASS
 CTILES = CLU // P
+ROWS = DIM // P
 
-HEAD_FIRST = 256
-HEAD_SECOND = 336
-HEAD_THIRD = 192
-CATCH_UP = 128
-SECOND = 0
-STEADY = 0
-GPSIMD_FIRST = 256
-GPSIMD_SECOND = 128
-GPSIMD_THIRD = 400
-HELD0, HELD1, HELD2 = 0, 1, 2
-WARM = 2
-SPLIT = 1
-GAP = 96
+VECTOR_URGENT = 336
+VECTOR_HEAD_LAST = 192
+VECTOR_CATCH_UP = 128
+SCALAR_WAITING = 96
+GPSIMD_BEHIND_CHUNK = 128
+GPSIMD_BEHIND_ROUNDING = 400
 
 
 def tile_vlad_residual_sums_k2_kernel(tc, a_words, a_scales, x, mass, centres, gain, out_0, out_1, out_2):
@@ -48,12 +42,12 @@ def tile_vlad_residual_sums_k2_kernel(tc, a_words, a_scales, x, mass, centres, g
         ident32 = keep.tile([P, P], F32, name="ident32", align_bytes=64)
         ident16 = keep.tile([P, P], BF16, name="ident16", align_bytes=64)
         rows = keep.tile([P, P], BF16, name="rows", align_bytes=64)
-        cols = keep.tile([P, 8], BF16, name="cols", align_bytes=64)
-        neg_mass = keep.tile([P, 8], F32, name="neg_mass", align_bytes=64)
+        cols = keep.tile([P, ROWS], BF16, name="cols", align_bytes=64)
+        neg_mass = keep.tile([P, ROWS], F32, name="neg_mass", align_bytes=64)
         gain_all = psum.tile([P, DIM], BF16, name="gain_all")
         cen = [keep.tile([P, DIM], BF16, name="cen%d" % ct, align_bytes=64) for ct in range(CTILES)]
         a_codes = [keep.tile([P, PASSES, CLU], U32, name="a_codes%d" % b, align_bytes=64) for b in range(IMG)]
-        a_planes = [keep.tile([P, n * PASSES, CLU], U8, name="a_plane%d" % k, align_bytes=64) for k, n in enumerate((2, 2))]
+        a_planes = [keep.tile([P, 2 * PASSES, CLU], U8, name="a_plane%d" % k, align_bytes=64) for k in range(IMG // 2)]
         y_codes = [keep.tile([P, IMG * CLU], U32, name="y_codes%d" % h, align_bytes=64) for h in range(2)]
         y_plane = keep.tile([P, IMG * CLU], U8, name="y_plane", align_bytes=64)
         handed = [keep.tile([P, HALF * PACK], BF16, name="handed%d" % k, align_bytes=64) for k in range(2)]
@@ -71,11 +65,11 @@ def tile_vlad_residual_sums_k2_kernel(tc, a_words, a_scales, x, mass, centres, g
         def load_centres(ct):
             nc.sync.dma_start(out=cen[ct][:], in_=centres[ct * P:(ct + 1) * P, :])
 
-        def load_scales(plane, b0, b1):
+        def load_scales(pair):
+            groups = slice(2 * PASSES * pair, 2 * PASSES * (pair + 1))
             for r in range(4):
-                nc.sync.dma_start(
-                    out=plane[r:P:32, :, :].bitcast(I32),
-                    in_=a_scales[PASSES * b0:PASSES * b1, r:16:4, :].rearrange("g q n -> q g n").bitcast(I32))
+                nc.sync.dma_start(out=a_planes[pair][r:P:32, :, :].bitcast(I32),
+                                  in_=a_scales[groups, r:16:4, :].rearrange("g q n -> q g n").bitcast(I32))
 
         nc.vector.memset(rows[:], 0.0)
         for plane in a_planes:
@@ -83,27 +77,27 @@ def tile_vlad_residual_sums_k2_kernel(tc, a_words, a_scales, x, mass, centres, g
         make_identity(nc, ident32[:])
 
         load_x(0, 0)
-        nc.sync.dma_start(out=rows[0:8, :], in_=gain.rearrange("(r c) -> r c", c=P))
-        nc.sync.dma_start(out=rows[8:16, :], in_=mass.rearrange("b (h c) -> (b h) c", c=P))
+        nc.sync.dma_start(out=rows[0:ROWS, :], in_=gain.rearrange("(r c) -> r c", c=P))
+        nc.sync.dma_start(out=rows[ROWS:2 * ROWS, :], in_=mass.rearrange("b (h c) -> (b h) c", c=P))
         nc.scalar.copy(out=ident16[:], in_=ident32[:])
         load_x(0, 1)
-        load_scales(a_planes[0], 0, 2)
+        load_scales(0)
         load_a(0)
-        load_centres(0)
-        load_x(1, 0)
-        load_centres(1)
-        load_x(1, 1)
+        for g in range(PASSES):
+            load_centres(g)
+            load_x(1, g)
         load_a(1)
         load_x(2, 0)
         load_x(2, 1)
         load_x(3, 0)
-        load_scales(a_planes[1], 2, IMG)
+        load_scales(1)
         load_a(2)
         load_x(3, 1)
         load_a(3)
 
-        grouped = {(0, 1, 1): handed[0], (1, 0, 1): handed[0], (1, 1, 1): handed[1], (2, 0, 1): handed[1], (2, 1, 1): handed[0], (3, 1, 1): handed[1]}
-        y16 = {(0, 0): handed[0], (0, 1): handed[1]}
+        grouped = {(b, 1, 1): handed[b % 2] for b in range(IMG)}
+        grouped[1, 0, 1], grouped[2, 0, 1] = handed
+        y16 = {(0, h): handed[h] for h in range(2)}
         xq = {}
         acc = {}
         yb = [keep.tile([P, IMG * CLU, 2], F32, name="yb%d" % h, align_bytes=64) for h in range(2)]
@@ -137,7 +131,7 @@ def tile_vlad_residual_sums_k2_kernel(tc, a_words, a_scales, x, mass, centres, g
             nc.vector.quantize_mx(out=codes[:].bitcast(E4M3X4), scales=plane[:], in_=grouped[b, g, h][:])
             xq[b, g, h] = (codes, plane)
 
-        def multiply(b, h, ct, g, first=0):
+        def multiply(b, h, ct, g, first):
             cl = slice(ct * P, (ct + 1) * P)
             if g == first:
                 acc[ct, h] = psum.tile([P, HALF], F32, name="acc%d%d" % (ct, h))
@@ -149,45 +143,46 @@ def tile_vlad_residual_sums_k2_kernel(tc, a_words, a_scales, x, mass, centres, g
                 rhs=codes[:].bitcast(E4M3X4), rhs_scale=plane[:],
                 start=(g == first), stop=(g != first))
 
-        def multiply_by_bank(b, h):
-            for ct in range(CTILES):
-                for g in (h, 1 - h):
-                    multiply(b, h, ct, g, h)
+        def fill_bank(b, h, ct):
+            for g in (h, 1 - h):
+                multiply(b, h, ct, g, h)
 
-        def multiply_by_pass(b, g, h0=0, h1=2):
-            for h in range(h0, h1):
+        def fill_by_pass(b, h):
+            for g in range(PASSES):
                 for ct in range(CTILES):
-                    multiply(b, h, ct, g)
+                    multiply(b, h, ct, g, 0)
 
-        def residual(b, ct, h):
-            u = b * CTILES + ct
-            nc.vector.scalar_tensor_tensor(
-                out=ys[b][h][:, ct, :], in0=cen[ct][:, h * HALF:(h + 1) * HALF], scalar=neg_mass[:, u:u + 1], in1=acc[ct, h][:],
-                op0=ALU.mult, op1=ALU.add)
+        def warm_up(b):
+            for ct in range(CTILES):
+                idle = psum.tile([P, HALF], F32, name="acc%d1" % ct)
+                codes, plane = xq[b, 1, 1]
+                nc.tensor.matmul_mx(
+                    out=idle[:], lhsT=a_codes[0][:, 0, 0:P].bitcast(E5M2X4), lhsT_scale=a_planes[0][:, 0, 0:P],
+                    rhs=codes[:].bitcast(E4M3X4), rhs_scale=plane[:], start=True, stop=True)
 
-        def scale(b, ct, h):
+        def residual(b, h, c0=0, c1=CTILES):
+            for ct in range(c0, c1):
+                u = b * CTILES + ct
+                nc.vector.scalar_tensor_tensor(
+                    out=ys[b][h][:, ct, :], in0=cen[ct][:, h * HALF:(h + 1) * HALF], scalar=neg_mass[:, u:u + 1],
+                    in1=acc[ct, h][:], op0=ALU.mult, op1=ALU.add)
+
+        def scale(b, h, ct):
             nc.vector.tensor_tensor(out=ys[b][h][:, ct, :], in0=ys[b][h][:, ct, :], in1=gain_all[:, h * HALF:(h + 1) * HALF], op=ALU.mult)
 
-        def scale_both(b, h):
+        def scale_part(b, h):
             spread = gain_all[:, h * HALF:(h + 1) * HALF].unsqueeze(1).to_broadcast([P, CTILES, HALF])
             nc.vector.tensor_tensor(out=ys[b][h][:], in0=ys[b][h][:], in1=spread, op=ALU.mult)
 
-        def scale_held(b, held):
-            if held == CTILES:
-                scale_both(b, 1)
-            elif held:
-                scale(b, 1, 1)
+        def store_y(b, h, c0=0, c1=CTILES):
+            dst = out_0[b, c0 * P:c1 * P, h * HALF:(h + 1) * HALF].rearrange("(k p) d -> p k d", p=P)
+            nc.sync.dma_start(out=dst, in_=ys[b][h][:, c0:c1, :])
 
-        def scale_rounded(b, ct, h):
-            nc.vector.tensor_tensor(out=rounded(b, h)[:, :, ct * P:(ct + 1) * P, :],
-                                    in0=ys[b][h][:, ct, :].rearrange("p (q w e) -> p w q e", w=2, e=2),
-                                    in1=gain_all[:, h * HALF:(h + 1) * HALF].rearrange("p (q w e) -> p w q e", w=2, e=2), op=ALU.mult)
-
-        def epilogue(b, h):
+        def open_window(b):
+            residual(b, 0)
             for ct in range(CTILES):
-                residual(b, ct, h)
-            for ct in range(CTILES):
-                scale(b, ct, h)
+                scale(b, 0, ct)
+            store_y(b, 0)
 
         def rounded(b, h):
             if (b, h) not in y16:
@@ -205,11 +200,8 @@ def tile_vlad_residual_sums_k2_kernel(tc, a_words, a_scales, x, mass, centres, g
             dst, src = round_views(b, h, c0, c1)
             nc.scalar.copy(out=dst, in_=src)
 
-        def turn(b, h, c0=0, c1=CTILES, freed=None):
-            if freed is None:
-                bank = psum.tile([P, c1 - c0, 2, P], F32, name="turned", bufs=3)
-            else:
-                bank = psum.tile([P, c1 - c0, 2, P], F32, name="acc%d%d" % freed)
+        def turn(b, h, c0=0, c1=CTILES):
+            bank = psum.tile([P, c1 - c0, 2, P], F32, name="turned", bufs=3)
             turned[b, h, c0] = bank
             for ct in range(c0, c1):
                 for w in range(2):
@@ -217,14 +209,11 @@ def tile_vlad_residual_sums_k2_kernel(tc, a_words, a_scales, x, mass, centres, g
                     nc.tensor.transpose(bank[:, ct - c0, w, :], words, ident32[:])
 
         def gather_words(b, h, c0=0, c1=CTILES):
-            nc.scalar.copy(out=yb[h][:, b * CLU + c0 * P:b * CLU + c1 * P, :].rearrange("p (k c i) w -> p k c w i", k=c1 - c0, i=2),
+            dst = yb[h][:, b * CLU + c0 * P:b * CLU + c1 * P, :]
+            nc.scalar.copy(out=dst.rearrange("p (k c i) w -> p k c w i", k=c1 - c0, i=2),
                            in_=turned[b, h, c0][:].rearrange("p k w (c i) -> p k c w i", i=2))
 
-        def store_y(b, h, c0=0, c1=CTILES):
-            dst = out_0[b, c0 * P:c1 * P, h * HALF:(h + 1) * HALF].rearrange("(k p) d -> p k d", p=P)
-            nc.sync.dma_start(out=dst, in_=ys[b][h][:, c0:c1, :])
-
-        def finish_planes(h, b0, b1):
+        def quantize_y(h, b0, b1):
             cl = slice(b0 * CLU, b1 * CLU)
             nc.vector.quantize_mx(out=y_codes[h][:, cl].bitcast(E4M3X4), scales=y_plane[4 * h:, cl],
                                   in_=yb[h][:, cl, :].rearrange("p c w -> p (c w)").bitcast(BF16))
@@ -236,146 +225,126 @@ def tile_vlad_residual_sums_k2_kernel(tc, a_words, a_scales, x, mass, centres, g
         def spread_constants():
             first = psum.tile([P, P], BF16, name="turned", bufs=3)
             nc.tensor.transpose(first[:], rows[:], ident16[:])
-            nc.vector.tensor_copy(out=cols[:], in_=first[:, 0:8])
-            nc.vector.tensor_scalar(out=neg_mass[:], in0=first[:, 8:16], scalar1=-1.0, scalar2=None, op0=ALU.mult)
-            for j in range(8):
+            nc.vector.tensor_copy(out=cols[:], in_=first[:, 0:ROWS])
+            nc.vector.tensor_scalar(out=neg_mass[:], in0=first[:, ROWS:2 * ROWS], scalar1=-1.0, scalar2=None, op0=ALU.mult)
+            for j in range(ROWS):
                 nc.tensor.transpose(gain_all[:, j * P:(j + 1) * P], cols[:, j:j + 1].to_broadcast([P, P]), ident16[:])
 
-        def warm_up(b, ct):
-            idle = psum.tile([P, HALF], F32, name="acc%d1" % ct)
-            codes, plane = xq[b, 1, 1]
-            nc.tensor.matmul_mx(
-                out=idle[:], lhsT=a_codes[0][:, 0, 0:P].bitcast(E5M2X4), lhsT_scale=a_planes[0][:, 0, 0:P],
-                rhs=codes[:].bitcast(E4M3X4), rhs_scale=plane[:], start=True, stop=True)
-
-        def window(b, held_in, held_out):
-            scale_held(b - 1, held_in)
-            if held_in:
-                store_y(b - 1, 1)
-            epilogue(b, 0)
-            store_y(b, 0)
-            for ct in range(CTILES):
-                residual(b, ct, 1)
-            for ct in range(CTILES - held_out):
-                scale(b, ct, 1)
-            if not held_out:
-                store_y(b, 1)
-
         for h in range(2):
-            interleave_on_vector(0, 0, h, 0, HEAD_FIRST)
-            interleave_on_scalar(0, 0, h, HEAD_FIRST, HALF)
+            interleave_on_vector(0, 0, h, 0, HALF // 2)
+            interleave_on_scalar(0, 0, h, HALF // 2, HALF)
         spread_constants()
         quantize_x(0, 0, 0)
-        interleave_on_vector(0, 1, 0, 0, HEAD_SECOND)
-        interleave_on_scalar(0, 1, 0, HEAD_SECOND, HALF)
-        interleave_on_vector(0, 1, 1, 0, HEAD_THIRD)
-        interleave_on_scalar(0, 1, 1, HEAD_THIRD, HALF)
-        quantize_x(0, 1, 0)
-        quantize_x(0, 0, 1)
-        quantize_x(0, 1, 1)
+        for h, share in enumerate((VECTOR_URGENT, VECTOR_HEAD_LAST)):
+            interleave_on_vector(0, 1, h, 0, share)
+            interleave_on_scalar(0, 1, h, share, HALF)
+        for g, h in ((1, 0), (0, 1), (1, 1)):
+            quantize_x(0, g, h)
         for h in range(2):
-            for g in range(PASSES):
-                multiply_by_pass(0, g, h, h + 1)
+            fill_by_pass(0, h)
 
-        window(0, 0, HELD0)
-        for ct in range(WARM):
-            warm_up(0, ct)
-        interleave_on_gpsimd(1, 0, 1, GAP, HALF)
-        if GPSIMD_FIRST:
-            interleave_on_gpsimd(1, 1, 0, HALF - GPSIMD_FIRST, HALF)
+        def close_block(b):
+            for g, h in ((1, 0), (1, 1), (0, 1)):
+                quantize_x(b, g, h)
+
+        residual(0, 0, 0, 1)
+        scale(0, 0, 0)
+        residual(0, 0, 1, 2)
+        residual(0, 1, 0, 1)
+        scale(0, 0, 1)
+        store_y(0, 0)
+        residual(0, 1, 1, 2)
+        for ct in range(CTILES):
+            scale(0, 1, ct)
+        store_y(0, 1)
+        warm_up(0)
+        interleave_on_gpsimd(1, 0, 1, SCALAR_WAITING, HALF)
+        interleave_on_gpsimd(1, 1, 0, HALF // 2, HALF)
         interleave_on_scalar(1, 0, 0)
-        interleave_on_scalar(1, 0, 1, 0, GAP)
-        interleave_on_scalar(1, 1, 0, 0, HALF - GPSIMD_FIRST)
-        interleave_on_scalar(1, 1, 1, CATCH_UP, HALF)
+        interleave_on_scalar(1, 0, 1, 0, SCALAR_WAITING)
+        interleave_on_scalar(1, 1, 0, 0, HALF // 2)
+        interleave_on_scalar(1, 1, 1, VECTOR_CATCH_UP, HALF)
         quantize_x(1, 0, 0)
-        interleave_on_vector(1, 1, 1, 0, CATCH_UP)
-        quantize_x(1, 1, 0)
-        quantize_x(1, 1, 1)
-        quantize_x(1, 0, 1)
-        for g in range(PASSES):
-            multiply_by_pass(1, g, 0, 1)
-        multiply_by_bank(1, 1)
+        interleave_on_vector(1, 1, 1, 0, VECTOR_CATCH_UP)
+        close_block(1)
+        fill_by_pass(1, 0)
+        for ct in range(CTILES):
+            fill_bank(1, 1, ct)
 
-        window(1, HELD0, HELD1)
-        for ct in range(WARM):
-            warm_up(1, ct)
+        open_window(1)
+        residual(1, 1)
+        scale(1, 1, 0)
+        warm_up(1)
         interleave_on_gpsimd(2, 0, 1, 0, HALF)
-        interleave_on_gpsimd(2, 1, 1, HALF - GPSIMD_SECOND, HALF)
+        interleave_on_gpsimd(2, 1, 1, HALF - GPSIMD_BEHIND_CHUNK, HALF)
         interleave_on_scalar(2, 0, 0)
         interleave_on_scalar(2, 1, 0)
-        interleave_on_scalar(2, 1, 1, SECOND, HALF - GPSIMD_SECOND)
+        interleave_on_scalar(2, 1, 1, 0, HALF - GPSIMD_BEHIND_CHUNK)
         quantize_x(2, 0, 0)
-        if SECOND:
-            interleave_on_vector(2, 1, 1, 0, SECOND)
-        for g, h in ((1, 0), (1, 1), (0, 1)):
-            quantize_x(2, g, h)
+        close_block(2)
         for h in range(2):
-            multiply_by_bank(2, h)
+            for ct in range(CTILES):
+                fill_bank(2, h, ct)
 
-        window(2, HELD1, HELD2)
+        scale(1, 1, 1)
+        store_y(1, 1)
+        open_window(2)
+        residual(2, 1)
         round_on_gpsimd(0, 0)
         turn(0, 0)
-        for ct in range(WARM):
-            warm_up(2, ct)
-        interleave_on_gpsimd(3, 0, 1, HALF - GPSIMD_THIRD, HALF)
+        warm_up(2)
+        interleave_on_gpsimd(3, 0, 1, HALF - GPSIMD_BEHIND_ROUNDING, HALF)
         interleave_on_scalar(3, 0, 0)
         interleave_on_scalar(3, 1, 0)
-        if GPSIMD_THIRD < HALF:
-            interleave_on_scalar(3, 0, 1, 0, HALF - GPSIMD_THIRD)
-        interleave_on_scalar(3, 1, 1, STEADY, HALF)
+        interleave_on_scalar(3, 0, 1, 0, HALF - GPSIMD_BEHIND_ROUNDING)
+        interleave_on_scalar(3, 1, 1)
         round_on_scalar(1, 1)
         gather_words(0, 0)
         round_on_scalar(2, 0)
         quantize_x(3, 0, 0)
-        quantize_x(3, 1, 0)
-        if STEADY:
-            interleave_on_vector(3, 1, 1, 0, STEADY)
-        quantize_x(3, 1, 1)
-        quantize_x(3, 0, 1)
-        multiply_by_bank(3, 0)
-        for g in (1, 0):
-            multiply(3, 1, 0, g, 1)
+        close_block(3)
+        for h, ct in ((0, 0), (0, 1), (1, 0)):
+            fill_bank(3, h, ct)
         turn(1, 1)
         turn(2, 0)
         round_on_gpsimd(0, 1, 1, 2)
         round_on_scalar(0, 1, 0, 1)
-        for g in (1, 0):
-            multiply(3, 1, 1, g, 1)
+        fill_bank(3, 1, 1)
         turn(0, 1)
 
-        last = IMG - 1
-        scale_held(2, HELD2)
-        if HELD2:
-            store_y(2, 1)
+        scale_part(2, 1)
+        store_y(2, 1)
         round_on_gpsimd(1, 0)
         round_on_gpsimd(2, 1)
         gather_words(1, 1)
         gather_words(2, 0)
         turn(1, 0)
-        epilogue(last, 0)
-        store_y(last, 0)
-        round_on_scalar(last, 0, 0, 1)
+        open_window(3)
+        round_on_scalar(3, 0, 0, 1)
         gather_words(0, 1)
-        round_on_gpsimd(last, 0, 1, 2)
+        round_on_gpsimd(3, 0, 1, 2)
         turn(2, 1)
         gather_words(1, 0)
-        turn(last, 0)
-        for ct in range(CTILES):
-            residual(last, ct, 1)
+        turn(3, 0)
+        residual(3, 1)
         gather_words(2, 1)
         for ct in range(CTILES):
-            scale(last, ct, 1)
-            store_y(last, 1, ct, ct + 1)
-            round_on_scalar(last, 1, ct, ct + 1)
-        gather_words(last, 0)
+            scale(3, 1, ct)
+            store_y(3, 1, ct, ct + 1)
+            round_on_scalar(3, 1, ct, ct + 1)
+        gather_words(3, 0)
         for ct in range(CTILES):
-            turn(last, 1, ct, ct + 1)
-            gather_words(last, 1, ct, ct + 1)
-        for h, b0, b1 in ((0, 0, 2), (1, 2, 3), (1, 0, 2), (0, 2, 3), (0, 3, 4), (1, 3, 4)):
-            finish_planes(h, b0, b1)
-            if (h, b0) == (0, 2):
-                continue
-            store_codes(h, 2 if (h, b0) == (0, 3) else b0, b1)
+            turn(3, 1, ct, ct + 1)
+            gather_words(3, 1, ct, ct + 1)
+
+        for h, b0, b1 in ((0, 0, 2), (1, 2, 3), (1, 0, 2)):
+            quantize_y(h, b0, b1)
+            store_codes(h, b0, b1)
+        quantize_y(0, 2, 3)
+        quantize_y(0, 3, 4)
+        store_codes(0, 2, 4)
+        quantize_y(1, 3, 4)
+        store_codes(1, 3, 4)
         for q in range(4):
             queue = nc.scalar if q % 2 else nc.sync
             queue.dma_start(out=out_2[:, 4 * q:4 * q + 4, :].bitcast(I32), in_=y_plane[32 * q:32 * q + 8, :].bitcast(I32))

@@ -240,8 +240,14 @@ def tile_vlad_residual_sums_k2_kernel(tc, a_words, a_scales, x, mass, centres, g
             interleave_on_scalar(0, 1, h, share, HALF)
         for g, h in ((1, 0), (0, 1), (1, 1)):
             quantize_x(0, g, h)
-        for h in range(2):
-            fill_by_pass(0, h)
+        for ct in range(CTILES):
+            multiply(0, 0, ct, 0, 0)
+        multiply(0, 0, 0, 1, 0)
+        for g in range(PASSES):
+            multiply(0, 1, 0, g, 0)
+        multiply(0, 0, 1, 1, 0)
+        for g in range(PASSES):
+            multiply(0, 1, 1, g, 0)
 
         def close_block(b):
             for g, h in ((1, 0), (1, 1), (0, 1)):
@@ -249,13 +255,13 @@ def tile_vlad_residual_sums_k2_kernel(tc, a_words, a_scales, x, mass, centres, g
 
         residual(0, 0, 0, 1)
         scale(0, 0, 0)
-        residual(0, 0, 1, 2)
         residual(0, 1, 0, 1)
+        residual(0, 0, 1, 2)
+        scale(0, 1, 0)
+        residual(0, 1, 1, 2)
         scale(0, 0, 1)
         store_y(0, 0)
-        residual(0, 1, 1, 2)
-        for ct in range(CTILES):
-            scale(0, 1, ct)
+        scale(0, 1, 1)
         store_y(0, 1)
         warm_up(0)
         interleave_on_gpsimd(1, 0, 1, SCALAR_WAITING, HALF)

@@ -22,13 +22,13 @@ HALF = 512
 PASSES = PTS // K_PASS
 CTILES = CLU // P
 ROWS = DIM // P
+CHUNK = HALF * PACK
 
 VECTOR_URGENT = 336
 VECTOR_HEAD_LAST = 192
-VECTOR_CATCH_UP = 128
-SCALAR_WAITING = 96
-GPSIMD_BEHIND_CHUNK = 128
-GPSIMD_BEHIND_ROUNDING = 400
+GPSIMD_FIRST = 160
+GPSIMD_SECOND = 240
+VECTOR_CATCH_UP = 352
 
 
 def tile_vlad_residual_sums_k2_kernel(tc, a_words, a_scales, x, mass, centres, gain, out_0, out_1, out_2):
@@ -45,13 +45,14 @@ def tile_vlad_residual_sums_k2_kernel(tc, a_words, a_scales, x, mass, centres, g
         cols = keep.tile([P, ROWS], BF16, name="cols", align_bytes=64)
         neg_mass = keep.tile([P, ROWS], F32, name="neg_mass", align_bytes=64)
         gain_all = psum.tile([P, DIM], BF16, name="gain_all")
-        cen = [keep.tile([P, DIM], BF16, name="cen%d" % ct, align_bytes=64) for ct in range(CTILES)]
+        cen = [keep.tile([P, CTILES, HALF], BF16, name="cen%d" % h, align_bytes=64) for h in range(2)]
         a_codes = [keep.tile([P, PASSES, CLU], U32, name="a_codes%d" % b, align_bytes=64) for b in range(IMG)]
         a_planes = [keep.tile([P, 2 * PASSES, CLU], U8, name="a_plane%d" % k, align_bytes=64) for k in range(IMG // 2)]
         y_codes = [keep.tile([P, IMG * CLU], U32, name="y_codes%d" % h, align_bytes=64) for h in range(2)]
         y_plane = keep.tile([P, IMG * CLU], U8, name="y_plane", align_bytes=64)
-        handed = [keep.tile([P, HALF * PACK], BF16, name="handed%d" % k, align_bytes=64) for k in range(2)]
-        ys = [[keep.tile([P, CTILES, HALF], F32, name="y%d%d" % (b, h), align_bytes=64) for h in range(2)] for b in range(IMG)]
+        arena = keep.tile([P, 6 * CHUNK], BF16, name="arena", align_bytes=64)
+        ys = [keep.tile([P, 2 * CTILES * HALF], F32, name="y%d" % b, align_bytes=64) for b in range(IMG)]
+        yb = [keep.tile([P, IMG * CLU * PACK], BF16, name="yb%d" % h, align_bytes=64) for h in range(2)]
         raw = {}
 
         def load_x(b, g):
@@ -62,8 +63,8 @@ def tile_vlad_residual_sums_k2_kernel(tc, a_words, a_scales, x, mass, centres, g
             src = a_words[PASSES * b:PASSES * (b + 1)].rearrange("g p n t -> p g (n t)").bitcast(I32)
             nc.sync.dma_start(out=a_codes[b][:].bitcast(I32), in_=src)
 
-        def load_centres(ct):
-            nc.sync.dma_start(out=cen[ct][:], in_=centres[ct * P:(ct + 1) * P, :])
+        def load_centres(h):
+            nc.sync.dma_start(out=cen[h][:], in_=centres[:, h * HALF:(h + 1) * HALF].rearrange("(k p) d -> p k d", p=P))
 
         def load_scales(pair):
             groups = slice(2 * PASSES * pair, 2 * PASSES * (pair + 1))
@@ -83,9 +84,10 @@ def tile_vlad_residual_sums_k2_kernel(tc, a_words, a_scales, x, mass, centres, g
         load_x(0, 1)
         load_scales(0)
         load_a(0)
-        for g in range(PASSES):
-            load_centres(g)
-            load_x(1, g)
+        load_centres(0)
+        load_x(1, 0)
+        load_x(1, 1)
+        load_centres(1)
         load_a(1)
         load_x(2, 0)
         load_x(2, 1)
@@ -95,109 +97,96 @@ def tile_vlad_residual_sums_k2_kernel(tc, a_words, a_scales, x, mass, centres, g
         load_x(3, 1)
         load_a(3)
 
-        grouped = {(b, 1, 1): handed[b % 2] for b in range(IMG)}
-        grouped[1, 0, 1], grouped[2, 0, 1] = handed
-        y16 = {(0, h): handed[h] for h in range(2)}
+        place = {(0, 0, 0): 0, (0, 0, 1): 1, (0, 1, 1): 2, (0, 1, 0): 3,
+                 (1, 0, 0): 1, (1, 0, 1): 2, (1, 1, 0): 3, (1, 1, 1): 1,
+                 (2, 0, 0): 2, (2, 0, 1): 3, (2, 1, 0): 0, (2, 1, 1): 5,
+                 (3, 0, 0): 4, (3, 0, 1): 5, (3, 1, 0): 2, (3, 1, 1): 1}
         xq = {}
         acc = {}
-        yb = [keep.tile([P, IMG * CLU, 2], F32, name="yb%d" % h, align_bytes=64) for h in range(2)]
+        y16 = {}
         turned = {}
 
-        def chunk_views(b, g, h, c0, c1):
-            if (b, g, h) not in grouped:
-                grouped[b, g, h] = work.tile([P, HALF * PACK], BF16, name="grouped", bufs=6, align_bytes=64)
-            dst = grouped[b, g, h][:].rearrange("p (c t) -> p c t", t=PACK)
-            return dst[:, c0:c1, :], raw[b, g][:, :, h * HALF + c0:h * HALF + c1]
+        def load_views(b, g, c0, c1):
+            at = place[b, g, c0 // HALF] * CHUNK + (c0 % HALF) * PACK
+            dst = arena[:, at:at + (c1 - c0) * PACK].rearrange("p (c t) -> p c t", t=PACK)
+            return dst, raw[b, g][:, :, c0:c1]
 
-        def interleave_on_vector(b, g, h, c0, c1):
-            dst, src = chunk_views(b, g, h, c0, c1)
+        def interleave_on_vector(b, g, c0, c1):
+            dst, src = load_views(b, g, c0, c1)
             nc.vector.tensor_copy(out=dst.rearrange("p (c i) t -> p c t i", i=4), in_=src.rearrange("p t (c i) -> p c t i", i=4))
 
         def gpsimd_copy(out, in_):
             nc.gpsimd.tensor_scalar(out=out, in0=in_, scalar1=1.0, scalar2=0.0, op0=ALU.mult, op1=ALU.add)
 
-        def interleave_on_gpsimd(b, g, h, c0, c1):
-            dst, src = chunk_views(b, g, h, c0, c1)
+        def interleave_on_gpsimd(b, g, c0, c1):
+            dst, src = load_views(b, g, c0, c1)
             gpsimd_copy(dst, src.rearrange("p t c -> p c t"))
 
-        def interleave_on_scalar(b, g, h, c0=0, c1=HALF):
-            dst, src = chunk_views(b, g, h, c0, c1)
+        def interleave_on_scalar(b, g, c0, c1):
+            dst, src = load_views(b, g, c0, c1)
             nc.scalar.copy(out=dst.rearrange("p (c i) (s t) -> p c s i t", i=8, t=2),
                            in_=src.rearrange("p (s t) (c i) -> p c s i t", i=8, t=2))
 
-        def quantize_x(b, g, h):
-            codes = work.tile([P, HALF], U32, name="x_codes", bufs=6, align_bytes=64)
-            plane = work.tile([P, HALF], U8, name="x_plane", bufs=6, align_bytes=64)
-            nc.vector.quantize_mx(out=codes[:].bitcast(E4M3X4), scales=plane[:], in_=grouped[b, g, h][:])
-            xq[b, g, h] = (codes, plane)
+        def quantize_x(b, g, h, h1=None):
+            if (b, g) not in xq:
+                codes = work.tile([P, DIM], U32, name="x_codes", align_bytes=64)
+                plane = work.tile([P, DIM], U8, name="x_plane", align_bytes=64)
+                xq[b, g] = (codes, plane)
+            codes, plane = xq[b, g]
+            n = (h1 or h + 1) - h
+            at = place[b, g, h] * CHUNK
+            cl = slice(h * HALF, (h + n) * HALF)
+            nc.vector.quantize_mx(out=codes[:, cl].bitcast(E4M3X4), scales=plane[:, cl], in_=arena[:, at:at + n * CHUNK])
 
-        def multiply(b, h, ct, g, first):
+        def multiply(b, h, ct, g, first=0):
             cl = slice(ct * P, (ct + 1) * P)
             if g == first:
                 acc[ct, h] = psum.tile([P, HALF], F32, name="acc%d%d" % (ct, h))
             a_scale = a_planes[b // 2][:, PASSES * (b % 2) + g, :]
-            codes, plane = xq[b, g, h]
+            codes, plane = xq[b, g]
             nc.tensor.matmul_mx(
                 out=acc[ct, h][:],
                 lhsT=a_codes[b][:, g, cl].bitcast(E5M2X4), lhsT_scale=a_scale[:, cl],
-                rhs=codes[:].bitcast(E4M3X4), rhs_scale=plane[:],
+                rhs=codes[:, h * HALF:(h + 1) * HALF].bitcast(E4M3X4), rhs_scale=plane[:, h * HALF:(h + 1) * HALF],
                 start=(g == first), stop=(g != first))
 
-        def fill_bank(b, h, ct):
-            for g in (h, 1 - h):
-                multiply(b, h, ct, g, h)
-
-        def fill_by_pass(b, h):
-            for g in range(PASSES):
+        def passes(b, g, h0=0, h1=2):
+            for h in range(h0, h1):
                 for ct in range(CTILES):
-                    multiply(b, h, ct, g, 0)
+                    multiply(b, h, ct, g)
 
-        def warm_up(b):
-            for ct in range(CTILES):
-                idle = psum.tile([P, HALF], F32, name="acc%d1" % ct)
-                codes, plane = xq[b, 1, 1]
-                nc.tensor.matmul_mx(
-                    out=idle[:], lhsT=a_codes[0][:, 0, 0:P].bitcast(E5M2X4), lhsT_scale=a_planes[0][:, 0, 0:P],
-                    rhs=codes[:].bitcast(E4M3X4), rhs_scale=plane[:], start=True, stop=True)
+        def y_of(b, h, c0, c1):
+            return ys[b][:, (h * CTILES + c0) * HALF:(h * CTILES + c1) * HALF]
 
-        def residual(b, h, c0=0, c1=CTILES):
-            for ct in range(c0, c1):
-                u = b * CTILES + ct
-                nc.vector.scalar_tensor_tensor(
-                    out=ys[b][h][:, ct, :], in0=cen[ct][:, h * HALF:(h + 1) * HALF], scalar=neg_mass[:, u:u + 1],
-                    in1=acc[ct, h][:], op0=ALU.mult, op1=ALU.add)
+        def residual(b, h, ct):
+            u = b * CTILES + ct
+            nc.vector.scalar_tensor_tensor(
+                out=y_of(b, h, ct, ct + 1), in0=cen[h][:, ct, :], scalar=neg_mass[:, u:u + 1],
+                in1=acc[ct, h][:], op0=ALU.mult, op1=ALU.add)
 
-        def scale(b, h, ct):
-            nc.vector.tensor_tensor(out=ys[b][h][:, ct, :], in0=ys[b][h][:, ct, :], in1=gain_all[:, h * HALF:(h + 1) * HALF], op=ALU.mult)
-
-        def scale_part(b, h):
-            spread = gain_all[:, h * HALF:(h + 1) * HALF].unsqueeze(1).to_broadcast([P, CTILES, HALF])
-            nc.vector.tensor_tensor(out=ys[b][h][:], in0=ys[b][h][:], in1=spread, op=ALU.mult)
+        def scale(b, h, c0=0, c1=CTILES):
+            part = y_of(b, h, c0, c1).rearrange("p (k d) -> p k d", d=HALF)
+            spread = gain_all[:, h * HALF:(h + 1) * HALF].unsqueeze(1).to_broadcast([P, c1 - c0, HALF])
+            nc.vector.tensor_tensor(out=part, in0=part, in1=spread, op=ALU.mult)
 
         def store_y(b, h, c0=0, c1=CTILES):
             dst = out_0[b, c0 * P:c1 * P, h * HALF:(h + 1) * HALF].rearrange("(k p) d -> p k d", p=P)
-            nc.sync.dma_start(out=dst, in_=ys[b][h][:, c0:c1, :])
+            nc.sync.dma_start(out=dst, in_=y_of(b, h, c0, c1).rearrange("p (k d) -> p k d", d=HALF))
 
-        def open_window(b):
-            residual(b, 0)
-            for ct in range(CTILES):
-                scale(b, 0, ct)
-            store_y(b, 0)
+        def round_views(b, h, c0, c1, room):
+            n = c1 - c0
+            if room is None:
+                room = work.tile([P, CTILES * HALF], BF16, name="y16", bufs=8, align_bytes=64)[:, 0:n * HALF]
+            dst = room.rearrange("p (w q e) -> p w q e", w=2, e=2)
+            for k in range(n):
+                y16[b, h + (c0 + k) // CTILES, (c0 + k) % CTILES] = dst[:, :, k * P:(k + 1) * P, :]
+            return dst, y_of(b, h, c0, c1).rearrange("p (q w e) -> p w q e", w=2, e=2)
 
-        def rounded(b, h):
-            if (b, h) not in y16:
-                y16[b, h] = work.tile([P, CTILES * HALF], BF16, name="y16", bufs=6, align_bytes=64)
-            return y16[b, h][:, 0:CTILES * HALF].rearrange("p (w q e) -> p w q e", w=2, e=2)
-
-        def round_views(b, h, c0, c1):
-            src = ys[b][h][:, c0:c1, :].rearrange("p k (q w e) -> p w (k q) e", w=2, e=2)
-            return rounded(b, h)[:, :, c0 * P:c1 * P, :], src
-
-        def round_on_gpsimd(b, h, c0=0, c1=CTILES):
-            gpsimd_copy(*round_views(b, h, c0, c1))
+        def round_on_gpsimd(b, h, c0=0, c1=CTILES, room=None):
+            gpsimd_copy(*round_views(b, h, c0, c1, room))
 
         def round_on_scalar(b, h, c0=0, c1=CTILES):
-            dst, src = round_views(b, h, c0, c1)
+            dst, src = round_views(b, h, c0, c1, None)
             nc.scalar.copy(out=dst, in_=src)
 
         def turn(b, h, c0=0, c1=CTILES):
@@ -205,18 +194,30 @@ def tile_vlad_residual_sums_k2_kernel(tc, a_words, a_scales, x, mass, centres, g
             turned[b, h, c0] = bank
             for ct in range(c0, c1):
                 for w in range(2):
-                    words = rounded(b, h)[:, w, ct * P:(ct + 1) * P, :].rearrange("p q e -> p (q e)").bitcast(F32)
+                    words = y16[b, h, ct][:, w, :, :].rearrange("p q e -> p (q e)").bitcast(F32)
                     nc.tensor.transpose(bank[:, ct - c0, w, :], words, ident32[:])
 
         def gather_words(b, h, c0=0, c1=CTILES):
-            dst = yb[h][:, b * CLU + c0 * P:b * CLU + c1 * P, :]
-            nc.scalar.copy(out=dst.rearrange("p (k c i) w -> p k c w i", k=c1 - c0, i=2),
+            dst = yb[h][:, (b * CLU + c0 * P) * PACK:(b * CLU + c1 * P) * PACK].bitcast(F32)
+            nc.scalar.copy(out=dst.rearrange("p (k c i w) -> p k c w i", k=c1 - c0, i=2, w=2),
                            in_=turned[b, h, c0][:].rearrange("p k w (c i) -> p k c w i", i=2))
+
+        def turn_values(b, h, ct):
+            bank = psum.tile([P, PACK, P], F32, name="turned", bufs=3)
+            turned[b, h, ct] = bank
+            values = y_of(b, h, ct, ct + 1).rearrange("p (q t) -> p t q", t=PACK)
+            for s in range(PACK):
+                nc.tensor.transpose(bank[:, s, :], values[:, s, :], ident32[:])
+
+        def gather_values(b, h, ct):
+            dst = yb[h][:, (b * CLU + ct * P) * PACK:(b * CLU + (ct + 1) * P) * PACK]
+            nc.scalar.copy(out=dst.rearrange("p (c i t) -> p c t i", i=2, t=PACK),
+                           in_=turned[b, h, ct][:].rearrange("p t (c i) -> p c t i", i=2))
 
         def quantize_y(h, b0, b1):
             cl = slice(b0 * CLU, b1 * CLU)
             nc.vector.quantize_mx(out=y_codes[h][:, cl].bitcast(E4M3X4), scales=y_plane[4 * h:, cl],
-                                  in_=yb[h][:, cl, :].rearrange("p c w -> p (c w)").bitcast(BF16))
+                                  in_=yb[h][:, b0 * CLU * PACK:b1 * CLU * PACK])
 
         def store_codes(h, b0, b1):
             dst = out_1[h][:, b0 * CLU:b1 * CLU, :].rearrange("p m t -> p (m t)").bitcast(I32)
@@ -231,111 +232,120 @@ def tile_vlad_residual_sums_k2_kernel(tc, a_words, a_scales, x, mass, centres, g
                 nc.tensor.transpose(gain_all[:, j * P:(j + 1) * P], cols[:, j:j + 1].to_broadcast([P, P]), ident16[:])
 
         for h in range(2):
-            interleave_on_vector(0, 0, h, 0, HALF // 2)
-            interleave_on_scalar(0, 0, h, HALF // 2, HALF)
+            interleave_on_vector(0, 0, h * HALF, h * HALF + HALF // 2)
+            interleave_on_scalar(0, 0, h * HALF + HALF // 2, (h + 1) * HALF)
         spread_constants()
         quantize_x(0, 0, 0)
         for h, share in enumerate((VECTOR_URGENT, VECTOR_HEAD_LAST)):
-            interleave_on_vector(0, 1, h, 0, share)
-            interleave_on_scalar(0, 1, h, share, HALF)
+            interleave_on_vector(0, 1, h * HALF, h * HALF + share)
+            interleave_on_scalar(0, 1, h * HALF + share, (h + 1) * HALF)
         for g, h in ((1, 0), (0, 1), (1, 1)):
             quantize_x(0, g, h)
+        passes(0, 0, 0, 1)
+        passes(0, 1, 0, 1)
         for ct in range(CTILES):
-            multiply(0, 0, ct, 0, 0)
-        multiply(0, 0, 0, 1, 0)
-        for g in range(PASSES):
-            multiply(0, 1, 0, g, 0)
-        multiply(0, 0, 1, 1, 0)
-        for g in range(PASSES):
-            multiply(0, 1, 1, g, 0)
+            multiply(0, 1, ct, 0)
+            multiply(0, 1, ct, 1)
 
-        def close_block(b):
-            for g, h in ((1, 0), (1, 1), (0, 1)):
+        residual(0, 0, 0)
+        residual(0, 0, 1)
+        scale(0, 0, 0, 1)
+        scale(0, 0, 1, 2)
+        store_y(0, 0)
+        interleave_on_gpsimd(1, 0, DIM - GPSIMD_FIRST, DIM)
+        interleave_on_scalar(1, 0, 0, DIM - GPSIMD_FIRST - VECTOR_CATCH_UP)
+        interleave_on_vector(1, 0, DIM - GPSIMD_FIRST - VECTOR_CATCH_UP, DIM - GPSIMD_FIRST)
+        quantize_x(1, 0, 0)
+        quantize_x(1, 0, 1)
+        passes(1, 0, 0, 1)
+        residual(0, 1, 0)
+        residual(0, 1, 1)
+        scale(0, 1, 0, 1)
+        passes(1, 0, 1, 2)
+        interleave_on_gpsimd(1, 1, DIM - GPSIMD_SECOND, DIM)
+        interleave_on_scalar(1, 1, 0, HALF)
+        interleave_on_scalar(1, 1, HALF, DIM - GPSIMD_SECOND)
+        quantize_x(1, 1, 0)
+        quantize_x(1, 1, 1)
+        passes(1, 1)
+        scale(0, 1, 1, 2)
+        store_y(0, 1)
+
+        def next_image(b, first, second):
+            interleave_on_gpsimd(b, 0, DIM - first, DIM)
+            if second:
+                interleave_on_gpsimd(b, 1, DIM - second, DIM)
+            interleave_on_scalar(b, 0, 0, DIM - first)
+            interleave_on_scalar(b, 1, 0, HALF)
+            interleave_on_scalar(b, 1, HALF, DIM - second)
+
+        def block(b):
+            for g, h in ((0, 0), (1, 0), (1, 1), (0, 1)):
                 quantize_x(b, g, h)
 
-        residual(0, 0, 0, 1)
-        scale(0, 0, 0)
-        residual(0, 1, 0, 1)
-        residual(0, 0, 1, 2)
-        scale(0, 1, 0)
-        residual(0, 1, 1, 2)
-        scale(0, 0, 1)
-        store_y(0, 0)
-        scale(0, 1, 1)
-        store_y(0, 1)
-        warm_up(0)
-        interleave_on_gpsimd(1, 0, 1, SCALAR_WAITING, HALF)
-        interleave_on_gpsimd(1, 1, 0, HALF // 2, HALF)
-        interleave_on_scalar(1, 0, 0)
-        interleave_on_scalar(1, 0, 1, 0, SCALAR_WAITING)
-        interleave_on_scalar(1, 1, 0, 0, HALF // 2)
-        interleave_on_scalar(1, 1, 1, VECTOR_CATCH_UP, HALF)
-        quantize_x(1, 0, 0)
-        interleave_on_vector(1, 1, 1, 0, VECTOR_CATCH_UP)
-        close_block(1)
-        fill_by_pass(1, 0)
-        for ct in range(CTILES):
-            fill_bank(1, 1, ct)
+        def fill_bank(b, h, ct):
+            for g in (h, 1 - h):
+                multiply(b, h, ct, g, h)
+
+        def open_window(b):
+            for ct in range(CTILES):
+                residual(b, 0, ct)
+            for ct in range(CTILES):
+                scale(b, 0, ct, ct + 1)
+            store_y(b, 0)
+            for ct in range(CTILES):
+                residual(b, 1, ct)
 
         open_window(1)
-        residual(1, 1)
-        scale(1, 1, 0)
-        warm_up(1)
-        interleave_on_gpsimd(2, 0, 1, 0, HALF)
-        interleave_on_gpsimd(2, 1, 1, HALF - GPSIMD_BEHIND_CHUNK, HALF)
-        interleave_on_scalar(2, 0, 0)
-        interleave_on_scalar(2, 1, 0)
-        interleave_on_scalar(2, 1, 1, 0, HALF - GPSIMD_BEHIND_CHUNK)
-        quantize_x(2, 0, 0)
-        close_block(2)
+        scale(1, 1, 0, 1)
+        for h, ct in ((0, 0), (0, 1), (1, 0)):
+            turn_values(0, h, ct)
+        next_image(2, 544, 176)
+        block(2)
         for h in range(2):
             for ct in range(CTILES):
                 fill_bank(2, h, ct)
 
-        scale(1, 1, 1)
+        scale(1, 1, 1, 2)
         store_y(1, 1)
         open_window(2)
-        residual(2, 1)
-        round_on_gpsimd(0, 0)
-        turn(0, 0)
-        warm_up(2)
-        interleave_on_gpsimd(3, 0, 1, HALF - GPSIMD_BEHIND_ROUNDING, HALF)
-        interleave_on_scalar(3, 0, 0)
-        interleave_on_scalar(3, 1, 0)
-        interleave_on_scalar(3, 0, 1, 0, HALF - GPSIMD_BEHIND_ROUNDING)
-        interleave_on_scalar(3, 1, 1)
-        round_on_scalar(1, 1)
-        gather_words(0, 0)
-        round_on_scalar(2, 0)
-        quantize_x(3, 0, 0)
-        close_block(3)
+        next_image(3, 656, 0)
+        block(3)
         for h, ct in ((0, 0), (0, 1), (1, 0)):
             fill_bank(3, h, ct)
-        turn(1, 1)
-        turn(2, 0)
-        round_on_gpsimd(0, 1, 1, 2)
-        round_on_scalar(0, 1, 0, 1)
-        fill_bank(3, 1, 1)
-        turn(0, 1)
 
-        scale_part(2, 1)
+        for h, ct in ((0, 0), (0, 1), (1, 0)):
+            gather_values(0, h, ct)
+        round_on_scalar(0, 1, 1, 2)
+        round_on_scalar(2, 0)
+        round_on_scalar(1, 0)
+        late = place[3, 1, 1] * CHUNK
+        round_on_gpsimd(1, 1, 0, CTILES, arena[:, late:late + CTILES * HALF])
+        turn(0, 1, 1, 2)
+        turn(2, 0)
+        turn(1, 1)
+        fill_bank(3, 1, 1)
+        scale(2, 1)
         store_y(2, 1)
-        round_on_gpsimd(1, 0)
         round_on_gpsimd(2, 1)
-        gather_words(1, 1)
+        gather_words(0, 1, 1, 2)
         gather_words(2, 0)
         turn(1, 0)
-        open_window(3)
-        round_on_scalar(3, 0, 0, 1)
-        gather_words(0, 1)
-        round_on_gpsimd(3, 0, 1, 2)
+        residual(3, 0, 0)
+        residual(3, 0, 1)
+        for ct in range(CTILES):
+            scale(3, 0, ct, ct + 1)
+            store_y(3, 0, ct, ct + 1)
+            round_on_gpsimd(3, 0, ct, ct + 1)
+        gather_words(1, 1)
         turn(2, 1)
         gather_words(1, 0)
         turn(3, 0)
-        residual(3, 1)
         gather_words(2, 1)
+        residual(3, 1, 0)
+        residual(3, 1, 1)
         for ct in range(CTILES):
-            scale(3, 1, ct)
+            scale(3, 1, ct, ct + 1)
             store_y(3, 1, ct, ct + 1)
             round_on_scalar(3, 1, ct, ct + 1)
         gather_words(3, 0)

@@ -26,9 +26,9 @@ CHUNK = HALF * PACK
 
 VECTOR_URGENT = 336
 VECTOR_HEAD_LAST = 192
-GPSIMD_FIRST = 160
-GPSIMD_SECOND = 240
-VECTOR_CATCH_UP = 352
+GPSIMD_FIRST = 416
+GPSIMD_SECOND = 208
+VECTOR_CATCH_UP = 96
 
 
 def tile_vlad_residual_sums_k2_kernel(tc, a_words, a_scales, x, mass, centres, gain, out_0, out_1, out_2):
@@ -45,12 +45,13 @@ def tile_vlad_residual_sums_k2_kernel(tc, a_words, a_scales, x, mass, centres, g
         cols = keep.tile([P, ROWS], BF16, name="cols", align_bytes=64)
         neg_mass = keep.tile([P, ROWS], F32, name="neg_mass", align_bytes=64)
         gain_all = psum.tile([P, DIM], BF16, name="gain_all")
+        gain_high = keep.tile([P, HALF], BF16, name="gain_high", align_bytes=64)
         cen = [keep.tile([P, CTILES, HALF], BF16, name="cen%d" % h, align_bytes=64) for h in range(2)]
         a_codes = [keep.tile([P, PASSES, CLU], U32, name="a_codes%d" % b, align_bytes=64) for b in range(IMG)]
         a_planes = [keep.tile([P, 2 * PASSES, CLU], U8, name="a_plane%d" % k, align_bytes=64) for k in range(IMG // 2)]
         y_codes = [keep.tile([P, IMG * CLU], U32, name="y_codes%d" % h, align_bytes=64) for h in range(2)]
         y_plane = keep.tile([P, IMG * CLU], U8, name="y_plane", align_bytes=64)
-        arena = keep.tile([P, 6 * CHUNK], BF16, name="arena", align_bytes=64)
+        arena = keep.tile([P, 7 * CHUNK], BF16, name="arena", align_bytes=64)
         ys = [keep.tile([P, 2 * CTILES * HALF], F32, name="y%d" % b, align_bytes=64) for b in range(IMG)]
         yb = [keep.tile([P, IMG * CLU * PACK], BF16, name="yb%d" % h, align_bytes=64) for h in range(2)]
         raw = {}
@@ -84,10 +85,9 @@ def tile_vlad_residual_sums_k2_kernel(tc, a_words, a_scales, x, mass, centres, g
         load_x(0, 1)
         load_scales(0)
         load_a(0)
-        load_centres(0)
-        load_x(1, 0)
-        load_x(1, 1)
-        load_centres(1)
+        for g in range(PASSES):
+            load_centres(g)
+            load_x(1, g)
         load_a(1)
         load_x(2, 0)
         load_x(2, 1)
@@ -98,13 +98,14 @@ def tile_vlad_residual_sums_k2_kernel(tc, a_words, a_scales, x, mass, centres, g
         load_a(3)
 
         place = {(0, 0, 0): 0, (0, 0, 1): 1, (0, 1, 1): 2, (0, 1, 0): 3,
-                 (1, 0, 0): 1, (1, 0, 1): 2, (1, 1, 0): 3, (1, 1, 1): 1,
-                 (2, 0, 0): 2, (2, 0, 1): 3, (2, 1, 0): 0, (2, 1, 1): 5,
-                 (3, 0, 0): 4, (3, 0, 1): 5, (3, 1, 0): 2, (3, 1, 1): 1}
+                 (1, 0, 0): 1, (1, 0, 1): 2, (1, 1, 0): 0, (1, 1, 1): 4,
+                 (2, 0, 0): 3, (2, 0, 1): 4, (2, 1, 0): 1, (2, 1, 1): 6,
+                 (3, 0, 0): 5, (3, 0, 1): 6, (3, 1, 0): 2, (3, 1, 1): 0}
         xq = {}
         acc = {}
         y16 = {}
         turned = {}
+        moved = {}
 
         def load_views(b, g, c0, c1):
             at = place[b, g, c0 // HALF] * CHUNK + (c0 % HALF) * PACK
@@ -155,7 +156,9 @@ def tile_vlad_residual_sums_k2_kernel(tc, a_words, a_scales, x, mass, centres, g
                 for ct in range(CTILES):
                     multiply(b, h, ct, g)
 
-        def y_of(b, h, c0, c1):
+        def y_of(b, h, c0, c1, done=False):
+            if done and (b, h) in moved:
+                return moved[b, h][:, c0 * HALF:c1 * HALF]
             return ys[b][:, (h * CTILES + c0) * HALF:(h * CTILES + c1) * HALF]
 
         def residual(b, h, ct):
@@ -167,20 +170,24 @@ def tile_vlad_residual_sums_k2_kernel(tc, a_words, a_scales, x, mass, centres, g
         def scale(b, h, c0=0, c1=CTILES):
             part = y_of(b, h, c0, c1).rearrange("p (k d) -> p k d", d=HALF)
             spread = gain_all[:, h * HALF:(h + 1) * HALF].unsqueeze(1).to_broadcast([P, c1 - c0, HALF])
-            nc.vector.tensor_tensor(out=part, in0=part, in1=spread, op=ALU.mult)
+            done = y_of(b, h, c0, c1, True).rearrange("p (k d) -> p k d", d=HALF)
+            nc.vector.tensor_tensor(out=done, in0=part, in1=spread, op=ALU.mult)
+
+        def scale_on_gpsimd(b, ct):
+            nc.gpsimd.tensor_tensor(out=y_of(b, 1, ct, ct + 1, True), in0=y_of(b, 1, ct, ct + 1), in1=gain_high[:], op=ALU.mult)
 
         def store_y(b, h, c0=0, c1=CTILES):
             dst = out_0[b, c0 * P:c1 * P, h * HALF:(h + 1) * HALF].rearrange("(k p) d -> p k d", p=P)
-            nc.sync.dma_start(out=dst, in_=y_of(b, h, c0, c1).rearrange("p (k d) -> p k d", d=HALF))
+            nc.sync.dma_start(out=dst, in_=y_of(b, h, c0, c1, True).rearrange("p (k d) -> p k d", d=HALF))
 
         def round_views(b, h, c0, c1, room):
             n = c1 - c0
             if room is None:
-                room = work.tile([P, CTILES * HALF], BF16, name="y16", bufs=8, align_bytes=64)[:, 0:n * HALF]
+                room = keep.tile([P, n * HALF], BF16, name="y16_%d%d%d" % (b, h, c0), align_bytes=64)[:]
             dst = room.rearrange("p (w q e) -> p w q e", w=2, e=2)
             for k in range(n):
                 y16[b, h + (c0 + k) // CTILES, (c0 + k) % CTILES] = dst[:, :, k * P:(k + 1) * P, :]
-            return dst, y_of(b, h, c0, c1).rearrange("p (q w e) -> p w q e", w=2, e=2)
+            return dst, y_of(b, h, c0, c1, True).rearrange("p (q w e) -> p w q e", w=2, e=2)
 
         def round_on_gpsimd(b, h, c0=0, c1=CTILES, room=None):
             gpsimd_copy(*round_views(b, h, c0, c1, room))
@@ -224,21 +231,25 @@ def tile_vlad_residual_sums_k2_kernel(tc, a_words, a_scales, x, mass, centres, g
             nc.sync.dma_start(out=dst, in_=y_codes[h][:, b0 * CLU:b1 * CLU].bitcast(I32))
 
         def spread_constants():
-            first = psum.tile([P, P], BF16, name="turned", bufs=3)
-            nc.tensor.transpose(first[:], rows[:], ident16[:])
+            first = psum.tile([P, P + HALF], BF16, name="turned", bufs=3)
+            nc.tensor.transpose(first[:, 0:P], rows[:], ident16[:])
             nc.vector.tensor_copy(out=cols[:], in_=first[:, 0:ROWS])
             nc.vector.tensor_scalar(out=neg_mass[:], in0=first[:, ROWS:2 * ROWS], scalar1=-1.0, scalar2=None, op0=ALU.mult)
             for j in range(ROWS):
                 nc.tensor.transpose(gain_all[:, j * P:(j + 1) * P], cols[:, j:j + 1].to_broadcast([P, P]), ident16[:])
+            for j in range(ROWS // 2):
+                column = cols[:, ROWS // 2 + j:ROWS // 2 + j + 1]
+                nc.tensor.transpose(first[:, (j + 1) * P:(j + 2) * P], column.to_broadcast([P, P]), ident16[:])
+            return first[:, P:]
 
-        for h in range(2):
-            interleave_on_vector(0, 0, h * HALF, h * HALF + HALF // 2)
-            interleave_on_scalar(0, 0, h * HALF + HALF // 2, (h + 1) * HALF)
-        spread_constants()
+        interleave_on_vector(0, 0, 0, HALF)
+        interleave_on_scalar(0, 0, HALF, DIM)
+        spare = spread_constants()
         quantize_x(0, 0, 0)
         for h, share in enumerate((VECTOR_URGENT, VECTOR_HEAD_LAST)):
             interleave_on_vector(0, 1, h * HALF, h * HALF + share)
             interleave_on_scalar(0, 1, h * HALF + share, (h + 1) * HALF)
+        nc.scalar.copy(out=gain_high[:], in_=spare)
         for g, h in ((1, 0), (0, 1), (1, 1)):
             quantize_x(0, g, h)
         passes(0, 0, 0, 1)
@@ -247,29 +258,31 @@ def tile_vlad_residual_sums_k2_kernel(tc, a_words, a_scales, x, mass, centres, g
             multiply(0, 1, ct, 0)
             multiply(0, 1, ct, 1)
 
+        def open_window(b):
+            for h in range(2):
+                for ct in range(CTILES):
+                    residual(b, h, ct)
+            scale(b, 0)
+            store_y(b, 0)
+
         residual(0, 0, 0)
         residual(0, 0, 1)
-        scale(0, 0, 0, 1)
-        scale(0, 0, 1, 2)
-        store_y(0, 0)
-        interleave_on_gpsimd(1, 0, DIM - GPSIMD_FIRST, DIM)
-        interleave_on_scalar(1, 0, 0, DIM - GPSIMD_FIRST - VECTOR_CATCH_UP)
-        interleave_on_vector(1, 0, DIM - GPSIMD_FIRST - VECTOR_CATCH_UP, DIM - GPSIMD_FIRST)
-        quantize_x(1, 0, 0)
-        quantize_x(1, 0, 1)
-        passes(1, 0, 0, 1)
         residual(0, 1, 0)
+        scale(0, 0)
+        store_y(0, 0)
         residual(0, 1, 1)
-        scale(0, 1, 0, 1)
-        passes(1, 0, 1, 2)
-        interleave_on_gpsimd(1, 1, DIM - GPSIMD_SECOND, DIM)
-        interleave_on_scalar(1, 1, 0, HALF)
-        interleave_on_scalar(1, 1, HALF, DIM - GPSIMD_SECOND)
-        quantize_x(1, 1, 0)
-        quantize_x(1, 1, 1)
-        passes(1, 1)
-        scale(0, 1, 1, 2)
+        for ct in range(CTILES):
+            scale(0, 1, ct, ct + 1)
         store_y(0, 1)
+        interleave_on_gpsimd(1, 0, DIM - GPSIMD_FIRST, DIM)
+        interleave_on_gpsimd(1, 1, HALF - GPSIMD_SECOND, HALF)
+        interleave_on_scalar(1, 0, 0, DIM - GPSIMD_FIRST)
+        interleave_on_scalar(1, 1, 0, HALF - GPSIMD_SECOND)
+        interleave_on_scalar(1, 1, HALF + VECTOR_CATCH_UP, DIM)
+        quantize_x(1, 0, 0)
+        interleave_on_vector(1, 1, HALF, HALF + VECTOR_CATCH_UP)
+        for g, h in ((1, 0), (1, 1), (0, 1)):
+            quantize_x(1, g, h)
 
         def next_image(b, first, second):
             interleave_on_gpsimd(b, 0, DIM - first, DIM)
@@ -280,24 +293,20 @@ def tile_vlad_residual_sums_k2_kernel(tc, a_words, a_scales, x, mass, centres, g
             interleave_on_scalar(b, 1, HALF, DIM - second)
 
         def block(b):
-            for g, h in ((0, 0), (1, 0), (1, 1), (0, 1)):
+            for g, h in ((1, 0), (0, 0), (1, 1), (0, 1)):
                 quantize_x(b, g, h)
 
         def fill_bank(b, h, ct):
-            for g in (h, 1 - h):
-                multiply(b, h, ct, g, h)
+            for g in (1, 0):
+                multiply(b, h, ct, g, 1)
 
-        def open_window(b):
-            for ct in range(CTILES):
-                residual(b, 0, ct)
-            for ct in range(CTILES):
-                scale(b, 0, ct, ct + 1)
-            store_y(b, 0)
-            for ct in range(CTILES):
-                residual(b, 1, ct)
+        passes(1, 0, 0, 1)
+        passes(1, 1, 0, 1)
+        for ct in range(CTILES):
+            fill_bank(1, 1, ct)
 
         open_window(1)
-        scale(1, 1, 0, 1)
+        scale(1, 1, 1, 2)
         for h, ct in ((0, 0), (0, 1), (1, 0)):
             turn_values(0, h, ct)
         next_image(2, 544, 176)
@@ -306,61 +315,61 @@ def tile_vlad_residual_sums_k2_kernel(tc, a_words, a_scales, x, mass, centres, g
             for ct in range(CTILES):
                 fill_bank(2, h, ct)
 
-        scale(1, 1, 1, 2)
+        scale(1, 1, 0, 1)
         store_y(1, 1)
         open_window(2)
-        next_image(3, 656, 0)
+        for ct in range(CTILES):
+            gather_values(0, 0, ct)
+            turn_values(1, 0, ct)
+        next_image(3, 736, 0)
         block(3)
         for h, ct in ((0, 0), (0, 1), (1, 0)):
             fill_bank(3, h, ct)
 
-        for h, ct in ((0, 0), (0, 1), (1, 0)):
-            gather_values(0, h, ct)
+        gather_values(0, 1, 0)
+        for ct in range(CTILES):
+            gather_values(1, 0, ct)
         round_on_scalar(0, 1, 1, 2)
         round_on_scalar(2, 0)
-        round_on_scalar(1, 0)
+        round_on_scalar(1, 1)
         late = place[3, 1, 1] * CHUNK
-        round_on_gpsimd(1, 1, 0, CTILES, arena[:, late:late + CTILES * HALF])
-        turn(0, 1, 1, 2)
-        turn(2, 0)
-        turn(1, 1)
-        fill_bank(3, 1, 1)
-        scale(2, 1)
+        moved[2, 1] = arena[:, late:late + CHUNK].bitcast(F32)
+        scale(2, 1, 0, 1)
+        scale_on_gpsimd(2, 1)
         store_y(2, 1)
         round_on_gpsimd(2, 1)
+        turn(0, 1, 1, 2)
+        turn(2, 0)
+        fill_bank(3, 1, 1)
+        turn(1, 1)
         gather_words(0, 1, 1, 2)
+        turn(2, 1)
         gather_words(2, 0)
-        turn(1, 0)
-        residual(3, 0, 0)
-        residual(3, 0, 1)
+        for ct in range(CTILES):
+            residual(3, 0, ct)
         for ct in range(CTILES):
             scale(3, 0, ct, ct + 1)
-            store_y(3, 0, ct, ct + 1)
             round_on_gpsimd(3, 0, ct, ct + 1)
+        store_y(3, 0)
+        for ct in range(CTILES):
+            residual(3, 1, ct)
+        turn(3, 0, 0, 1)
         gather_words(1, 1)
-        turn(2, 1)
-        gather_words(1, 0)
-        turn(3, 0)
+        turn(3, 0, 1, 2)
         gather_words(2, 1)
-        residual(3, 1, 0)
-        residual(3, 1, 1)
+        gather_words(3, 0, 0, 1)
         for ct in range(CTILES):
             scale(3, 1, ct, ct + 1)
             store_y(3, 1, ct, ct + 1)
             round_on_scalar(3, 1, ct, ct + 1)
-        gather_words(3, 0)
-        for ct in range(CTILES):
             turn(3, 1, ct, ct + 1)
+        gather_words(3, 0, 1, 2)
+        for ct in range(CTILES):
             gather_words(3, 1, ct, ct + 1)
 
-        for h, b0, b1 in ((0, 0, 2), (1, 2, 3), (1, 0, 2)):
+        for h, b0, b1 in ((0, 0, 2), (1, 2, 3), (1, 0, 2), (0, 3, 4), (0, 2, 3), (1, 3, 4)):
             quantize_y(h, b0, b1)
             store_codes(h, b0, b1)
-        quantize_y(0, 2, 3)
-        quantize_y(0, 3, 4)
-        store_codes(0, 2, 4)
-        quantize_y(1, 3, 4)
-        store_codes(1, 3, 4)
         for q in range(4):
             queue = nc.scalar if q % 2 else nc.sync
             queue.dma_start(out=out_2[:, 4 * q:4 * q + 4, :].bitcast(I32), in_=y_plane[32 * q:32 * q + 8, :].bitcast(I32))

@@ -26,9 +26,9 @@ CHUNK = HALF * PACK
 
 VECTOR_URGENT = 336
 VECTOR_HEAD_LAST = 192
-GPSIMD_FIRST = 416
-GPSIMD_SECOND = 208
-VECTOR_CATCH_UP = 96
+GPSIMD_FIRST = 400
+GPSIMD_SECOND = 320
+GPSIMD_THIRD = 576
 
 
 def tile_vlad_residual_sums_k2_kernel(tc, a_words, a_scales, x, mass, centres, gain, out_0, out_1, out_2):
@@ -51,7 +51,7 @@ def tile_vlad_residual_sums_k2_kernel(tc, a_words, a_scales, x, mass, centres, g
         a_planes = [keep.tile([P, 2 * PASSES, CLU], U8, name="a_plane%d" % k, align_bytes=64) for k in range(IMG // 2)]
         y_codes = [keep.tile([P, IMG * CLU], U32, name="y_codes%d" % h, align_bytes=64) for h in range(2)]
         y_plane = keep.tile([P, IMG * CLU], U8, name="y_plane", align_bytes=64)
-        arena = keep.tile([P, 7 * CHUNK], BF16, name="arena", align_bytes=64)
+        arena = keep.tile([P, 6 * CHUNK], BF16, name="arena", align_bytes=64)
         ys = [keep.tile([P, 2 * CTILES * HALF], F32, name="y%d" % b, align_bytes=64) for b in range(IMG)]
         yb = [keep.tile([P, IMG * CLU * PACK], BF16, name="yb%d" % h, align_bytes=64) for h in range(2)]
         raw = {}
@@ -97,18 +97,22 @@ def tile_vlad_residual_sums_k2_kernel(tc, a_words, a_scales, x, mass, centres, g
         load_x(3, 1)
         load_a(3)
 
-        place = {(0, 0, 0): 0, (0, 0, 1): 1, (0, 1, 1): 2, (0, 1, 0): 3,
-                 (1, 0, 0): 1, (1, 0, 1): 2, (1, 1, 0): 0, (1, 1, 1): 4,
-                 (2, 0, 0): 3, (2, 0, 1): 4, (2, 1, 0): 1, (2, 1, 1): 6,
-                 (3, 0, 0): 5, (3, 0, 1): 6, (3, 1, 0): 2, (3, 1, 1): 0}
+        place = {(0, 0, 0): 0, (0, 0, 1): HALF, (0, 1, 1): 3 * HALF, (0, 1, 0): 4 * HALF,
+                 (1, 0, 0): 2 * HALF, (1, 0, 1): 3 * HALF, (1, 1, 1): 5 * HALF,
+                 (2, 1, 0): 3 * HALF, (2, 1, 1): 5 * HALF,
+                 (3, 0, 0): 4 * HALF, (3, 0, 1): 5 * HALF, (3, 1, 0): 0, (3, 1, 1): HALF}
+        place[1, 1, 0] = place[1, 0, 0] - (HALF - GPSIMD_SECOND)
+        place[2, 0, 0] = place[1, 1, 0] - (DIM - GPSIMD_THIRD)
+        place[2, 0, 1] = place[2, 0, 0] + HALF
         xq = {}
         acc = {}
         y16 = {}
         turned = {}
-        moved = {}
+        late = place[3, 1, 1] * PACK
+        moved = {(2, 1, True): arena[:, late:late + CHUNK].bitcast(F32)}
 
         def load_views(b, g, c0, c1):
-            at = place[b, g, c0 // HALF] * CHUNK + (c0 % HALF) * PACK
+            at = (place[b, g, c0 // HALF] + c0 % HALF) * PACK
             dst = arena[:, at:at + (c1 - c0) * PACK].rearrange("p (c t) -> p c t", t=PACK)
             return dst, raw[b, g][:, :, c0:c1]
 
@@ -135,7 +139,7 @@ def tile_vlad_residual_sums_k2_kernel(tc, a_words, a_scales, x, mass, centres, g
                 xq[b, g] = (codes, plane)
             codes, plane = xq[b, g]
             n = (h1 or h + 1) - h
-            at = place[b, g, h] * CHUNK
+            at = place[b, g, h] * PACK
             cl = slice(h * HALF, (h + n) * HALF)
             nc.vector.quantize_mx(out=codes[:, cl].bitcast(E4M3X4), scales=plane[:, cl], in_=arena[:, at:at + n * CHUNK])
 
@@ -157,8 +161,8 @@ def tile_vlad_residual_sums_k2_kernel(tc, a_words, a_scales, x, mass, centres, g
                     multiply(b, h, ct, g)
 
         def y_of(b, h, c0, c1, done=False):
-            if done and (b, h) in moved:
-                return moved[b, h][:, c0 * HALF:c1 * HALF]
+            if (b, h, done) in moved:
+                return moved[b, h, done][:, c0 * HALF:c1 * HALF]
             return ys[b][:, (h * CTILES + c0) * HALF:(h * CTILES + c1) * HALF]
 
         def residual(b, h, ct):
@@ -212,7 +216,7 @@ def tile_vlad_residual_sums_k2_kernel(tc, a_words, a_scales, x, mass, centres, g
         def turn_values(b, h, ct):
             bank = psum.tile([P, PACK, P], F32, name="turned", bufs=3)
             turned[b, h, ct] = bank
-            values = y_of(b, h, ct, ct + 1).rearrange("p (q t) -> p t q", t=PACK)
+            values = y_of(b, h, ct, ct + 1, True).rearrange("p (q t) -> p t q", t=PACK)
             for s in range(PACK):
                 nc.tensor.transpose(bank[:, s, :], values[:, s, :], ident32[:])
 
@@ -270,19 +274,22 @@ def tile_vlad_residual_sums_k2_kernel(tc, a_words, a_scales, x, mass, centres, g
         residual(0, 1, 0)
         scale(0, 0)
         store_y(0, 0)
+        interleave_on_gpsimd(1, 0, DIM - GPSIMD_FIRST, DIM)
+        interleave_on_scalar(1, 0, 0, HALF)
+        interleave_on_scalar(1, 0, HALF, DIM - GPSIMD_FIRST)
+        quantize_x(1, 0, 0)
+        quantize_x(1, 0, 1)
         residual(0, 1, 1)
         for ct in range(CTILES):
             scale(0, 1, ct, ct + 1)
         store_y(0, 1)
-        interleave_on_gpsimd(1, 0, DIM - GPSIMD_FIRST, DIM)
         interleave_on_gpsimd(1, 1, HALF - GPSIMD_SECOND, HALF)
-        interleave_on_scalar(1, 0, 0, DIM - GPSIMD_FIRST)
         interleave_on_scalar(1, 1, 0, HALF - GPSIMD_SECOND)
-        interleave_on_scalar(1, 1, HALF + VECTOR_CATCH_UP, DIM)
-        quantize_x(1, 0, 0)
-        interleave_on_vector(1, 1, HALF, HALF + VECTOR_CATCH_UP)
-        for g, h in ((1, 0), (1, 1), (0, 1)):
-            quantize_x(1, g, h)
+        interleave_on_scalar(1, 1, HALF, DIM)
+        passes(1, 0)
+        for h in range(2):
+            quantize_x(1, 1, h)
+        passes(1, 1)
 
         def next_image(b, first, second):
             interleave_on_gpsimd(b, 0, DIM - first, DIM)
@@ -300,16 +307,12 @@ def tile_vlad_residual_sums_k2_kernel(tc, a_words, a_scales, x, mass, centres, g
             for g in (1, 0):
                 multiply(b, h, ct, g, 1)
 
-        passes(1, 0, 0, 1)
-        passes(1, 1, 0, 1)
-        for ct in range(CTILES):
-            fill_bank(1, 1, ct)
 
         open_window(1)
         scale(1, 1, 1, 2)
         for h, ct in ((0, 0), (0, 1), (1, 0)):
             turn_values(0, h, ct)
-        next_image(2, 544, 176)
+        next_image(2, GPSIMD_THIRD, 208)
         block(2)
         for h in range(2):
             for ct in range(CTILES):
@@ -318,31 +321,26 @@ def tile_vlad_residual_sums_k2_kernel(tc, a_words, a_scales, x, mass, centres, g
         scale(1, 1, 0, 1)
         store_y(1, 1)
         open_window(2)
-        for ct in range(CTILES):
-            gather_values(0, 0, ct)
-            turn_values(1, 0, ct)
-        next_image(3, 736, 0)
+        for done, then in (((0, 0, 0), (0, 1, 1)), ((0, 0, 1), (1, 0, 0)), ((0, 1, 0), (1, 0, 1))):
+            gather_values(*done)
+            turn_values(*then)
+        next_image(3, 800, 0)
         block(3)
         for h, ct in ((0, 0), (0, 1), (1, 0)):
             fill_bank(3, h, ct)
 
-        gather_values(0, 1, 0)
+        gather_values(0, 1, 1)
         for ct in range(CTILES):
             gather_values(1, 0, ct)
-        round_on_scalar(0, 1, 1, 2)
         round_on_scalar(2, 0)
         round_on_scalar(1, 1)
-        late = place[3, 1, 1] * CHUNK
-        moved[2, 1] = arena[:, late:late + CHUNK].bitcast(F32)
         scale(2, 1, 0, 1)
         scale_on_gpsimd(2, 1)
         store_y(2, 1)
         round_on_gpsimd(2, 1)
-        turn(0, 1, 1, 2)
         turn(2, 0)
         fill_bank(3, 1, 1)
         turn(1, 1)
-        gather_words(0, 1, 1, 2)
         turn(2, 1)
         gather_words(2, 0)
         for ct in range(CTILES):

@@ -27,7 +27,7 @@ CHUNK = HALF * PACK
 VECTOR_URGENT = 336
 VECTOR_HEAD_LAST = 192
 GPSIMD_FIRST = 400
-GPSIMD_SECOND = 320
+GPSIMD_SECOND = 312
 GPSIMD_THIRD = 576
 
 
@@ -98,12 +98,10 @@ def tile_vlad_residual_sums_k2_kernel(tc, a_words, a_scales, x, mass, centres, g
         load_a(3)
 
         place = {(0, 0, 0): 0, (0, 0, 1): HALF, (0, 1, 1): 3 * HALF, (0, 1, 0): 4 * HALF,
-                 (1, 0, 0): 2 * HALF, (1, 0, 1): 3 * HALF, (1, 1, 1): 5 * HALF,
-                 (2, 1, 0): 3 * HALF, (2, 1, 1): 5 * HALF,
-                 (3, 0, 0): 4 * HALF, (3, 0, 1): 5 * HALF, (3, 1, 0): 0, (3, 1, 1): HALF}
-        place[1, 1, 0] = place[1, 0, 0] - (HALF - GPSIMD_SECOND)
-        place[2, 0, 0] = place[1, 1, 0] - (DIM - GPSIMD_THIRD)
-        place[2, 0, 1] = place[2, 0, 0] + HALF
+                 (1, 0, 0): 2 * HALF, (1, 0, 1): 3 * HALF, (1, 1, 0): 5 * HALF,
+                 (2, 0, 0): 4 * HALF, (2, 0, 1): 5 * HALF, (2, 1, 0): 3 * HALF, (2, 1, 1): 2 * HALF,
+                 (3, 0, 0): HALF, (3, 0, 1): 2 * HALF, (3, 1, 0): 4 * HALF, (3, 1, 1): 0}
+        place[1, 1, 1] = place[1, 0, 0] - (HALF - GPSIMD_SECOND)
         xq = {}
         acc = {}
         y16 = {}
@@ -225,10 +223,10 @@ def tile_vlad_residual_sums_k2_kernel(tc, a_words, a_scales, x, mass, centres, g
             nc.scalar.copy(out=dst.rearrange("p (c i t) -> p c t i", i=2, t=PACK),
                            in_=turned[b, h, ct][:].rearrange("p t (c i) -> p c t i", i=2))
 
-        def quantize_y(h, b0, b1):
-            cl = slice(b0 * CLU, b1 * CLU)
+        def quantize_y(h, u0, u1):
+            cl = slice(u0 * P, u1 * P)
             nc.vector.quantize_mx(out=y_codes[h][:, cl].bitcast(E4M3X4), scales=y_plane[4 * h:, cl],
-                                  in_=yb[h][:, b0 * CLU * PACK:b1 * CLU * PACK])
+                                  in_=yb[h][:, u0 * P * PACK:u1 * P * PACK])
 
         def store_codes(h, b0, b1):
             dst = out_1[h][:, b0 * CLU:b1 * CLU, :].rearrange("p m t -> p (m t)").bitcast(I32)
@@ -283,9 +281,9 @@ def tile_vlad_residual_sums_k2_kernel(tc, a_words, a_scales, x, mass, centres, g
         for ct in range(CTILES):
             scale(0, 1, ct, ct + 1)
         store_y(0, 1)
-        interleave_on_gpsimd(1, 1, HALF - GPSIMD_SECOND, HALF)
-        interleave_on_scalar(1, 1, 0, HALF - GPSIMD_SECOND)
-        interleave_on_scalar(1, 1, HALF, DIM)
+        interleave_on_gpsimd(1, 1, DIM - GPSIMD_SECOND, DIM)
+        interleave_on_scalar(1, 1, 0, HALF)
+        interleave_on_scalar(1, 1, HALF, DIM - GPSIMD_SECOND)
         passes(1, 0)
         for h in range(2):
             quantize_x(1, 1, h)
@@ -320,27 +318,36 @@ def tile_vlad_residual_sums_k2_kernel(tc, a_words, a_scales, x, mass, centres, g
 
         scale(1, 1, 0, 1)
         store_y(1, 1)
-        open_window(2)
-        for done, then in (((0, 0, 0), (0, 1, 1)), ((0, 0, 1), (1, 0, 0)), ((0, 1, 0), (1, 0, 1))):
-            gather_values(*done)
-            turn_values(*then)
-        next_image(3, 800, 0)
+        for ct in range(CTILES):
+            residual(2, 0, ct)
+        for ct in range(CTILES):
+            scale(2, 0, ct, ct + 1)
+        store_y(2, 0)
+        for ct in range(CTILES):
+            residual(2, 1, ct)
+        for ct in range(CTILES):
+            gather_values(0, 0, ct)
+            turn_values(1, 0, ct)
+        next_image(3, 752, 0)
         block(3)
         for h, ct in ((0, 0), (0, 1), (1, 0)):
             fill_bank(3, h, ct)
 
-        gather_values(0, 1, 1)
+        gather_values(0, 1, 0)
         for ct in range(CTILES):
             gather_values(1, 0, ct)
+        round_on_scalar(0, 1, 1, 2)
         round_on_scalar(2, 0)
         round_on_scalar(1, 1)
         scale(2, 1, 0, 1)
         scale_on_gpsimd(2, 1)
         store_y(2, 1)
         round_on_gpsimd(2, 1)
+        turn(0, 1, 1, 2)
         turn(2, 0)
         fill_bank(3, 1, 1)
         turn(1, 1)
+        gather_words(0, 1, 1, 2)
         turn(2, 1)
         gather_words(2, 0)
         for ct in range(CTILES):
@@ -365,9 +372,15 @@ def tile_vlad_residual_sums_k2_kernel(tc, a_words, a_scales, x, mass, centres, g
         for ct in range(CTILES):
             gather_words(3, 1, ct, ct + 1)
 
-        for h, b0, b1 in ((0, 0, 2), (1, 2, 3), (1, 0, 2), (0, 3, 4), (0, 2, 3), (1, 3, 4)):
-            quantize_y(h, b0, b1)
+        for h, b0, b1 in ((0, 0, 2), (1, 2, 3), (1, 0, 2)):
+            quantize_y(h, CTILES * b0, CTILES * b1)
             store_codes(h, b0, b1)
+        quantize_y(0, 4, 7)
+        quantize_y(0, 7, 8)
+        store_codes(0, 2, 4)
+        quantize_y(1, 6, 7)
+        quantize_y(1, 7, 8)
+        store_codes(1, 3, 4)
         for q in range(4):
             queue = nc.scalar if q % 2 else nc.sync
             queue.dma_start(out=out_2[:, 4 * q:4 * q + 4, :].bitcast(I32), in_=y_plane[32 * q:32 * q + 8, :].bitcast(I32))

@@ -24,11 +24,13 @@ CTILES = CLU // P
 ROWS = DIM // P
 CHUNK = HALF * PACK
 
-VECTOR_URGENT = 336
+VECTOR_URGENT = 304
 VECTOR_HEAD_LAST = 192
-GPSIMD_FIRST = 400
+GPSIMD_FIRST = 368
 GPSIMD_SECOND = 312
 GPSIMD_THIRD = 576
+GPSIMD_FOURTH = 192
+GPSIMD_FIFTH = 752
 
 
 def tile_vlad_residual_sums_k2_kernel(tc, a_words, a_scales, x, mass, centres, gain, out_0, out_1, out_2):
@@ -46,7 +48,7 @@ def tile_vlad_residual_sums_k2_kernel(tc, a_words, a_scales, x, mass, centres, g
         neg_mass = keep.tile([P, ROWS], F32, name="neg_mass", align_bytes=64)
         gain_all = psum.tile([P, DIM], BF16, name="gain_all")
         gain_high = keep.tile([P, HALF], BF16, name="gain_high", align_bytes=64)
-        cen = [keep.tile([P, CTILES, HALF], BF16, name="cen%d" % h, align_bytes=64) for h in range(2)]
+        cen = [[keep.tile([P, HALF], BF16, name="cen%d%d" % (h, ct), align_bytes=64) for ct in range(CTILES)] for h in range(2)]
         a_codes = [keep.tile([P, PASSES, CLU], U32, name="a_codes%d" % b, align_bytes=64) for b in range(IMG)]
         a_planes = [keep.tile([P, 2 * PASSES, CLU], U8, name="a_plane%d" % k, align_bytes=64) for k in range(IMG // 2)]
         y_codes = [keep.tile([P, IMG * CLU], U32, name="y_codes%d" % h, align_bytes=64) for h in range(2)]
@@ -64,8 +66,8 @@ def tile_vlad_residual_sums_k2_kernel(tc, a_words, a_scales, x, mass, centres, g
             src = a_words[PASSES * b:PASSES * (b + 1)].rearrange("g p n t -> p g (n t)").bitcast(I32)
             nc.sync.dma_start(out=a_codes[b][:].bitcast(I32), in_=src)
 
-        def load_centres(h):
-            nc.sync.dma_start(out=cen[h][:], in_=centres[:, h * HALF:(h + 1) * HALF].rearrange("(k p) d -> p k d", p=P))
+        def load_centres(h, ct):
+            nc.sync.dma_start(out=cen[h][ct][:], in_=centres[ct * P:(ct + 1) * P, h * HALF:(h + 1) * HALF])
 
         def load_scales(pair):
             groups = slice(2 * PASSES * pair, 2 * PASSES * (pair + 1))
@@ -85,9 +87,12 @@ def tile_vlad_residual_sums_k2_kernel(tc, a_words, a_scales, x, mass, centres, g
         load_x(0, 1)
         load_scales(0)
         load_a(0)
-        for g in range(PASSES):
-            load_centres(g)
-            load_x(1, g)
+        load_centres(0, 0)
+        load_x(1, 0)
+        load_centres(0, 1)
+        load_centres(1, 0)
+        load_x(1, 1)
+        load_centres(1, 1)
         load_a(1)
         load_x(2, 0)
         load_x(2, 1)
@@ -166,7 +171,7 @@ def tile_vlad_residual_sums_k2_kernel(tc, a_words, a_scales, x, mass, centres, g
         def residual(b, h, ct):
             u = b * CTILES + ct
             nc.vector.scalar_tensor_tensor(
-                out=y_of(b, h, ct, ct + 1), in0=cen[h][:, ct, :], scalar=neg_mass[:, u:u + 1],
+                out=y_of(b, h, ct, ct + 1), in0=cen[h][ct][:], scalar=neg_mass[:, u:u + 1],
                 in1=acc[ct, h][:], op0=ALU.mult, op1=ALU.add)
 
         def scale(b, h, c0=0, c1=CTILES):
@@ -284,18 +289,11 @@ def tile_vlad_residual_sums_k2_kernel(tc, a_words, a_scales, x, mass, centres, g
         interleave_on_gpsimd(1, 1, DIM - GPSIMD_SECOND, DIM)
         interleave_on_scalar(1, 1, 0, HALF)
         interleave_on_scalar(1, 1, HALF, DIM - GPSIMD_SECOND)
+        turn_values(0, 0, 0)
         passes(1, 0)
         for h in range(2):
             quantize_x(1, 1, h)
         passes(1, 1)
-
-        def next_image(b, first, second):
-            interleave_on_gpsimd(b, 0, DIM - first, DIM)
-            if second:
-                interleave_on_gpsimd(b, 1, DIM - second, DIM)
-            interleave_on_scalar(b, 0, 0, DIM - first)
-            interleave_on_scalar(b, 1, 0, HALF)
-            interleave_on_scalar(b, 1, HALF, DIM - second)
 
         def block(b):
             for g, h in ((1, 0), (0, 0), (1, 1), (0, 1)):
@@ -308,9 +306,15 @@ def tile_vlad_residual_sums_k2_kernel(tc, a_words, a_scales, x, mass, centres, g
 
         open_window(1)
         scale(1, 1, 1, 2)
-        for h, ct in ((0, 0), (0, 1), (1, 0)):
-            turn_values(0, h, ct)
-        next_image(2, GPSIMD_THIRD, 208)
+        turn_values(0, 0, 1)
+        turn_values(0, 1, 0)
+        interleave_on_gpsimd(2, 0, DIM - GPSIMD_THIRD, DIM)
+        interleave_on_gpsimd(2, 1, DIM - GPSIMD_FOURTH, DIM)
+        interleave_on_scalar(2, 0, 0, DIM - GPSIMD_THIRD)
+        gather_values(0, 0, 0)
+        turn_values(0, 1, 1)
+        interleave_on_scalar(2, 1, 0, HALF)
+        interleave_on_scalar(2, 1, HALF, DIM - GPSIMD_FOURTH)
         block(2)
         for h in range(2):
             for ct in range(CTILES):
@@ -326,28 +330,29 @@ def tile_vlad_residual_sums_k2_kernel(tc, a_words, a_scales, x, mass, centres, g
         for ct in range(CTILES):
             residual(2, 1, ct)
         for ct in range(CTILES):
-            gather_values(0, 0, ct)
+            gather_values(0, ct, 1 - ct)
             turn_values(1, 0, ct)
-        next_image(3, 752, 0)
+        interleave_on_gpsimd(3, 0, DIM - GPSIMD_FIFTH, DIM)
+        interleave_on_scalar(3, 0, 0, DIM - GPSIMD_FIFTH)
+        for h in range(2):
+            interleave_on_scalar(3, 1, h * HALF, (h + 1) * HALF)
         block(3)
         for h, ct in ((0, 0), (0, 1), (1, 0)):
             fill_bank(3, h, ct)
 
-        gather_values(0, 1, 0)
-        for ct in range(CTILES):
-            gather_values(1, 0, ct)
-        round_on_scalar(0, 1, 1, 2)
+        gather_values(0, 1, 1)
         round_on_scalar(2, 0)
+        gather_values(1, 0, 0)
         round_on_scalar(1, 1)
+        gather_values(1, 0, 1)
         scale(2, 1, 0, 1)
+        store_y(2, 1, 0, 1)
         scale_on_gpsimd(2, 1)
-        store_y(2, 1)
+        store_y(2, 1, 1, 2)
         round_on_gpsimd(2, 1)
-        turn(0, 1, 1, 2)
         turn(2, 0)
         fill_bank(3, 1, 1)
         turn(1, 1)
-        gather_words(0, 1, 1, 2)
         turn(2, 1)
         gather_words(2, 0)
         for ct in range(CTILES):

@@ -24,13 +24,13 @@ CTILES = CLU // P
 ROWS = DIM // P
 CHUNK = HALF * PACK
 
-VECTOR_URGENT = 304
+VECTOR_URGENT = 336
 VECTOR_HEAD_LAST = 192
-GPSIMD_FIRST = 368
+GPSIMD_FIRST = 400
 GPSIMD_SECOND = 312
-GPSIMD_THIRD = 576
-GPSIMD_FOURTH = 192
-GPSIMD_FIFTH = 752
+GPSIMD_THIRD = 512
+GPSIMD_FOURTH = 272
+GPSIMD_FIFTH = 784
 
 
 def tile_vlad_residual_sums_k2_kernel(tc, a_words, a_scales, x, mass, centres, gain, out_0, out_1, out_2):
@@ -50,7 +50,7 @@ def tile_vlad_residual_sums_k2_kernel(tc, a_words, a_scales, x, mass, centres, g
         gain_high = keep.tile([P, HALF], BF16, name="gain_high", align_bytes=64)
         cen = [[keep.tile([P, HALF], BF16, name="cen%d%d" % (h, ct), align_bytes=64) for ct in range(CTILES)] for h in range(2)]
         a_codes = [keep.tile([P, PASSES, CLU], U32, name="a_codes%d" % b, align_bytes=64) for b in range(IMG)]
-        a_planes = [keep.tile([P, 2 * PASSES, CLU], U8, name="a_plane%d" % k, align_bytes=64) for k in range(IMG // 2)]
+        a_planes = [keep.tile([P, PASSES * (1 + k // 2), CLU], U8, name="a_plane%d" % k, align_bytes=64) for k in range(3)]
         y_codes = [keep.tile([P, IMG * CLU], U32, name="y_codes%d" % h, align_bytes=64) for h in range(2)]
         y_plane = keep.tile([P, IMG * CLU], U8, name="y_plane", align_bytes=64)
         arena = keep.tile([P, 6 * CHUNK], BF16, name="arena", align_bytes=64)
@@ -70,7 +70,7 @@ def tile_vlad_residual_sums_k2_kernel(tc, a_words, a_scales, x, mass, centres, g
             nc.sync.dma_start(out=cen[h][ct][:], in_=centres[ct * P:(ct + 1) * P, h * HALF:(h + 1) * HALF])
 
         def load_scales(pair):
-            groups = slice(2 * PASSES * pair, 2 * PASSES * (pair + 1))
+            groups = slice(PASSES * pair, PASSES * (pair + 1 + pair // 2))
             for r in range(4):
                 nc.sync.dma_start(out=a_planes[pair][r:P:32, :, :].bitcast(I32),
                                   in_=a_scales[groups, r:16:4, :].rearrange("g q n -> q g n").bitcast(I32))
@@ -93,11 +93,12 @@ def tile_vlad_residual_sums_k2_kernel(tc, a_words, a_scales, x, mass, centres, g
         load_centres(1, 0)
         load_x(1, 1)
         load_centres(1, 1)
+        load_scales(1)
         load_a(1)
         load_x(2, 0)
         load_x(2, 1)
         load_x(3, 0)
-        load_scales(1)
+        load_scales(2)
         load_a(2)
         load_x(3, 1)
         load_a(3)
@@ -150,7 +151,7 @@ def tile_vlad_residual_sums_k2_kernel(tc, a_words, a_scales, x, mass, centres, g
             cl = slice(ct * P, (ct + 1) * P)
             if g == first:
                 acc[ct, h] = psum.tile([P, HALF], F32, name="acc%d%d" % (ct, h))
-            a_scale = a_planes[b // 2][:, PASSES * (b % 2) + g, :]
+            a_scale = a_planes[min(b, 2)][:, PASSES * (b // 3) + g, :]
             codes, plane = xq[b, g]
             nc.tensor.matmul_mx(
                 out=acc[ct, h][:],
@@ -293,7 +294,8 @@ def tile_vlad_residual_sums_k2_kernel(tc, a_words, a_scales, x, mass, centres, g
         passes(1, 0)
         for h in range(2):
             quantize_x(1, 1, h)
-        passes(1, 1)
+        for h, ct in ((0, 0), (0, 1), (1, 1), (1, 0)):
+            multiply(1, h, ct, 1)
 
         def block(b):
             for g, h in ((1, 0), (0, 0), (1, 1), (0, 1)):
@@ -310,15 +312,14 @@ def tile_vlad_residual_sums_k2_kernel(tc, a_words, a_scales, x, mass, centres, g
         turn_values(0, 1, 0)
         interleave_on_gpsimd(2, 0, DIM - GPSIMD_THIRD, DIM)
         interleave_on_gpsimd(2, 1, DIM - GPSIMD_FOURTH, DIM)
-        interleave_on_scalar(2, 0, 0, DIM - GPSIMD_THIRD)
         gather_values(0, 0, 0)
+        interleave_on_scalar(2, 0, 0, DIM - GPSIMD_THIRD)
         turn_values(0, 1, 1)
         interleave_on_scalar(2, 1, 0, HALF)
         interleave_on_scalar(2, 1, HALF, DIM - GPSIMD_FOURTH)
         block(2)
-        for h in range(2):
-            for ct in range(CTILES):
-                fill_bank(2, h, ct)
+        for h, ct in ((0, 0), (0, 1), (1, 1), (1, 0)):
+            fill_bank(2, h, ct)
 
         scale(1, 1, 0, 1)
         store_y(1, 1)

@@ -47,7 +47,7 @@ def tile_vlad_residual_sums_k2_kernel(tc, a_words, a_scales, x, mass, centres, g
         cols = keep.tile([P, ROWS], BF16, name="cols", align_bytes=64)
         neg_mass = keep.tile([P, ROWS], F32, name="neg_mass", align_bytes=64)
         gain_all = psum.tile([P, DIM], BF16, name="gain_all")
-        gain_high = keep.tile([P, HALF], BF16, name="gain_high", align_bytes=64)
+        gain_sb = keep.tile([P, DIM], BF16, name="gain_sb", align_bytes=64)
         cen = [[keep.tile([P, HALF], BF16, name="cen%d%d" % (h, ct), align_bytes=64) for ct in range(CTILES)] for h in range(2)]
         a_codes = [keep.tile([P, PASSES, CLU], U32, name="a_codes%d" % b, align_bytes=64) for b in range(IMG)]
         a_planes = [keep.tile([P, PASSES * (1 + k // 2), CLU], U8, name="a_plane%d" % k, align_bytes=64) for k in range(3)]
@@ -150,7 +150,7 @@ def tile_vlad_residual_sums_k2_kernel(tc, a_words, a_scales, x, mass, centres, g
         def multiply(b, h, ct, g, first=0):
             cl = slice(ct * P, (ct + 1) * P)
             if g == first:
-                acc[ct, h] = psum.tile([P, HALF], F32, name="acc%d%d" % (ct, h))
+                acc[ct, h] = psum.tile([P, HALF], F32, name="acc%d%d" % ((0, 0) if (b, h, ct) == (IMG - 1, 1, 1) else (ct, h)))
             a_scale = a_planes[min(b, 2)][:, PASSES * (b // 3) + g, :]
             codes, plane = xq[b, g]
             nc.tensor.matmul_mx(
@@ -181,8 +181,9 @@ def tile_vlad_residual_sums_k2_kernel(tc, a_words, a_scales, x, mass, centres, g
             done = y_of(b, h, c0, c1, True).rearrange("p (k d) -> p k d", d=HALF)
             nc.vector.tensor_tensor(out=done, in0=part, in1=spread, op=ALU.mult)
 
-        def scale_on_gpsimd(b, ct):
-            nc.gpsimd.tensor_tensor(out=y_of(b, 1, ct, ct + 1, True), in0=y_of(b, 1, ct, ct + 1), in1=gain_high[:], op=ALU.mult)
+        def scale_on_gpsimd(b, h, ct):
+            nc.gpsimd.tensor_tensor(out=y_of(b, h, ct, ct + 1, True), in0=y_of(b, h, ct, ct + 1),
+                                    in1=gain_sb[:, h * HALF:(h + 1) * HALF], op=ALU.mult)
 
         def store_y(b, h, c0=0, c1=CTILES):
             dst = out_0[b, c0 * P:c1 * P, h * HALF:(h + 1) * HALF].rearrange("(k p) d -> p k d", p=P)
@@ -204,8 +205,11 @@ def tile_vlad_residual_sums_k2_kernel(tc, a_words, a_scales, x, mass, centres, g
             dst, src = round_views(b, h, c0, c1, None)
             nc.scalar.copy(out=dst, in_=src)
 
-        def turn(b, h, c0=0, c1=CTILES):
-            bank = psum.tile([P, c1 - c0, 2, P], F32, name="turned", bufs=3)
+        def turn(b, h, c0=0, c1=CTILES, spare=None):
+            if spare is None:
+                bank = psum.tile([P, c1 - c0, 2, P], F32, name="turned", bufs=3)
+            else:
+                bank = psum.tile([P, c1 - c0, 2, P], F32, name="acc%d1" % spare)
             turned[b, h, c0] = bank
             for ct in range(c0, c1):
                 for w in range(2):
@@ -234,21 +238,20 @@ def tile_vlad_residual_sums_k2_kernel(tc, a_words, a_scales, x, mass, centres, g
             nc.vector.quantize_mx(out=y_codes[h][:, cl].bitcast(E4M3X4), scales=y_plane[4 * h:, cl],
                                   in_=yb[h][:, u0 * P * PACK:u1 * P * PACK])
 
-        def store_codes(h, b0, b1):
-            dst = out_1[h][:, b0 * CLU:b1 * CLU, :].rearrange("p m t -> p (m t)").bitcast(I32)
-            nc.sync.dma_start(out=dst, in_=y_codes[h][:, b0 * CLU:b1 * CLU].bitcast(I32))
+        def store_codes(h, u0, u1):
+            dst = out_1[h][:, u0 * P:u1 * P, :].rearrange("p m t -> p (m t)").bitcast(I32)
+            nc.sync.dma_start(out=dst, in_=y_codes[h][:, u0 * P:u1 * P].bitcast(I32))
 
         def spread_constants():
-            first = psum.tile([P, P + HALF], BF16, name="turned", bufs=3)
-            nc.tensor.transpose(first[:, 0:P], rows[:], ident16[:])
+            first = psum.tile([P, P], BF16, name="turned", bufs=3)
+            second = psum.tile([P, DIM], BF16, name="turned", bufs=3)
+            nc.tensor.transpose(first[:], rows[:], ident16[:])
             nc.vector.tensor_copy(out=cols[:], in_=first[:, 0:ROWS])
             nc.vector.tensor_scalar(out=neg_mass[:], in0=first[:, ROWS:2 * ROWS], scalar1=-1.0, scalar2=None, op0=ALU.mult)
-            for j in range(ROWS):
-                nc.tensor.transpose(gain_all[:, j * P:(j + 1) * P], cols[:, j:j + 1].to_broadcast([P, P]), ident16[:])
-            for j in range(ROWS // 2):
-                column = cols[:, ROWS // 2 + j:ROWS // 2 + j + 1]
-                nc.tensor.transpose(first[:, (j + 1) * P:(j + 2) * P], column.to_broadcast([P, P]), ident16[:])
-            return first[:, P:]
+            for bank in (gain_all, second):
+                for j in range(ROWS):
+                    nc.tensor.transpose(bank[:, j * P:(j + 1) * P], cols[:, j:j + 1].to_broadcast([P, P]), ident16[:])
+            return second
 
         interleave_on_vector(0, 0, 0, HALF)
         interleave_on_scalar(0, 0, HALF, DIM)
@@ -257,7 +260,7 @@ def tile_vlad_residual_sums_k2_kernel(tc, a_words, a_scales, x, mass, centres, g
         for h, share in enumerate((VECTOR_URGENT, VECTOR_HEAD_LAST)):
             interleave_on_vector(0, 1, h * HALF, h * HALF + share)
             interleave_on_scalar(0, 1, h * HALF + share, (h + 1) * HALF)
-        nc.scalar.copy(out=gain_high[:], in_=spare)
+        nc.scalar.copy(out=gain_sb[:], in_=spare[:])
         for g, h in ((1, 0), (0, 1), (1, 1)):
             quantize_x(0, g, h)
         passes(0, 0, 0, 1)
@@ -337,56 +340,61 @@ def tile_vlad_residual_sums_k2_kernel(tc, a_words, a_scales, x, mass, centres, g
         interleave_on_scalar(3, 0, 0, DIM - GPSIMD_FIFTH)
         for h in range(2):
             interleave_on_scalar(3, 1, h * HALF, (h + 1) * HALF)
-        block(3)
+        for g in (1, 0):
+            quantize_x(3, g, 0)
+        quantize_y(0, 0, 2)
+        store_codes(0, 0, 2)
+        for g in (1, 0):
+            quantize_x(3, g, 1)
         for h, ct in ((0, 0), (0, 1), (1, 0)):
             fill_bank(3, h, ct)
 
-        gather_values(0, 1, 1)
         round_on_scalar(2, 0)
-        gather_values(1, 0, 0)
         round_on_scalar(1, 1)
-        gather_values(1, 0, 1)
+        turn(2, 0, spare=1)
+        gather_values(0, 1, 1)
+        for ct in range(CTILES):
+            gather_values(1, 0, ct)
         scale(2, 1, 0, 1)
         store_y(2, 1, 0, 1)
-        scale_on_gpsimd(2, 1)
+        scale_on_gpsimd(2, 1, 1)
         store_y(2, 1, 1, 2)
-        round_on_gpsimd(2, 1)
-        turn(2, 0)
+        round_on_scalar(2, 1)
+        residual(3, 0, 0)
         fill_bank(3, 1, 1)
+        residual(3, 0, 1)
         turn(1, 1)
         turn(2, 1)
-        gather_words(2, 0)
-        for ct in range(CTILES):
-            residual(3, 0, ct)
-        for ct in range(CTILES):
-            scale(3, 0, ct, ct + 1)
-            round_on_gpsimd(3, 0, ct, ct + 1)
+        scale_on_gpsimd(3, 0, 0)
+        residual(3, 1, 0)
+        scale(3, 0, 1, 2)
         store_y(3, 0)
         for ct in range(CTILES):
-            residual(3, 1, ct)
-        turn(3, 0, 0, 1)
+            round_on_gpsimd(3, 0, ct, ct + 1)
+        turn(3, 0)
+        residual(3, 1, 1)
+        gather_words(2, 0)
         gather_words(1, 1)
-        turn(3, 0, 1, 2)
         gather_words(2, 1)
-        gather_words(3, 0, 0, 1)
         for ct in range(CTILES):
             scale(3, 1, ct, ct + 1)
             store_y(3, 1, ct, ct + 1)
             round_on_scalar(3, 1, ct, ct + 1)
             turn(3, 1, ct, ct + 1)
-        gather_words(3, 0, 1, 2)
+        gather_words(3, 0)
         for ct in range(CTILES):
             gather_words(3, 1, ct, ct + 1)
 
-        for h, b0, b1 in ((0, 0, 2), (1, 2, 3), (1, 0, 2)):
-            quantize_y(h, CTILES * b0, CTILES * b1)
-            store_codes(h, b0, b1)
-        quantize_y(0, 4, 7)
-        quantize_y(0, 7, 8)
-        store_codes(0, 2, 4)
+        quantize_y(0, 2, 6)
+        store_codes(0, 2, 6)
+        quantize_y(1, 0, 2)
+        quantize_y(1, 2, 6)
+        store_codes(1, 0, 6)
+        quantize_y(0, 6, 8)
+        store_codes(0, 6, 8)
         quantize_y(1, 6, 7)
         quantize_y(1, 7, 8)
-        store_codes(1, 3, 4)
+        store_codes(1, 6, 8)
         for q in range(4):
             queue = nc.scalar if q % 2 else nc.sync
             queue.dma_start(out=out_2[:, 4 * q:4 * q + 4, :].bitcast(I32), in_=y_plane[32 * q:32 * q + 8, :].bitcast(I32))

@@ -30,7 +30,7 @@ GPSIMD_FIRST = 400
 GPSIMD_SECOND = 312
 GPSIMD_THIRD = 512
 GPSIMD_FOURTH = 272
-GPSIMD_FIFTH = 784
+GPSIMD_FIFTH = 752
 
 
 def tile_vlad_residual_sums_k2_kernel(tc, a_words, a_scales, x, mass, centres, gain, out_0, out_1, out_2):
@@ -47,7 +47,7 @@ def tile_vlad_residual_sums_k2_kernel(tc, a_words, a_scales, x, mass, centres, g
         cols = keep.tile([P, ROWS], BF16, name="cols", align_bytes=64)
         neg_mass = keep.tile([P, ROWS], F32, name="neg_mass", align_bytes=64)
         gain_all = psum.tile([P, DIM], BF16, name="gain_all")
-        gain_sb = keep.tile([P, DIM], BF16, name="gain_sb", align_bytes=64)
+        gain_sb = keep.tile([P, DIM], F32, name="gain_sb", align_bytes=64)
         cen = [[keep.tile([P, HALF], BF16, name="cen%d%d" % (h, ct), align_bytes=64) for ct in range(CTILES)] for h in range(2)]
         a_codes = [keep.tile([P, PASSES, CLU], U32, name="a_codes%d" % b, align_bytes=64) for b in range(IMG)]
         a_planes = [keep.tile([P, PASSES * (1 + k // 2), CLU], U8, name="a_plane%d" % k, align_bytes=64) for k in range(3)]
@@ -110,7 +110,7 @@ def tile_vlad_residual_sums_k2_kernel(tc, a_words, a_scales, x, mass, centres, g
         place[1, 1, 1] = place[1, 0, 0] - (HALF - GPSIMD_SECOND)
         xq = {}
         acc = {}
-        y16 = {}
+        words = {}
         turned = {}
         late = place[3, 1, 1] * PACK
         moved = {(2, 1, True): arena[:, late:late + CHUNK].bitcast(F32)}
@@ -150,7 +150,7 @@ def tile_vlad_residual_sums_k2_kernel(tc, a_words, a_scales, x, mass, centres, g
         def multiply(b, h, ct, g, first=0):
             cl = slice(ct * P, (ct + 1) * P)
             if g == first:
-                acc[ct, h] = psum.tile([P, HALF], F32, name="acc%d%d" % ((0, 0) if (b, h, ct) == (IMG - 1, 1, 1) else (ct, h)))
+                acc[ct, h] = psum.tile([P, HALF], F32, name="acc%d%d" % (ct, h))
             a_scale = a_planes[min(b, 2)][:, PASSES * (b // 3) + g, :]
             codes, plane = xq[b, g]
             nc.tensor.matmul_mx(
@@ -195,26 +195,26 @@ def tile_vlad_residual_sums_k2_kernel(tc, a_words, a_scales, x, mass, centres, g
                 room = keep.tile([P, n * HALF], BF16, name="y16_%d%d%d" % (b, h, c0), align_bytes=64)[:]
             dst = room.rearrange("p (w q e) -> p w q e", w=2, e=2)
             for k in range(n):
-                y16[b, h + (c0 + k) // CTILES, (c0 + k) % CTILES] = dst[:, :, k * P:(k + 1) * P, :]
+                words[b, h, c0 + k] = [dst[:, w, k * P:(k + 1) * P, :].rearrange("p q e -> p (q e)").bitcast(F32) for w in range(2)]
             return dst, y_of(b, h, c0, c1, True).rearrange("p (q w e) -> p w q e", w=2, e=2)
 
-        def round_on_gpsimd(b, h, c0=0, c1=CTILES, room=None):
-            gpsimd_copy(*round_views(b, h, c0, c1, room))
+        def round_on_gpsimd(b, h, c0=0, c1=CTILES):
+            room = keep.tile([P, (c1 - c0) * HALF], BF16, name="y16_%d%d%d" % (b, h, c0), align_bytes=64)
+            gpsimd_copy(room[:], y_of(b, h, c0, c1, True))
+            for ct in range(c0, c1):
+                pairs = room[:, (ct - c0) * HALF:(ct - c0 + 1) * HALF].bitcast(F32).rearrange("p (q w) -> p w q", w=2)
+                words[b, h, ct] = [pairs[:, w, :] for w in range(2)]
 
         def round_on_scalar(b, h, c0=0, c1=CTILES):
             dst, src = round_views(b, h, c0, c1, None)
             nc.scalar.copy(out=dst, in_=src)
 
-        def turn(b, h, c0=0, c1=CTILES, spare=None):
-            if spare is None:
-                bank = psum.tile([P, c1 - c0, 2, P], F32, name="turned", bufs=3)
-            else:
-                bank = psum.tile([P, c1 - c0, 2, P], F32, name="acc%d1" % spare)
+        def turn(b, h, c0=0, c1=CTILES):
+            bank = psum.tile([P, c1 - c0, 2, P], F32, name="turned", bufs=3)
             turned[b, h, c0] = bank
             for ct in range(c0, c1):
                 for w in range(2):
-                    words = y16[b, h, ct][:, w, :, :].rearrange("p q e -> p (q e)").bitcast(F32)
-                    nc.tensor.transpose(bank[:, ct - c0, w, :], words, ident32[:])
+                    nc.tensor.transpose(bank[:, ct - c0, w, :], words[b, h, ct][w], ident32[:])
 
         def gather_words(b, h, c0=0, c1=CTILES):
             dst = yb[h][:, (b * CLU + c0 * P) * PACK:(b * CLU + c1 * P) * PACK].bitcast(F32)
@@ -346,34 +346,36 @@ def tile_vlad_residual_sums_k2_kernel(tc, a_words, a_scales, x, mass, centres, g
         store_codes(0, 0, 2)
         for g in (1, 0):
             quantize_x(3, g, 1)
-        for h, ct in ((0, 0), (0, 1), (1, 0)):
-            fill_bank(3, h, ct)
+        for ct in range(CTILES):
+            fill_bank(3, 0, ct)
 
         round_on_scalar(2, 0)
-        round_on_scalar(1, 1)
-        turn(2, 0, spare=1)
         gather_values(0, 1, 1)
+        turn(2, 0)
         for ct in range(CTILES):
+            fill_bank(3, 1, ct)
             gather_values(1, 0, ct)
+        round_on_scalar(1, 1)
         scale(2, 1, 0, 1)
         store_y(2, 1, 0, 1)
         scale_on_gpsimd(2, 1, 1)
         store_y(2, 1, 1, 2)
-        round_on_scalar(2, 1)
-        residual(3, 0, 0)
-        fill_bank(3, 1, 1)
-        residual(3, 0, 1)
+        round_on_gpsimd(2, 1, 1, 2)
+        round_on_scalar(2, 1, 0, 1)
+        gather_words(2, 0)
         turn(1, 1)
         turn(2, 1)
-        scale_on_gpsimd(3, 0, 0)
-        residual(3, 1, 0)
-        scale(3, 0, 1, 2)
-        store_y(3, 0)
         for ct in range(CTILES):
-            round_on_gpsimd(3, 0, ct, ct + 1)
+            residual(3, 0, ct)
+        scale(3, 0, 0, 1)
+        round_on_scalar(3, 0, 0, 1)
+        scale_on_gpsimd(3, 0, 1)
+        round_on_gpsimd(3, 0, 1, 2)
+        for ct in range(CTILES):
+            store_y(3, 0, ct, ct + 1)
         turn(3, 0)
-        residual(3, 1, 1)
-        gather_words(2, 0)
+        for ct in range(CTILES):
+            residual(3, 1, ct)
         gather_words(1, 1)
         gather_words(2, 1)
         for ct in range(CTILES):

from contextlib import ExitStack

import concourse.mybir as mybir
from concourse.masks import make_identity

IMG, PTS, CLU, DIM = 4, 1024, 256, 1024
FLOPS = 2 * IMG * PTS * CLU * DIM

F32 = mybir.dt.float32
BF16 = mybir.dt.bfloat16
U32 = mybir.dt.uint32
I32 = mybir.dt.int32
U8 = mybir.dt.uint8
E4M3X4 = mybir.dt.float8_e4m3fn_x4
E5M2X4 = mybir.dt.float8_e5m2_x4
ALU = mybir.AluOpType

P = 128
PACK = 4
K_PASS = P * PACK
HALF = 512
PASSES = PTS // K_PASS
CTILES = CLU // P
ROWS = DIM // P
CHUNK = HALF * PACK

VECTOR_URGENT = 336
VECTOR_HEAD_LAST = 192
GPSIMD_FIRST = 400
GPSIMD_SECOND = 312
GPSIMD_THIRD = 512
GPSIMD_FOURTH = 272
GPSIMD_FIFTH = 752


def tile_vlad_residual_sums_k2_kernel(tc, a_words, a_scales, x, mass, centres, gain, out_0, out_1, out_2):
    nc = tc.nc
    with ExitStack() as ctx:
        keep = ctx.enter_context(tc.tile_pool(name="keep", bufs=1))
        work = ctx.enter_context(tc.tile_pool(name="work", bufs=4))
        psum = ctx.enter_context(tc.psum_pool(name="psum", bufs=1))
        ctx.enter_context(tc.manual_schedule())

        ident32 = keep.tile([P, P], F32, name="ident32", align_bytes=64)
        ident16 = keep.tile([P, P], BF16, name="ident16", align_bytes=64)
        rows = keep.tile([P, P], BF16, name="rows", align_bytes=64)
        cols = keep.tile([P, ROWS], BF16, name="cols", align_bytes=64)
        neg_mass = keep.tile([P, ROWS], F32, name="neg_mass", align_bytes=64)
        gain_all = psum.tile([P, DIM], BF16, name="gain_all")
        gain_sb = keep.tile([P, DIM], F32, name="gain_sb", align_bytes=64)
        cen = [[keep.tile([P, HALF], BF16, name="cen%d%d" % (h, ct), align_bytes=64) for ct in range(CTILES)] for h in range(2)]
        a_codes = [keep.tile([P, PASSES, CLU], U32, name="a_codes%d" % b, align_bytes=64) for b in range(IMG)]
        a_planes = [keep.tile([P, PASSES * (1 + k // 2), CLU], U8, name="a_plane%d" % k, align_bytes=64) for k in range(3)]
        y_codes = [keep.tile([P, IMG * CLU], U32, name="y_codes%d" % h, align_bytes=64) for h in range(2)]
        y_plane = keep.tile([P, IMG * CLU], U8, name="y_plane", align_bytes=64)
        arena = keep.tile([P, 6 * CHUNK], BF16, name="arena", align_bytes=64)
        ys = [keep.tile([P, 2 * CTILES * HALF], F32, name="y%d" % b, align_bytes=64) for b in range(IMG)]
        yb = [keep.tile([P, IMG * CLU * PACK], BF16, name="yb%d" % h, align_bytes=64) for h in range(2)]
        raw = {}

        def load_x(b, g):
            raw[b, g] = keep.tile([P, PACK, DIM], BF16, name="raw%d%d" % (b, g), align_bytes=64)
            nc.sync.dma_start(out=raw[b, g][:], in_=x[b, g * K_PASS:(g + 1) * K_PASS, :].rearrange("(p j) d -> p j d", j=PACK))

        def load_a(b):
            src = a_words[PASSES * b:PASSES * (b + 1)].rearrange("g p n t -> p g (n t)").bitcast(I32)
            nc.sync.dma_start(out=a_codes[b][:].bitcast(I32), in_=src)

        def load_centres(h, ct):
            nc.sync.dma_start(out=cen[h][ct][:], in_=centres[ct * P:(ct + 1) * P, h * HALF:(h + 1) * HALF])

        def load_scales(pair):
            groups = slice(PASSES * pair, PASSES * (pair + 1 + pair // 2))
            for r in range(4):
                nc.sync.dma_start(out=a_planes[pair][r:P:32, :, :].bitcast(I32),
                                  in_=a_scales[groups, r:16:4, :].rearrange("g q n -> q g n").bitcast(I32))

        nc.vector.memset(rows[:], 0.0)
        for plane in a_planes:
            nc.vector.memset(plane[:].rearrange("p g n -> p (g n)").bitcast(I32), 0)
        make_identity(nc, ident32[:])

        load_x(0, 0)
        nc.sync.dma_start(out=rows[0:ROWS, :], in_=gain.rearrange("(r c) -> r c", c=P))
        nc.sync.dma_start(out=rows[ROWS:2 * ROWS, :], in_=mass.rearrange("b (h c) -> (b h) c", c=P))
        nc.scalar.copy(out=ident16[:], in_=ident32[:])
        load_x(0, 1)
        load_scales(0)
        load_a(0)
        load_centres(0, 0)
        load_x(1, 0)
        load_centres(0, 1)
        load_centres(1, 0)
        load_x(1, 1)
        load_centres(1, 1)
        load_scales(1)
        load_a(1)
        load_x(2, 0)
        load_x(2, 1)
        load_x(3, 0)
        load_scales(2)
        load_a(2)
        load_x(3, 1)
        load_a(3)

        place = {(0, 0, 0): 0, (0, 0, 1): HALF, (0, 1, 1): 3 * HALF, (0, 1, 0): 4 * HALF,
                 (1, 0, 0): 2 * HALF, (1, 0, 1): 3 * HALF, (1, 1, 0): 5 * HALF,
                 (2, 0, 0): 4 * HALF, (2, 0, 1): 5 * HALF, (2, 1, 0): 3 * HALF, (2, 1, 1): 2 * HALF,
                 (3, 0, 0): HALF, (3, 0, 1): 2 * HALF, (3, 1, 0): 4 * HALF, (3, 1, 1): 0}
        place[1, 1, 1] = place[1, 0, 0] - (HALF - GPSIMD_SECOND)
        xq = {}
        acc = {}
        words = {}
        turned = {}
        late = place[3, 1, 1] * PACK
        moved = {(2, 1, True): arena[:, late:late + CHUNK].bitcast(F32)}

        def load_views(b, g, c0, c1):
            at = (place[b, g, c0 // HALF] + c0 % HALF) * PACK
            dst = arena[:, at:at + (c1 - c0) * PACK].rearrange("p (c t) -> p c t", t=PACK)
            return dst, raw[b, g][:, :, c0:c1]

        def interleave_on_vector(b, g, c0, c1):
            dst, src = load_views(b, g, c0, c1)
            nc.vector.tensor_copy(out=dst.rearrange("p (c i) t -> p c t i", i=4), in_=src.rearrange("p t (c i) -> p c t i", i=4))

        def gpsimd_copy(out, in_):
            nc.gpsimd.tensor_scalar(out=out, in0=in_, scalar1=1.0, scalar2=0.0, op0=ALU.mult, op1=ALU.add)

        def interleave_on_gpsimd(b, g, c0, c1):
            dst, src = load_views(b, g, c0, c1)
            gpsimd_copy(dst, src.rearrange("p t c -> p c t"))

        def interleave_on_scalar(b, g, c0, c1):
            dst, src = load_views(b, g, c0, c1)
            nc.scalar.copy(out=dst.rearrange("p (c i) (s t) -> p c s i t", i=8, t=2),
                           in_=src.rearrange("p (s t) (c i) -> p c s i t", i=8, t=2))

        def quantize_x(b, g, h, h1=None):
            if (b, g) not in xq:
                codes = work.tile([P, DIM], U32, name="x_codes", align_bytes=64)
                plane = work.tile([P, DIM], U8, name="x_plane", align_bytes=64)
                xq[b, g] = (codes, plane)
            codes, plane = xq[b, g]
            n = (h1 or h + 1) - h
            at = place[b, g, h] * PACK
            cl = slice(h * HALF, (h + n) * HALF)
            nc.vector.quantize_mx(out=codes[:, cl].bitcast(E4M3X4), scales=plane[:, cl], in_=arena[:, at:at + n * CHUNK])

        def multiply(b, h, ct, g, first=0):
            cl = slice(ct * P, (ct + 1) * P)
            if g == first:
                acc[ct, h] = psum.tile([P, HALF], F32, name="acc%d%d" % (ct, h))
            a_scale = a_planes[min(b, 2)][:, PASSES * (b // 3) + g, :]
            codes, plane = xq[b, g]
            nc.tensor.matmul_mx(
                out=acc[ct, h][:],
                lhsT=a_codes[b][:, g, cl].bitcast(E5M2X4), lhsT_scale=a_scale[:, cl],
                rhs=codes[:, h * HALF:(h + 1) * HALF].bitcast(E4M3X4), rhs_scale=plane[:, h * HALF:(h + 1) * HALF],
                start=(g == first), stop=(g != first))

        def passes(b, g, h0=0, h1=2):
            for h in range(h0, h1):
                for ct in range(CTILES):
                    multiply(b, h, ct, g)

        def y_of(b, h, c0, c1, done=False):
            if (b, h, done) in moved:
                return moved[b, h, done][:, c0 * HALF:c1 * HALF]
            return ys[b][:, (h * CTILES + c0) * HALF:(h * CTILES + c1) * HALF]

        def residual(b, h, ct):
            u = b * CTILES + ct
            nc.vector.scalar_tensor_tensor(
                out=y_of(b, h, ct, ct + 1), in0=cen[h][ct][:], scalar=neg_mass[:, u:u + 1],
                in1=acc[ct, h][:], op0=ALU.mult, op1=ALU.add)

        def scale(b, h, c0=0, c1=CTILES):
            part = y_of(b, h, c0, c1).rearrange("p (k d) -> p k d", d=HALF)
            spread = gain_all[:, h * HALF:(h + 1) * HALF].unsqueeze(1).to_broadcast([P, c1 - c0, HALF])
            done = y_of(b, h, c0, c1, True).rearrange("p (k d) -> p k d", d=HALF)
            nc.vector.tensor_tensor(out=done, in0=part, in1=spread, op=ALU.mult)

        def scale_on_gpsimd(b, h, ct):
            nc.gpsimd.tensor_tensor(out=y_of(b, h, ct, ct + 1, True), in0=y_of(b, h, ct, ct + 1),
                                    in1=gain_sb[:, h * HALF:(h + 1) * HALF], op=ALU.mult)

        def store_y(b, h, c0=0, c1=CTILES):
            dst = out_0[b, c0 * P:c1 * P, h * HALF:(h + 1) * HALF].rearrange("(k p) d -> p k d", p=P)
            nc.sync.dma_start(out=dst, in_=y_of(b, h, c0, c1, True).rearrange("p (k d) -> p k d", d=HALF))

        def round_views(b, h, c0, c1, room):
            n = c1 - c0
            if room is None:
                room = keep.tile([P, n * HALF], BF16, name="y16_%d%d%d" % (b, h, c0), align_bytes=64)[:]
            dst = room.rearrange("p (w q e) -> p w q e", w=2, e=2)
            for k in range(n):
                words[b, h, c0 + k] = [dst[:, w, k * P:(k + 1) * P, :].rearrange("p q e -> p (q e)").bitcast(F32) for w in range(2)]
            return dst, y_of(b, h, c0, c1, True).rearrange("p (q w e) -> p w q e", w=2, e=2)

        def round_on_gpsimd(b, h, c0=0, c1=CTILES):
            room = keep.tile([P, (c1 - c0) * HALF], BF16, name="y16_%d%d%d" % (b, h, c0), align_bytes=64)
            gpsimd_copy(room[:], y_of(b, h, c0, c1, True))
            for ct in range(c0, c1):
                pairs = room[:, (ct - c0) * HALF:(ct - c0 + 1) * HALF].bitcast(F32).rearrange("p (q w) -> p w q", w=2)
                words[b, h, ct] = [pairs[:, w, :] for w in range(2)]

        def round_on_scalar(b, h, c0=0, c1=CTILES):
            dst, src = round_views(b, h, c0, c1, None)
            nc.scalar.copy(out=dst, in_=src)

        def turn(b, h, c0=0, c1=CTILES):
            bank = psum.tile([P, c1 - c0, 2, P], F32, name="turned", bufs=3)
            turned[b, h, c0] = bank
            for ct in range(c0, c1):
                for w in range(2):
                    nc.tensor.transpose(bank[:, ct - c0, w, :], words[b, h, ct][w], ident32[:])

        def gather_words(b, h, c0=0, c1=CTILES):
            dst = yb[h][:, (b * CLU + c0 * P) * PACK:(b * CLU + c1 * P) * PACK].bitcast(F32)
            nc.scalar.copy(out=dst.rearrange("p (k c i w) -> p k c w i", k=c1 - c0, i=2, w=2),
                           in_=turned[b, h, c0][:].rearrange("p k w (c i) -> p k c w i", i=2))

        def turn_values(b, h, ct):
            bank = psum.tile([P, PACK, P], F32, name="turned", bufs=3)
            turned[b, h, ct] = bank
            values = y_of(b, h, ct, ct + 1, True).rearrange("p (q t) -> p t q", t=PACK)
            for s in range(PACK):
                nc.tensor.transpose(bank[:, s, :], values[:, s, :], ident32[:])

        def gather_values(b, h, ct):
            dst = yb[h][:, (b * CLU + ct * P) * PACK:(b * CLU + (ct + 1) * P) * PACK]
            nc.scalar.copy(out=dst.rearrange("p (c i t) -> p c t i", i=2, t=PACK),
                           in_=turned[b, h, ct][:].rearrange("p t (c i) -> p c t i", i=2))

        def quantize_y(h, u0, u1):
            cl = slice(u0 * P, u1 * P)
            nc.vector.quantize_mx(out=y_codes[h][:, cl].bitcast(E4M3X4), scales=y_plane[4 * h:, cl],
                                  in_=yb[h][:, u0 * P * PACK:u1 * P * PACK])

        def store_codes(h, u0, u1):
            dst = out_1[h][:, u0 * P:u1 * P, :].rearrange("p m t -> p (m t)").bitcast(I32)
            nc.sync.dma_start(out=dst, in_=y_codes[h][:, u0 * P:u1 * P].bitcast(I32))

        def spread_constants():
            first = psum.tile([P, P], BF16, name="turned", bufs=3)
            second = psum.tile([P, DIM], BF16, name="turned", bufs=3)
            nc.tensor.transpose(first[:], rows[:], ident16[:])
            nc.vector.tensor_copy(out=cols[:], in_=first[:, 0:ROWS])
            nc.vector.tensor_scalar(out=neg_mass[:], in0=first[:, ROWS:2 * ROWS], scalar1=-1.0, scalar2=None, op0=ALU.mult)
            for bank in (gain_all, second):
                for j in range(ROWS):
                    nc.tensor.transpose(bank[:, j * P:(j + 1) * P], cols[:, j:j + 1].to_broadcast([P, P]), ident16[:])
            return second

        interleave_on_vector(0, 0, 0, HALF)
        interleave_on_scalar(0, 0, HALF, DIM)
        spare = spread_constants()
        quantize_x(0, 0, 0)
        for h, share in enumerate((VECTOR_URGENT, VECTOR_HEAD_LAST)):
            interleave_on_vector(0, 1, h * HALF, h * HALF + share)
            interleave_on_scalar(0, 1, h * HALF + share, (h + 1) * HALF)
        nc.scalar.copy(out=gain_sb[:], in_=spare[:])
        for g, h in ((1, 0), (0, 1), (1, 1)):
            quantize_x(0, g, h)
        passes(0, 0, 0, 1)
        passes(0, 1, 0, 1)
        for ct in range(CTILES):
            multiply(0, 1, ct, 0)
            multiply(0, 1, ct, 1)

        def open_window(b):
            for h in range(2):
                for ct in range(CTILES):
                    residual(b, h, ct)
            scale(b, 0)
            store_y(b, 0)

        residual(0, 0, 0)
        residual(0, 0, 1)
        residual(0, 1, 0)
        scale(0, 0)
        store_y(0, 0)
        interleave_on_gpsimd(1, 0, DIM - GPSIMD_FIRST, DIM)
        interleave_on_scalar(1, 0, 0, HALF)
        interleave_on_scalar(1, 0, HALF, DIM - GPSIMD_FIRST)
        quantize_x(1, 0, 0)
        quantize_x(1, 0, 1)
        residual(0, 1, 1)
        for ct in range(CTILES):
            scale(0, 1, ct, ct + 1)
        store_y(0, 1)
        interleave_on_gpsimd(1, 1, DIM - GPSIMD_SECOND, DIM)
        interleave_on_scalar(1, 1, 0, HALF)
        interleave_on_scalar(1, 1, HALF, DIM - GPSIMD_SECOND)
        turn_values(0, 0, 0)
        passes(1, 0)
        for h in range(2):
            quantize_x(1, 1, h)
        for h, ct in ((0, 0), (0, 1), (1, 1), (1, 0)):
            multiply(1, h, ct, 1)

        def block(b):
            for g, h in ((1, 0), (0, 0), (1, 1), (0, 1)):
                quantize_x(b, g, h)

        def fill_bank(b, h, ct):
            for g in (1, 0):
                multiply(b, h, ct, g, 1)


        open_window(1)
        scale(1, 1, 1, 2)
        turn_values(0, 0, 1)
        turn_values(0, 1, 0)
        interleave_on_gpsimd(2, 0, DIM - GPSIMD_THIRD, DIM)
        interleave_on_gpsimd(2, 1, DIM - GPSIMD_FOURTH, DIM)
        gather_values(0, 0, 0)
        interleave_on_scalar(2, 0, 0, DIM - GPSIMD_THIRD)
        turn_values(0, 1, 1)
        interleave_on_scalar(2, 1, 0, HALF)
        interleave_on_scalar(2, 1, HALF, DIM - GPSIMD_FOURTH)
        block(2)
        for h, ct in ((0, 0), (0, 1), (1, 1), (1, 0)):
            fill_bank(2, h, ct)

        scale(1, 1, 0, 1)
        store_y(1, 1)
        for ct in range(CTILES):
            residual(2, 0, ct)
        for ct in range(CTILES):
            scale(2, 0, ct, ct + 1)
        store_y(2, 0)
        for ct in range(CTILES):
            residual(2, 1, ct)
        for ct in range(CTILES):
            gather_values(0, ct, 1 - ct)
            turn_values(1, 0, ct)
        interleave_on_gpsimd(3, 0, DIM - GPSIMD_FIFTH, DIM)
        interleave_on_scalar(3, 0, 0, DIM - GPSIMD_FIFTH)
        for h in range(2):
            interleave_on_scalar(3, 1, h * HALF, (h + 1) * HALF)
        for g in (1, 0):
            quantize_x(3, g, 0)
        quantize_y(0, 0, 2)
        store_codes(0, 0, 2)
        for g in (1, 0):
            quantize_x(3, g, 1)
        for ct in range(CTILES):
            fill_bank(3, 0, ct)

        round_on_scalar(2, 0)
        gather_values(0, 1, 1)
        turn(2, 0)
        for ct in range(CTILES):
            fill_bank(3, 1, ct)
            gather_values(1, 0, ct)
        round_on_scalar(1, 1)
        scale(2, 1, 0, 1)
        store_y(2, 1, 0, 1)
        scale_on_gpsimd(2, 1, 1)
        store_y(2, 1, 1, 2)
        round_on_gpsimd(2, 1, 1, 2)
        round_on_scalar(2, 1, 0, 1)
        gather_words(2, 0)
        turn(1, 1)
        turn(2, 1)
        for ct in range(CTILES):
            residual(3, 0, ct)
        scale(3, 0, 0, 1)
        round_on_scalar(3, 0, 0, 1)
        scale_on_gpsimd(3, 0, 1)
        round_on_gpsimd(3, 0, 1, 2)
        for ct in range(CTILES):
            store_y(3, 0, ct, ct + 1)
        turn(3, 0)
        for ct in range(CTILES):
            residual(3, 1, ct)
        gather_words(1, 1)
        gather_words(2, 1)
        for ct in range(CTILES):
            scale(3, 1, ct, ct + 1)
            store_y(3, 1, ct, ct + 1)
            round_on_scalar(3, 1, ct, ct + 1)
            turn(3, 1, ct, ct + 1)
        gather_words(3, 0)
        for ct in range(CTILES):
            gather_words(3, 1, ct, ct + 1)

        quantize_y(0, 2, 6)
        store_codes(0, 2, 6)
        quantize_y(1, 0, 2)
        quantize_y(1, 2, 6)
        store_codes(1, 0, 6)
        quantize_y(0, 6, 8)
        store_codes(0, 6, 8)
        quantize_y(1, 6, 7)
        quantize_y(1, 7, 8)
        store_codes(1, 6, 8)
        for q in range(4):
            queue = nc.scalar if q % 2 else nc.sync
            queue.dma_start(out=out_2[:, 4 * q:4 * q + 4, :].bitcast(I32), in_=y_plane[32 * q:32 * q + 8, :].bitcast(I32))
